import numpy as np
import ml_dtypes


def mxq(x, axis, fmt="e4m3"):
    dtype, down = {"e4m3": (ml_dtypes.float8_e4m3fn, 7), "e5m2": (ml_dtypes.float8_e5m2, 14)}[fmt]
    v = np.moveaxis(np.asarray(x, np.float32).astype(ml_dtypes.bfloat16).astype(np.float64), axis, -1)
    blocks = v.reshape(v.shape[:-1] + (-1, 32))
    amax = np.abs(blocks).max(-1, keepdims=True)
    byte = np.maximum(np.where(amax > 0, np.frexp(amax)[1] - 1 + 127, 0) - down, 1)
    scale = np.exp2(byte - 127.0)
    codes = (blocks / scale).astype(np.float32).astype(dtype).astype(np.float64)
    return np.moveaxis((codes * scale).reshape(v.shape), -1, axis)


WIDE = False


def mx_kscale(k):
    if not WIDE:
        return np.ones(k)
    levels = np.array([18, -18])
    if k % 512:
        return np.exp2(np.random.permutation(np.resize(levels, k // 32))).repeat(32)
    a = np.empty((k // 512, 16))
    for p in range(k // 512):
        a[p, :8] = np.random.permutation(np.resize(levels, 8))
        for g in range(8):
            far = levels[np.abs(levels - a[p, g]) >= 10]
            a[p, g + 8] = far[np.random.randint(len(far))]
    return np.exp2(a.ravel()).repeat(32)


def f64(x):
    return np.asarray(x).astype(np.float64)


def striped(idx):
    return np.tile(np.asarray(idx).reshape(-1, 16).T, (8, 1)).astype(np.uint16)


def unstriped(offs):
    return offs[:16].T.reshape(-1).astype(np.int64)

def planes(y):
    n, m = y.shape
    v = y.astype(np.float32).astype(ml_dtypes.bfloat16).astype(np.float64).reshape(n // 32, 32, m)
    top = np.abs(v).max(1)
    byte = np.clip(np.where(top > 0, np.frexp(top)[1] - 1 + 127 - 7, 1), 1, 254)
    codes = (v * np.exp2(127.0 - byte)[:, None, :]).reshape(n, m).astype(np.float32).astype(ml_dtypes.float8_e4m3fn).view(np.uint8)
    words = codes.reshape(n // 512, 128, 4, m).transpose(0, 1, 3, 2)
    return np.ascontiguousarray(words), np.ascontiguousarray(byte.astype(np.uint8).reshape(n // 512, 16, m))


V, K, E, D, DV = 1024, 2, 2048, 512, 512


def setup_inputs():
    n = np.random.standard_normal
    v = mx_kscale(DV)[:, None]
    coarse = lambda x: x.astype(np.float32).astype(ml_dtypes.bfloat16).astype(np.float64)
    return {
        "dyT": (coarse(n((DV, V))) * v).astype(np.float32),
        "hE": coarse(n((DV, E))).astype(np.float32),
        "wm": (n((DV, D)) / np.sqrt(DV) / v).astype(np.float32),
        "offs": striped(np.random.randint(0, V, E)),
        "offs2": striped(np.random.permutation(E)),
    }


def reference(dyT, hE, wm, offs, offs2):
    h = f64(hE)
    dz = f64(dyT)[:, unstriped(offs)] * 2.0 * np.maximum(h, 0.0)
    dm = mxq(f64(wm), 0, "e4m3").T @ mxq(dz, 0, "e5m2")
    out_0 = dm[:, unstriped(offs2)].reshape(D, V, K).sum(-1)
    return (out_0,) + planes(out_0)

@@ -1,0 +1,214 @@
+from contextlib import ExitStack
+
+import concourse.mybir as mybir
+
+V, E, D, DV = 1024, 2048, 512, 512
+FLOPS = 2 * DV * D * E
+
+F32 = mybir.dt.float32
+BF16 = mybir.dt.bfloat16
+I32 = mybir.dt.int32
+U32 = mybir.dt.uint32
+U16 = mybir.dt.uint16
+U8 = mybir.dt.uint8
+E4M3 = mybir.dt.float8_e4m3fn_x4
+E5M2 = mybir.dt.float8_e5m2_x4
+MULT = mybir.AluOpType.mult
+ADD = mybir.AluOpType.add
+MAX = mybir.AluOpType.max
+RELU = mybir.ActivationFunctionType.Relu
+
+P = 128
+PACK = 4
+CHUNK = 512
+CHUNKS = E // CHUNK
+PER_COL = 16
+EDGE_PIECES = [(0, 512), (512, 512), (1024, 512), (1536, 256), (1792, 128), (1920, 128)]
+NODE_PIECES = [(0, 512), (512, 256), (768, 128), (896, 128)]
+
+
+def interleaved_views(dst, src):
+    return (
+        dst[:].rearrange("p (c i) t -> p c t i", i=4),
+        src[:].rearrange("p t (c i) -> p c t i", i=4),
+    )
+
+
+def tile_attend_gmp_pl_kernel(tc, dyT, hE, wm, offs, offs2, out_0, out_1, out_2):
+    nc = tc.nc
+    dy_rows = dyT.rearrange("(p t) v -> p t v", t=PACK)
+    h_rows = hE.rearrange("(p t) e -> p t e", t=PACK)
+    w_rows = wm.rearrange("(p j) d -> p j d", j=PACK)
+    y_rows = out_0.rearrange("(p t) x -> p t x", t=PACK)
+    words_out = out_1.rearrange("o p x l -> p (o x l)").bitcast(I32)
+    scales_out = out_2.rearrange("o f x -> (o f) x").bitcast(I32)
+
+    with ExitStack() as ctx:
+        keep = ctx.enter_context(tc.tile_pool(name="keep", bufs=1))
+        ring = ctx.enter_context(tc.tile_pool(name="ring", bufs=3))
+        psum = ctx.enter_context(tc.psum_pool(name="psum", bufs=8))
+
+        dst_list = keep.tile([P, E // PER_COL], U16, name="dst_list")
+        src_list = keep.tile([P, E // PER_COL], U16, name="src_list")
+        dy = [keep.tile([P, V], F32, name="dy%d" % t) for t in range(PACK)]
+        h = {(t, c): keep.tile([P, CHUNK], F32, name="h%d_%d" % (t, c)) for t in range(PACK) for c in range(CHUNKS)}
+        w_raw = keep.tile([P, PACK, D], F32, name="w_raw")
+
+        def load_h(t, c):
+            nc.sync.dma_start(out=h[t, c][:], in_=h_rows[:, t, c * CHUNK : (c + 1) * CHUNK])
+
+        nc.sync.dma_start(dst_list[:], offs)
+        for t in range(PACK):
+            load_h(t, 0)
+            if t > 0:
+                load_h(t, 1)
+            nc.sync.dma_start(out=dy[t][:], in_=dy_rows[:, t, :])
+            if t == 0:
+                load_h(t, 1)
+        for c in range(2, CHUNKS):
+            for t in range(PACK):
+                load_h(t, c)
+        nc.sync.dma_start(out=w_raw[:], in_=w_rows)
+        nc.sync.dma_start(src_list[:], offs2)
+
+        def relu(t, c):
+            if (t, c) == (0, 0):
+                nc.vector.tensor_scalar(h[t, c][:], h[t, c][:], 0.0, 2.0, MAX, MULT)
+            else:
+                nc.scalar.activation(h[t, c][:], h[t, c][:], RELU, scale=2.0)
+
+        dz = [keep.tile([P, PACK, n], F32, name="dz%d" % e0) for e0, n in EDGE_PIECES]
+        dz_b = [keep.tile([P, n, PACK], BF16, name="dzb%d" % e0, align_bytes=64) for e0, n in EDGE_PIECES]
+        dz_codes = [keep.tile([P, CHUNK], U32, name="dzc%d" % c, align_bytes=64) for c in range(CHUNKS)]
+        dz_scales = [keep.tile([P, CHUNK], U8, name="dzs%d" % c, align_bytes=64) for c in range(CHUNKS)]
+        dm = [keep.tile([P, E], F32, name="dm%d" % t) for t in range(PACK)]
+        w_b = keep.tile([P, D * PACK], BF16, name="w_b", align_bytes=64)
+        w_codes = keep.tile([P, D], U32, name="w_codes", align_bytes=64)
+        w_scales = keep.tile([P, D], U8, name="w_scales", align_bytes=64)
+
+        def gather_dz(k, t):
+            e0, n = EDGE_PIECES[k]
+            c, r = divmod(e0, CHUNK)
+            picked = dy[t][:].indirect(dst_list[:, e0 // PER_COL : (e0 + n) // PER_COL])
+            nc.vector.tensor_tensor(dz[k][:, t, :], picked, h[t, c][:, r : r + n], MULT)
+
+        def round_dz(k):
+            dst, src = interleaved_views(dz_b[k], dz[k])
+            if k == len(EDGE_PIECES) - 1:
+                nc.vector.tensor_copy(dst, src)
+            else:
+                nc.scalar.copy(dst, src)
+
+        def quantize_dz(k):
+            e0, n = EDGE_PIECES[k]
+            c, r = divmod(e0, CHUNK)
+            nc.vector.quantize_mx(
+                out=dz_codes[c][:, r : r + n].bitcast(E5M2),
+                scales=dz_scales[c][:, r : r + n],
+                in_=dz_b[k][:].rearrange("p e t -> p (e t)"),
+            )
+
+        def round_w():
+            dst = w_b[:].rearrange("p (u i m j) -> p u m j i", u=2, i=2, j=PACK)
+            src = w_raw[:].rearrange("p j (m u i) -> p u m j i", u=2, i=2)
+            for u in range(2):
+                nc.vector.tensor_copy(dst[:, u], src[:, u])
+
+        def quantize_w():
+            nc.vector.quantize_mx(out=w_codes[:].bitcast(E4M3), scales=w_scales[:], in_=w_b[:])
+
+        def product(t, c):
+            acc = psum.tile([P, CHUNK], F32, name="acc")
+            nc.tensor.matmul_mx(
+                out=acc[:],
+                lhsT=w_codes[:, t * P : (t + 1) * P].bitcast(E4M3),
+                lhsT_scale=w_scales[:, t * P : (t + 1) * P],
+                rhs=dz_codes[c][:].bitcast(E5M2),
+                rhs_scale=dz_scales[c][:],
+                start=True,
+                stop=True,
+            )
+            nc.scalar.copy(dm[t][:, c * CHUNK : (c + 1) * CHUNK], acc[:])
+
+        for t in range(PACK):
+            for c in range(2):
+                relu(t, c)
+                gather_dz(c, t)
+        for t in range(PACK):
+            relu(t, 2)
+            gather_dz(2, t)
+        round_dz(0)
+        for t in range(PACK):
+            relu(t, 3)
+        round_dz(1)
+        quantize_dz(0)
+        for t in range(PACK):
+            gather_dz(3, t)
+        round_w()
+        round_dz(2)
+        quantize_dz(1)
+        quantize_w()
+        round_dz(3)
+        for t in range(PACK):
+            gather_dz(4, t)
+        quantize_dz(2)
+        round_dz(4)
+        for t in range(PACK):
+            gather_dz(5, t)
+        quantize_dz(3)
+        round_dz(5)
+        quantize_dz(4)
+        quantize_dz(5)
+        for t in range(PACK):
+            for c in range(CHUNKS):
+                product(t, c)
+
+        y = [keep.tile([P, PACK, n], F32, name="y%d" % x0) for x0, n in NODE_PIECES]
+        y_b = [keep.tile([P, n, PACK], BF16, name="yb%d" % x0, align_bytes=64) for x0, n in NODE_PIECES]
+        y_codes = [keep.tile([P, n], U32, name="yc%d" % x0, align_bytes=64) for x0, n in NODE_PIECES]
+        y_scales = keep.tile([P, V], U8, name="y_scales", align_bytes=64)
+        steps = [(k, t) for k in range(len(NODE_PIECES)) for t in range(PACK)]
+        pairs = {}
+
+        def gather_dm(k, t):
+            x0, n = NODE_PIECES[k]
+            pairs[k, t] = ring.tile([P, 2 * n], F32, name="pairs")
+            picked = dm[t][:].indirect(src_list[:, 2 * x0 // PER_COL : 2 * (x0 + n) // PER_COL])
+            nc.vector.tensor_copy(pairs[k, t][:], picked)
+
+        def add_pairs(k, t):
+            both = pairs[k, t][:].rearrange("p (x j) -> p j x", j=2)
+            nc.vector.tensor_tensor(y[k][:, t, :], both[:, 0, :], both[:, 1, :], ADD)
+
+        def round_y(k):
+            x0, n = NODE_PIECES[k]
+            nc.sync.dma_start(out=y_rows[:, :, x0 : x0 + n], in_=y[k][:])
+            dst, src = interleaved_views(y_b[k], y[k])
+            if k == len(NODE_PIECES) - 1:
+                nc.vector.tensor_copy(dst, src)
+            else:
+                nc.scalar.copy(dst, src)
+
+        def quantize_y(k):
+            x0, n = NODE_PIECES[k]
+            nc.vector.quantize_mx(
+                out=y_codes[k][:].bitcast(E4M3),
+                scales=y_scales[:, x0 : x0 + n],
+                in_=y_b[k][:].rearrange("p x t -> p (x t)"),
+            )
+            nc.sync.dma_start(out=words_out[:, x0 : x0 + n], in_=y_codes[k][:].bitcast(I32))
+
+        gather_dm(*steps[0])
+        for s in range(len(steps)):
+            if s + 1 < len(steps):
+                gather_dm(*steps[s + 1])
+            k, t = steps[s]
+            add_pairs(k, t)
+            if t == PACK - 1:
+                round_y(k)
+                if k > 0:
+                    quantize_y(k - 1)
+        quantize_y(len(NODE_PIECES) - 1)
+        for q in range(4):
+            queue = nc.scalar if q % 2 else nc.sync
+            queue.dma_start(out=scales_out[4 * q : 4 * q + 4, :], in_=y_scales[32 * q : 32 * q + 4, :].bitcast(I32))

@@ -24,13 +24,15 @@ CHUNK = 512
 CHUNKS = E // CHUNK
 PER_COL = 16
 EDGE_PIECES = [(0, 512), (512, 512), (1024, 512), (1536, 256), (1792, 128), (1920, 128)]
-NODE_PIECES = [(0, 512), (512, 256), (768, 128), (896, 128)]
+SUM_STEPS = [(t, x0, 512) for t in range(PACK - 1) for x0 in (0, 512)] + [
+    (PACK - 1, x0, n) for x0, n in [(0, 256), (256, 256), (512, 256), (768, 128), (896, 128)]
+]
 
 
 def interleaved_views(dst, src):
     return (
-        dst[:].rearrange("p (c i) t -> p c t i", i=4),
-        src[:].rearrange("p t (c i) -> p c t i", i=4),
+        dst.rearrange("p (c i t) -> p c t i", i=4, t=PACK),
+        src.rearrange("p t (c i) -> p c t i", i=4),
     )
 
 
@@ -45,7 +47,6 @@ def tile_attend_gmp_pl_kernel(tc, dyT, hE, wm, offs, offs2, out_0, out_1, out_2)
 
     with ExitStack() as ctx:
         keep = ctx.enter_context(tc.tile_pool(name="keep", bufs=1))
-        ring = ctx.enter_context(tc.tile_pool(name="ring", bufs=3))
         psum = ctx.enter_context(tc.psum_pool(name="psum", bufs=8))
 
         dst_list = keep.tile([P, E // PER_COL], U16, name="dst_list")
@@ -78,13 +79,16 @@ def tile_attend_gmp_pl_kernel(tc, dyT, hE, wm, offs, offs2, out_0, out_1, out_2)
                 nc.scalar.activation(h[t, c][:], h[t, c][:], RELU, scale=2.0)
 
         dz = [keep.tile([P, PACK, n], F32, name="dz%d" % e0) for e0, n in EDGE_PIECES]
-        dz_b = [keep.tile([P, n, PACK], BF16, name="dzb%d" % e0, align_bytes=64) for e0, n in EDGE_PIECES]
+        late_b = keep.tile([P, (PACK - 1) * D], BF16, name="late_b", align_bytes=64)
+        dz_b = [keep.tile([P, n * PACK], BF16, name="dzb%d" % e0, align_bytes=64)[:] for e0, n in EDGE_PIECES[:-2]]
+        dz_b = dz_b + [late_b[:, 0:512], late_b[:, 512:1024]]
         dz_codes = [keep.tile([P, CHUNK], U32, name="dzc%d" % c, align_bytes=64) for c in range(CHUNKS)]
         dz_scales = [keep.tile([P, CHUNK], U8, name="dzs%d" % c, align_bytes=64) for c in range(CHUNKS)]
         dm = [keep.tile([P, E], F32, name="dm%d" % t) for t in range(PACK)]
-        w_b = keep.tile([P, D * PACK], BF16, name="w_b", align_bytes=64)
+        w0_b = keep.tile([P, D], BF16, name="w0_b", align_bytes=64)
         w_codes = keep.tile([P, D], U32, name="w_codes", align_bytes=64)
         w_scales = keep.tile([P, D], U8, name="w_scales", align_bytes=64)
+        w_dealt = w_raw[:].rearrange("p j (m t) -> p m j t", t=PACK)
 
         def gather_dz(k, t):
             e0, n = EDGE_PIECES[k]
@@ -93,29 +97,21 @@ def tile_attend_gmp_pl_kernel(tc, dyT, hE, wm, offs, offs2, out_0, out_1, out_2)
             nc.vector.tensor_tensor(dz[k][:, t, :], picked, h[t, c][:, r : r + n], MULT)
 
         def round_dz(k):
-            dst, src = interleaved_views(dz_b[k], dz[k])
+            dst, src = interleaved_views(dz_b[k], dz[k][:])
             if k == len(EDGE_PIECES) - 1:
                 nc.vector.tensor_copy(dst, src)
             else:
                 nc.scalar.copy(dst, src)
 
-        def quantize_dz(k):
-            e0, n = EDGE_PIECES[k]
+        def quantize_dz(e0, n, rounded):
             c, r = divmod(e0, CHUNK)
             nc.vector.quantize_mx(
-                out=dz_codes[c][:, r : r + n].bitcast(E5M2),
-                scales=dz_scales[c][:, r : r + n],
-                in_=dz_b[k][:].rearrange("p e t -> p (e t)"),
+                out=dz_codes[c][:, r : r + n].bitcast(E5M2), scales=dz_scales[c][:, r : r + n], in_=rounded
             )
 
-        def round_w():
-            dst = w_b[:].rearrange("p (u i m j) -> p u m j i", u=2, i=2, j=PACK)
-            src = w_raw[:].rearrange("p j (m u i) -> p u m j i", u=2, i=2)
-            for u in range(2):
-                nc.vector.tensor_copy(dst[:, u], src[:, u])
-
-        def quantize_w():
-            nc.vector.quantize_mx(out=w_codes[:].bitcast(E4M3), scales=w_scales[:], in_=w_b[:])
+        def quantize_w(t0, t1, rounded):
+            cols = slice(t0 * P, t1 * P)
+            nc.vector.quantize_mx(out=w_codes[:, cols].bitcast(E4M3), scales=w_scales[:, cols], in_=rounded)
 
         def product(t, c):
             acc = psum.tile([P, CHUNK], F32, name="acc")
@@ -137,78 +133,82 @@ def tile_attend_gmp_pl_kernel(tc, dyT, hE, wm, offs, offs2, out_0, out_1, out_2)
         for t in range(PACK):
             relu(t, 2)
             gather_dz(2, t)
-        round_dz(0)
         for t in range(PACK):
             relu(t, 3)
+        round_dz(0)
+        nc.scalar.copy(w0_b[:].rearrange("p (m j) -> p m j", j=PACK), w_dealt[:, :, :, 0])
         round_dz(1)
-        quantize_dz(0)
-        for t in range(PACK):
-            gather_dz(3, t)
-        round_w()
-        round_dz(2)
-        quantize_dz(1)
-        quantize_w()
-        round_dz(3)
-        for t in range(PACK):
-            gather_dz(4, t)
-        quantize_dz(2)
-        round_dz(4)
-        for t in range(PACK):
-            gather_dz(5, t)
-        quantize_dz(3)
-        round_dz(5)
-        quantize_dz(4)
-        quantize_dz(5)
-        for t in range(PACK):
+        quantize_dz(*EDGE_PIECES[0], dz_b[0])
+        quantize_w(0, 1, w0_b[:])
+        for k in range(3, len(EDGE_PIECES)):
+            for t in range(PACK):
+                gather_dz(k, t)
+            round_dz(k - 1)
+            quantize_dz(*EDGE_PIECES[k - 2], dz_b[k - 2])
+        round_dz(len(EDGE_PIECES) - 1)
+        quantize_dz(EDGE_PIECES[-2][0], 256, late_b[:, 0:1024])
+        for c in range(CHUNKS):
+            product(0, c)
+        nc.vector.tensor_copy(late_b[:, 0:D].rearrange("p (m j) -> p m j", j=PACK), w_dealt[:, :, :, 1])
+        nc.vector.tensor_copy(
+            late_b[:, D : 3 * D].rearrange("p (t m j) -> p m j t", t=2, j=PACK), w_dealt[:, :, :, 2:4]
+        )
+        quantize_w(1, 2, late_b[:, 0:D])
+        quantize_w(2, 4, late_b[:, D : 3 * D])
+        for t in range(1, PACK):
             for c in range(CHUNKS):
                 product(t, c)
 
-        y = [keep.tile([P, PACK, n], F32, name="y%d" % x0) for x0, n in NODE_PIECES]
-        y_b = [keep.tile([P, n, PACK], BF16, name="yb%d" % x0, align_bytes=64) for x0, n in NODE_PIECES]
-        y_codes = [keep.tile([P, n], U32, name="yc%d" % x0, align_bytes=64) for x0, n in NODE_PIECES]
+        y = keep.tile([P, PACK, V], F32, name="y")
+        y_b = keep.tile([P, V * PACK], BF16, name="y_b", align_bytes=64)
+        y_codes = keep.tile([P, V], U32, name="y_codes", align_bytes=64)
         y_scales = keep.tile([P, V], U8, name="y_scales", align_bytes=64)
-        steps = [(k, t) for k in range(len(NODE_PIECES)) for t in range(PACK)]
-        pairs = {}
+        pairs = [keep.tile([P, 2 * n], F32, name="pairs%d" % s) for s, (t, x0, n) in enumerate(SUM_STEPS)]
+        last = len(SUM_STEPS) - 1
 
-        def gather_dm(k, t):
-            x0, n = NODE_PIECES[k]
-            pairs[k, t] = ring.tile([P, 2 * n], F32, name="pairs")
+        def gather_dm(s):
+            t, x0, n = SUM_STEPS[s]
             picked = dm[t][:].indirect(src_list[:, 2 * x0 // PER_COL : 2 * (x0 + n) // PER_COL])
-            nc.vector.tensor_copy(pairs[k, t][:], picked)
+            nc.vector.tensor_copy(pairs[s][:], picked)
 
-        def add_pairs(k, t):
-            both = pairs[k, t][:].rearrange("p (x j) -> p j x", j=2)
-            nc.vector.tensor_tensor(y[k][:, t, :], both[:, 0, :], both[:, 1, :], ADD)
+        def add_pairs(s):
+            t, x0, n = SUM_STEPS[s]
+            both = pairs[s][:].rearrange("p (x j) -> p j x", j=2)
+            engine = nc.vector if s == last else nc.gpsimd
+            engine.tensor_tensor(y[:, t, x0 : x0 + n], both[:, 0, :], both[:, 1, :], ADD)
 
-        def round_y(k):
-            x0, n = NODE_PIECES[k]
-            nc.sync.dma_start(out=y_rows[:, :, x0 : x0 + n], in_=y[k][:])
-            dst, src = interleaved_views(y_b[k], y[k])
-            if k == len(NODE_PIECES) - 1:
+        def store_y(t, x0, n):
+            nc.sync.dma_start(out=y_rows[:, t, x0 : x0 + n], in_=y[:, t, x0 : x0 + n])
+
+        def round_y(s):
+            t, x0, n = SUM_STEPS[s]
+            dst, src = interleaved_views(y_b[:, PACK * x0 : PACK * (x0 + n)], y[:, :, x0 : x0 + n])
+            if s == last:
                 nc.vector.tensor_copy(dst, src)
             else:
                 nc.scalar.copy(dst, src)
 
-        def quantize_y(k):
-            x0, n = NODE_PIECES[k]
+        def quantize_y(x0, n):
             nc.vector.quantize_mx(
-                out=y_codes[k][:].bitcast(E4M3),
+                out=y_codes[:, x0 : x0 + n].bitcast(E4M3),
                 scales=y_scales[:, x0 : x0 + n],
-                in_=y_b[k][:].rearrange("p x t -> p (x t)"),
+                in_=y_b[:, PACK * x0 : PACK * (x0 + n)],
             )
-            nc.sync.dma_start(out=words_out[:, x0 : x0 + n], in_=y_codes[k][:].bitcast(I32))
+            nc.sync.dma_start(out=words_out[:, x0 : x0 + n], in_=y_codes[:, x0 : x0 + n].bitcast(I32))
 
-        gather_dm(*steps[0])
-        for s in range(len(steps)):
-            if s + 1 < len(steps):
-                gather_dm(*steps[s + 1])
-            k, t = steps[s]
-            add_pairs(k, t)
+        gather_dm(0)
+        for s in range(last + 1):
+            if s < last:
+                gather_dm(s + 1)
+            t, x0, n = SUM_STEPS[s]
+            add_pairs(s)
+            if s < last - 1:
+                store_y(t, x0, n)
             if t == PACK - 1:
-                round_y(k)
-                if k > 0:
-                    quantize_y(k - 1)
-        quantize_y(len(NODE_PIECES) - 1)
+                round_y(s)
+        store_y(PACK - 1, 768, 256)
+        for x0 in range(0, V, 256):
+            quantize_y(x0, 256)
         for q in range(4):
             queue = nc.scalar if q % 2 else nc.sync
             queue.dma_start(out=scales_out[4 * q : 4 * q + 4, :], in_=y_scales[32 * q : 32 * q + 4, :].bitcast(I32))

@@ -23,9 +23,11 @@ PACK = 4
 CHUNK = 512
 CHUNKS = E // CHUNK
 PER_COL = 16
-EDGE_PIECES = [(0, 512), (512, 512), (1024, 512), (1536, 256), (1792, 128), (1920, 128)]
-SUM_STEPS = [(t, x0, 512) for t in range(PACK - 1) for x0 in (0, 512)] + [
-    (PACK - 1, x0, n) for x0, n in [(0, 256), (256, 256), (512, 256), (768, 128), (896, 128)]
+HALF = CHUNK // 2
+EDGE_PIECES = [(0, 512), (512, 512), (1024, 512), (1536, 256), (1792, 256)]
+NODE_PIECES = [(0, 512), (512, 256), (768, 128), (896, 128)]
+GATHER_STEPS = [(t, ks) for t in range(2) for ks in ([0], [1, 2, 3])] + [
+    (t, [k]) for k in range(len(NODE_PIECES)) for t in range(2, PACK)
 ]
 
 
@@ -79,9 +81,8 @@ def tile_attend_gmp_pl_kernel(tc, dyT, hE, wm, offs, offs2, out_0, out_1, out_2)
                 nc.scalar.activation(h[t, c][:], h[t, c][:], RELU, scale=2.0)
 
         dz = [keep.tile([P, PACK, n], F32, name="dz%d" % e0) for e0, n in EDGE_PIECES]
-        late_b = keep.tile([P, (PACK - 1) * D], BF16, name="late_b", align_bytes=64)
-        dz_b = [keep.tile([P, n * PACK], BF16, name="dzb%d" % e0, align_bytes=64)[:] for e0, n in EDGE_PIECES[:-2]]
-        dz_b = dz_b + [late_b[:, 0:512], late_b[:, 512:1024]]
+        dz_b = [keep.tile([P, CHUNK * PACK], BF16, name="dzb%d" % c, align_bytes=64) for c in range(CHUNKS)]
+        late_b = dz_b[CHUNKS - 1]
         dz_codes = [keep.tile([P, CHUNK], U32, name="dzc%d" % c, align_bytes=64) for c in range(CHUNKS)]
         dz_scales = [keep.tile([P, CHUNK], U8, name="dzs%d" % c, align_bytes=64) for c in range(CHUNKS)]
         dm = [keep.tile([P, E], F32, name="dm%d" % t) for t in range(PACK)]
@@ -97,17 +98,14 @@ def tile_attend_gmp_pl_kernel(tc, dyT, hE, wm, offs, offs2, out_0, out_1, out_2)
             nc.vector.tensor_tensor(dz[k][:, t, :], picked, h[t, c][:, r : r + n], MULT)
 
         def round_dz(k):
-            dst, src = interleaved_views(dz_b[k], dz[k][:])
-            if k == len(EDGE_PIECES) - 1:
-                nc.vector.tensor_copy(dst, src)
-            else:
-                nc.scalar.copy(dst, src)
-
-        def quantize_dz(e0, n, rounded):
+            e0, n = EDGE_PIECES[k]
             c, r = divmod(e0, CHUNK)
-            nc.vector.quantize_mx(
-                out=dz_codes[c][:, r : r + n].bitcast(E5M2), scales=dz_scales[c][:, r : r + n], in_=rounded
-            )
+            copy = nc.vector.tensor_copy if k == len(EDGE_PIECES) - 1 else nc.scalar.copy
+            for a in range(0, n, HALF):
+                copy(*interleaved_views(dz_b[c][:, PACK * (r + a) : PACK * (r + a + HALF)], dz[k][:, :, a : a + HALF]))
+
+        def quantize_dz(c):
+            nc.vector.quantize_mx(out=dz_codes[c][:].bitcast(E5M2), scales=dz_scales[c][:], in_=dz_b[c][:])
 
         def quantize_w(t0, t1, rounded):
             cols = slice(t0 * P, t1 * P)
@@ -138,15 +136,15 @@ def tile_attend_gmp_pl_kernel(tc, dyT, hE, wm, offs, offs2, out_0, out_1, out_2)
         round_dz(0)
         nc.scalar.copy(w0_b[:].rearrange("p (m j) -> p m j", j=PACK), w_dealt[:, :, :, 0])
         round_dz(1)
-        quantize_dz(*EDGE_PIECES[0], dz_b[0])
+        quantize_dz(0)
         quantize_w(0, 1, w0_b[:])
-        for k in range(3, len(EDGE_PIECES)):
+        for k in (3, 4):
             for t in range(PACK):
                 gather_dz(k, t)
             round_dz(k - 1)
-            quantize_dz(*EDGE_PIECES[k - 2], dz_b[k - 2])
-        round_dz(len(EDGE_PIECES) - 1)
-        quantize_dz(EDGE_PIECES[-2][0], 256, late_b[:, 0:1024])
+            quantize_dz(k - 2)
+        round_dz(4)
+        quantize_dz(3)
         for c in range(CHUNKS):
             product(0, c)
         nc.vector.tensor_copy(late_b[:, 0:D].rearrange("p (m j) -> p m j", j=PACK), w_dealt[:, :, :, 1])
@@ -155,38 +153,43 @@ def tile_attend_gmp_pl_kernel(tc, dyT, hE, wm, offs, offs2, out_0, out_1, out_2)
         )
         quantize_w(1, 2, late_b[:, 0:D])
         quantize_w(2, 4, late_b[:, D : 3 * D])
-        for t in range(1, PACK):
-            for c in range(CHUNKS):
+        for c in range(CHUNKS):
+            product(1, c)
+        for c in range(CHUNKS):
+            for t in (3, 2):
                 product(t, c)
 
-        y = keep.tile([P, PACK, V], F32, name="y")
+        y = [keep.tile([P, PACK, n], F32, name="y%d" % x0) for x0, n in NODE_PIECES]
         y_b = keep.tile([P, V * PACK], BF16, name="y_b", align_bytes=64)
         y_codes = keep.tile([P, V], U32, name="y_codes", align_bytes=64)
         y_scales = keep.tile([P, V], U8, name="y_scales", align_bytes=64)
-        pairs = [keep.tile([P, 2 * n], F32, name="pairs%d" % s) for s, (t, x0, n) in enumerate(SUM_STEPS)]
-        last = len(SUM_STEPS) - 1
+        ring = [keep.tile([P, V], F32, name="ring%d" % r) for r in range(3)]
+        pairs = {}
+        last = len(NODE_PIECES) - 1
 
         def gather_dm(s):
-            t, x0, n = SUM_STEPS[s]
-            picked = dm[t][:].indirect(src_list[:, 2 * x0 // PER_COL : 2 * (x0 + n) // PER_COL])
-            nc.vector.tensor_copy(pairs[s][:], picked)
+            t, ks = GATHER_STEPS[s]
+            first = NODE_PIECES[ks[0]][0]
+            end = sum(NODE_PIECES[ks[-1]])
+            picked = ring[s % len(ring)][:, 0 : 2 * (end - first)]
+            window = dm[t][:].indirect(src_list[:, 2 * first // PER_COL : 2 * end // PER_COL])
+            nc.vector.tensor_copy(picked, window)
+            for k in ks:
+                x0, n = NODE_PIECES[k]
+                pairs[t, k] = picked[:, 2 * (x0 - first) : 2 * (x0 - first + n)]
 
-        def add_pairs(s):
-            t, x0, n = SUM_STEPS[s]
-            both = pairs[s][:].rearrange("p (x j) -> p j x", j=2)
-            engine = nc.vector if s == last else nc.gpsimd
-            engine.tensor_tensor(y[:, t, x0 : x0 + n], both[:, 0, :], both[:, 1, :], ADD)
+        def add_pairs(t, k):
+            x0, n = NODE_PIECES[k]
+            both = pairs[t, k].rearrange("p (x j) -> p j x", j=2)
+            engine = nc.vector if k == last and t >= 2 else nc.gpsimd
+            engine.tensor_tensor(y[k][:, t, :], both[:, 0, :], both[:, 1, :], ADD)
+            if t % 2 == 1:
+                nc.sync.dma_start(out=y_rows[:, t - 1 : t + 1, x0 : x0 + n], in_=y[k][:, t - 1 : t + 1, :])
 
-        def store_y(t, x0, n):
-            nc.sync.dma_start(out=y_rows[:, t, x0 : x0 + n], in_=y[:, t, x0 : x0 + n])
-
-        def round_y(s):
-            t, x0, n = SUM_STEPS[s]
-            dst, src = interleaved_views(y_b[:, PACK * x0 : PACK * (x0 + n)], y[:, :, x0 : x0 + n])
-            if s == last:
-                nc.vector.tensor_copy(dst, src)
-            else:
-                nc.scalar.copy(dst, src)
+        def round_y(k):
+            x0, n = NODE_PIECES[k]
+            copy = nc.vector.tensor_copy if k == last else nc.scalar.copy
+            copy(*interleaved_views(y_b[:, PACK * x0 : PACK * (x0 + n)], y[k][:]))
 
         def quantize_y(x0, n):
             nc.vector.quantize_mx(
@@ -197,18 +200,15 @@ def tile_attend_gmp_pl_kernel(tc, dyT, hE, wm, offs, offs2, out_0, out_1, out_2)
             nc.sync.dma_start(out=words_out[:, x0 : x0 + n], in_=y_codes[:, x0 : x0 + n].bitcast(I32))
 
         gather_dm(0)
-        for s in range(last + 1):
-            if s < last:
+        for s, (t, ks) in enumerate(GATHER_STEPS):
+            if s + 1 < len(GATHER_STEPS):
                 gather_dm(s + 1)
-            t, x0, n = SUM_STEPS[s]
-            add_pairs(s)
-            if s < last - 1:
-                store_y(t, x0, n)
+            for k in ks:
+                add_pairs(t, k)
             if t == PACK - 1:
-                round_y(s)
-        store_y(PACK - 1, 768, 256)
-        for x0 in range(0, V, 256):
-            quantize_y(x0, 256)
+                round_y(ks[0])
+        for x0, n in [(0, 512), (512, 256), (768, 256)]:
+            quantize_y(x0, n)
         for q in range(4):
             queue = nc.scalar if q % 2 else nc.sync
             queue.dma_start(out=scales_out[4 * q : 4 * q + 4, :], in_=y_scales[32 * q : 32 * q + 4, :].bitcast(I32))

@@ -68,9 +68,11 @@ def tile_attend_gmp_pl_kernel(tc, dyT, hE, wm, offs, offs2, out_0, out_1, out_2)
             nc.sync.dma_start(out=dy[t][:], in_=dy_rows[:, t, :])
             if t == 0:
                 load_h(t, 1)
+                load_h(t, 2)
         for c in range(2, CHUNKS):
             for t in range(PACK):
-                load_h(t, c)
+                if (t, c) != (0, 2):
+                    load_h(t, c)
         nc.sync.dma_start(out=w_raw[:], in_=w_rows)
         nc.sync.dma_start(src_list[:], offs2)
 
@@ -102,7 +104,8 @@ def tile_attend_gmp_pl_kernel(tc, dyT, hE, wm, offs, offs2, out_0, out_1, out_2)
             c, r = divmod(e0, CHUNK)
             copy = nc.vector.tensor_copy if k == len(EDGE_PIECES) - 1 else nc.scalar.copy
             for a in range(0, n, HALF):
-                copy(*interleaved_views(dz_b[c][:, PACK * (r + a) : PACK * (r + a + HALF)], dz[k][:, :, a : a + HALF]))
+                b = min(a + HALF, n)
+                copy(*interleaved_views(dz_b[c][:, PACK * (r + a) : PACK * (r + b)], dz[k][:, :, a:b]))
 
         def quantize_dz(c):
             nc.vector.quantize_mx(out=dz_codes[c][:].bitcast(E5M2), scales=dz_scales[c][:], in_=dz_b[c][:])
@@ -125,10 +128,10 @@ def tile_attend_gmp_pl_kernel(tc, dyT, hE, wm, offs, offs2, out_0, out_1, out_2)
             nc.scalar.copy(dm[t][:, c * CHUNK : (c + 1) * CHUNK], acc[:])
 
         for t in range(PACK):
-            for c in range(2):
+            for c in range(3 if t == 0 else 2):
                 relu(t, c)
                 gather_dz(c, t)
-        for t in range(PACK):
+        for t in range(1, PACK):
             relu(t, 2)
             gather_dz(2, t)
         for t in range(PACK):

@@ -16,19 +16,16 @@ E5M2 = mybir.dt.float8_e5m2_x4
 MULT = mybir.AluOpType.mult
 ADD = mybir.AluOpType.add
 MAX = mybir.AluOpType.max
-RELU = mybir.ActivationFunctionType.Relu
+COPY = mybir.ActivationFunctionType.Copy
 
 P = 128
 PACK = 4
 CHUNK = 512
 CHUNKS = E // CHUNK
 PER_COL = 16
-HALF = CHUNK // 2
-EDGE_PIECES = [(0, 512), (512, 512), (1024, 512), (1536, 256), (1792, 256)]
-NODE_PIECES = [(0, 512), (512, 256), (768, 128), (896, 128)]
-GATHER_STEPS = [(t, ks) for t in range(2) for ks in ([0], [1, 2, 3])] + [
-    (t, [k]) for k in range(len(NODE_PIECES)) for t in range(2, PACK)
-]
+H_LOADS = [(0, 256), (256, 256), (512, 512), (1024, 512), (1536, 256), (1792, 256)]
+EDGE_PIECES = [(0, 256), (256, 256), (512, 512), (1024, 512), (1536, 256), (1792, 128), (1920, 128)]
+NODE_PIECES = [(0, 256), (256, 256), (512, 256), (768, 128), (896, 128)]
 
 
 def interleaved_views(dst, src):
@@ -54,164 +51,158 @@ def tile_attend_gmp_pl_kernel(tc, dyT, hE, wm, offs, offs2, out_0, out_1, out_2)
         dst_list = keep.tile([P, E // PER_COL], U16, name="dst_list")
         src_list = keep.tile([P, E // PER_COL], U16, name="src_list")
         dy = [keep.tile([P, V], F32, name="dy%d" % t) for t in range(PACK)]
-        h = {(t, c): keep.tile([P, CHUNK], F32, name="h%d_%d" % (t, c)) for t in range(PACK) for c in range(CHUNKS)}
+        h = [keep.tile([P, PACK, n], F32, name="h%d" % e0) for e0, n in H_LOADS]
         w_raw = keep.tile([P, PACK, D], F32, name="w_raw")
+        twos = keep.tile([P, CHUNK], F32, name="twos")
 
-        def load_h(t, c):
-            nc.sync.dma_start(out=h[t, c][:], in_=h_rows[:, t, c * CHUNK : (c + 1) * CHUNK])
-
+        nc.gpsimd.memset(twos[:], 2.0)
         nc.sync.dma_start(dst_list[:], offs)
         for t in range(PACK):
-            load_h(t, 0)
-            if t > 0:
-                load_h(t, 1)
             nc.sync.dma_start(out=dy[t][:], in_=dy_rows[:, t, :])
-            if t == 0:
-                load_h(t, 1)
-                load_h(t, 2)
-        for c in range(2, CHUNKS):
-            for t in range(PACK):
-                if (t, c) != (0, 2):
-                    load_h(t, c)
-        nc.sync.dma_start(out=w_raw[:], in_=w_rows)
+        for k, (e0, n) in enumerate(H_LOADS):
+            if e0 == 3 * CHUNK:
+                nc.sync.dma_start(out=w_raw[:], in_=w_rows)
+            nc.sync.dma_start(out=h[k][:], in_=h_rows[:, :, e0 : e0 + n])
         nc.sync.dma_start(src_list[:], offs2)
 
-        def relu(t, c):
-            if (t, c) == (0, 0):
-                nc.vector.tensor_scalar(h[t, c][:], h[t, c][:], 0.0, 2.0, MAX, MULT)
-            else:
-                nc.scalar.activation(h[t, c][:], h[t, c][:], RELU, scale=2.0)
-
-        dz = [keep.tile([P, PACK, n], F32, name="dz%d" % e0) for e0, n in EDGE_PIECES]
-        dz_b = [keep.tile([P, CHUNK * PACK], BF16, name="dzb%d" % c, align_bytes=64) for c in range(CHUNKS)]
-        late_b = dz_b[CHUNKS - 1]
+        g = [keep.tile([P, PACK, CHUNK], F32, name="g%d" % c) for c in range(CHUNKS - 1)]
+        g.append(g[0])
+        dz_b = [keep.tile([P, n * PACK], BF16, name="dzb%d" % e0, align_bytes=64) for e0, n in EDGE_PIECES]
         dz_codes = [keep.tile([P, CHUNK], U32, name="dzc%d" % c, align_bytes=64) for c in range(CHUNKS)]
         dz_scales = [keep.tile([P, CHUNK], U8, name="dzs%d" % c, align_bytes=64) for c in range(CHUNKS)]
         dm = [keep.tile([P, E], F32, name="dm%d" % t) for t in range(PACK)]
-        w0_b = keep.tile([P, D], BF16, name="w0_b", align_bytes=64)
+        w_b = [keep.tile([P, D], BF16, name="wb%d" % t, align_bytes=64) for t in range(PACK)]
         w_codes = keep.tile([P, D], U32, name="w_codes", align_bytes=64)
         w_scales = keep.tile([P, D], U8, name="w_scales", align_bytes=64)
         w_dealt = w_raw[:].rearrange("p j (m t) -> p m j t", t=PACK)
 
-        def gather_dz(k, t):
-            e0, n = EDGE_PIECES[k]
+        def gather_dy(on_vector, t, e0, n):
             c, r = divmod(e0, CHUNK)
             picked = dy[t][:].indirect(dst_list[:, e0 // PER_COL : (e0 + n) // PER_COL])
-            nc.vector.tensor_tensor(dz[k][:, t, :], picked, h[t, c][:, r : r + n], MULT)
+            if on_vector:
+                nc.vector.tensor_tensor(g[c][:, t, r : r + n], picked, twos[:, 0:n], MULT)
+            else:
+                nc.scalar.activation(g[c][:, t, r : r + n], picked, COPY, scale=2.0)
 
-        def round_dz(k):
+        def form_dz(k):
             e0, n = EDGE_PIECES[k]
             c, r = divmod(e0, CHUNK)
-            copy = nc.vector.tensor_copy if k == len(EDGE_PIECES) - 1 else nc.scalar.copy
-            for a in range(0, n, HALF):
-                b = min(a + HALF, n)
-                copy(*interleaved_views(dz_b[c][:, PACK * (r + a) : PACK * (r + b)], dz[k][:, :, a:b]))
+            load = max(i for i, (l0, ln) in enumerate(H_LOADS) if l0 <= e0)
+            a = e0 - H_LOADS[load][0]
+            nc.vector.scalar_tensor_tensor(
+                out=dz_b[k][:].rearrange("p (e t) -> p e t", t=PACK),
+                in0=h[load][:, :, a : a + n].rearrange("p t e -> p e t"),
+                scalar=0.0,
+                in1=g[c][:, :, r : r + n].rearrange("p t e -> p e t"),
+                op0=MAX,
+                op1=MULT,
+            )
 
-        def quantize_dz(c):
-            nc.vector.quantize_mx(out=dz_codes[c][:].bitcast(E5M2), scales=dz_scales[c][:], in_=dz_b[c][:])
+        def quantize_dz(k):
+            e0, n = EDGE_PIECES[k]
+            c, r = divmod(e0, CHUNK)
+            nc.vector.quantize_mx(
+                out=dz_codes[c][:, r : r + n].bitcast(E5M2), scales=dz_scales[c][:, r : r + n], in_=dz_b[k][:]
+            )
 
-        def quantize_w(t0, t1, rounded):
-            cols = slice(t0 * P, t1 * P)
-            nc.vector.quantize_mx(out=w_codes[:, cols].bitcast(E4M3), scales=w_scales[:, cols], in_=rounded)
+        def round_w(t):
+            nc.scalar.copy(w_b[t][:].rearrange("p (m j) -> p m j", j=PACK), w_dealt[:, :, :, t])
 
-        def product(t, c):
+        def quantize_w(t):
+            cols = slice(t * P, (t + 1) * P)
+            nc.vector.quantize_mx(out=w_codes[:, cols].bitcast(E4M3), scales=w_scales[:, cols], in_=w_b[t][:])
+
+        def product(t, e0, n):
+            c, r = divmod(e0, CHUNK)
             acc = psum.tile([P, CHUNK], F32, name="acc")
             nc.tensor.matmul_mx(
-                out=acc[:],
+                out=acc[:, 0:n],
                 lhsT=w_codes[:, t * P : (t + 1) * P].bitcast(E4M3),
                 lhsT_scale=w_scales[:, t * P : (t + 1) * P],
-                rhs=dz_codes[c][:].bitcast(E5M2),
-                rhs_scale=dz_scales[c][:],
+                rhs=dz_codes[c][:, r : r + n].bitcast(E5M2),
+                rhs_scale=dz_scales[c][:, r : r + n],
                 start=True,
                 stop=True,
             )
-            nc.scalar.copy(dm[t][:, c * CHUNK : (c + 1) * CHUNK], acc[:])
+            nc.scalar.copy(dm[t][:, e0 : e0 + n], acc[:, 0:n])
 
         for t in range(PACK):
-            for c in range(3 if t == 0 else 2):
-                relu(t, c)
-                gather_dz(c, t)
-        for t in range(1, PACK):
-            relu(t, 2)
-            gather_dz(2, t)
+            gather_dy(True, t, 0, CHUNK)
+            for c in (1, 2):
+                gather_dy(False, t, c * CHUNK, CHUNK)
+        form_dz(0)
+        for k in (1, 2, 3):
+            form_dz(k)
+            quantize_dz(k - 1)
         for t in range(PACK):
-            relu(t, 3)
-        round_dz(0)
-        nc.scalar.copy(w0_b[:].rearrange("p (m j) -> p m j", j=PACK), w_dealt[:, :, :, 0])
-        round_dz(1)
-        quantize_dz(0)
-        quantize_w(0, 1, w0_b[:])
-        for k in (3, 4):
-            for t in range(PACK):
-                gather_dz(k, t)
-            round_dz(k - 1)
-            quantize_dz(k - 2)
-        round_dz(4)
+            gather_dy(False, t, 3 * CHUNK, CHUNK // 2)
+        round_w(0)
+        for t in range(PACK):
+            gather_dy(False, t, 3 * CHUNK + CHUNK // 2, CHUNK // 2)
+        form_dz(4)
         quantize_dz(3)
-        for c in range(CHUNKS):
-            product(0, c)
-        nc.vector.tensor_copy(late_b[:, 0:D].rearrange("p (m j) -> p m j", j=PACK), w_dealt[:, :, :, 1])
-        nc.vector.tensor_copy(
-            late_b[:, D : 3 * D].rearrange("p (t m j) -> p m j t", t=2, j=PACK), w_dealt[:, :, :, 2:4]
-        )
-        quantize_w(1, 2, late_b[:, 0:D])
-        quantize_w(2, 4, late_b[:, D : 3 * D])
-        for c in range(CHUNKS):
-            product(1, c)
-        for c in range(CHUNKS):
-            for t in (3, 2):
-                product(t, c)
+        quantize_w(0)
+        for c in range(CHUNKS - 1):
+            product(0, c * CHUNK, CHUNK)
+        for k in (5, 6):
+            form_dz(k)
+            quantize_dz(k - 1)
+            product(0, *EDGE_PIECES[k - 1])
+        quantize_dz(6)
+        product(0, *EDGE_PIECES[6])
+        for t in range(1, PACK):
+            round_w(t)
+            quantize_w(t)
+        for t in (2, 1, 3):
+            for c in range(CHUNKS):
+                product(t, c * CHUNK, CHUNK)
 
+        picked = {(t, k): keep.tile([P, 2 * n], F32, name="pk%d_%d" % (t, x0)) for t in range(PACK) for k, (x0, n) in enumerate(NODE_PIECES)}
         y = [keep.tile([P, PACK, n], F32, name="y%d" % x0) for x0, n in NODE_PIECES]
-        y_b = keep.tile([P, V * PACK], BF16, name="y_b", align_bytes=64)
+        y_b = [keep.tile([P, n * PACK], BF16, name="yb%d" % x0, align_bytes=64) for x0, n in NODE_PIECES]
         y_codes = keep.tile([P, V], U32, name="y_codes", align_bytes=64)
         y_scales = keep.tile([P, V], U8, name="y_scales", align_bytes=64)
-        ring = [keep.tile([P, V], F32, name="ring%d" % r) for r in range(3)]
-        pairs = {}
         last = len(NODE_PIECES) - 1
 
-        def gather_dm(s):
-            t, ks = GATHER_STEPS[s]
-            first = NODE_PIECES[ks[0]][0]
-            end = sum(NODE_PIECES[ks[-1]])
-            picked = ring[s % len(ring)][:, 0 : 2 * (end - first)]
-            window = dm[t][:].indirect(src_list[:, 2 * first // PER_COL : 2 * end // PER_COL])
-            nc.vector.tensor_copy(picked, window)
-            for k in ks:
-                x0, n = NODE_PIECES[k]
-                pairs[t, k] = picked[:, 2 * (x0 - first) : 2 * (x0 - first + n)]
+        def gather_dm(on_vector, t, k):
+            x0, n = NODE_PIECES[k]
+            window = dm[t][:].indirect(src_list[:, 2 * x0 // PER_COL : 2 * (x0 + n) // PER_COL])
+            if on_vector:
+                nc.vector.tensor_copy(picked[t, k][:], window)
+            else:
+                nc.scalar.activation(picked[t, k][:], window, COPY)
 
         def add_pairs(t, k):
-            x0, n = NODE_PIECES[k]
-            both = pairs[t, k].rearrange("p (x j) -> p j x", j=2)
-            engine = nc.vector if k == last and t >= 2 else nc.gpsimd
+            both = picked[t, k][:].rearrange("p (x j) -> p j x", j=2)
+            engine = nc.vector if k == last and t % 2 == 1 else nc.gpsimd
             engine.tensor_tensor(y[k][:, t, :], both[:, 0, :], both[:, 1, :], ADD)
-            if t % 2 == 1:
-                nc.sync.dma_start(out=y_rows[:, t - 1 : t + 1, x0 : x0 + n], in_=y[k][:, t - 1 : t + 1, :])
 
-        def round_y(k):
+        def finish(k):
             x0, n = NODE_PIECES[k]
-            copy = nc.vector.tensor_copy if k == last else nc.scalar.copy
-            copy(*interleaved_views(y_b[:, PACK * x0 : PACK * (x0 + n)], y[k][:]))
+            nc.sync.dma_start(out=y_rows[:, :, x0 : x0 + n], in_=y[k][:])
+            nc.vector.tensor_copy(*interleaved_views(y_b[k][:], y[k][:]))
 
-        def quantize_y(x0, n):
+        def quantize_y(k):
+            x0, n = NODE_PIECES[k]
             nc.vector.quantize_mx(
-                out=y_codes[:, x0 : x0 + n].bitcast(E4M3),
-                scales=y_scales[:, x0 : x0 + n],
-                in_=y_b[:, PACK * x0 : PACK * (x0 + n)],
+                out=y_codes[:, x0 : x0 + n].bitcast(E4M3), scales=y_scales[:, x0 : x0 + n], in_=y_b[k][:]
             )
             nc.sync.dma_start(out=words_out[:, x0 : x0 + n], in_=y_codes[:, x0 : x0 + n].bitcast(I32))
 
-        gather_dm(0)
-        for s, (t, ks) in enumerate(GATHER_STEPS):
-            if s + 1 < len(GATHER_STEPS):
-                gather_dm(s + 1)
-            for k in ks:
+        for k in range(last + 1):
+            gather_dm(True, 0, k)
+            add_pairs(0, k)
+        for k in range(last + 1):
+            gather_dm(True, 2, k)
+            add_pairs(2, k)
+        for k in range(last + 1):
+            for t in (1, 3):
+                gather_dm(False, t, k)
                 add_pairs(t, k)
-            if t == PACK - 1:
-                round_y(ks[0])
-        for x0, n in [(0, 512), (512, 256), (768, 256)]:
-            quantize_y(x0, n)
+            finish(k)
+            if k > 0:
+                quantize_y(k - 1)
+        quantize_y(last)
         for q in range(4):
             queue = nc.scalar if q % 2 else nc.sync
             queue.dma_start(out=scales_out[4 * q : 4 * q + 4, :], in_=y_scales[32 * q : 32 * q + 4, :].bitcast(I32))

@@ -23,9 +23,18 @@ PACK = 4
 CHUNK = 512
 CHUNKS = E // CHUNK
 PER_COL = 16
-H_LOADS = [(0, 256), (256, 256), (512, 512), (1024, 512), (1536, 256), (1792, 256)]
-EDGE_PIECES = [(0, 256), (256, 256), (512, 512), (1024, 512), (1536, 256), (1792, 128), (1920, 128)]
-NODE_PIECES = [(0, 256), (256, 256), (512, 256), (768, 128), (896, 128)]
+H_LOADS = [(0, 256), (256, 256), (512, 256), (768, 512), (1280, 256), (1536, 256), (1792, 256)]
+W_BEFORE = 1280
+EDGE_PIECES = H_LOADS[:-1] + [(1792, 128), (1920, 128)]
+GATHER_GROUPS = [
+    (0, 512, 0, 0),
+    (512, 768, 1, 0),
+    (1280, 256, 0, 0),
+    (1536, 256, 0, 256),
+    (1792, 128, 1, 0),
+    (1920, 128, 1, 128),
+]
+NODE_PIECES = [(0, 384), (384, 256), (640, 128), (768, 128), (896, 128)]
 
 
 def interleaved_views(dst, src):
@@ -46,7 +55,7 @@ def tile_attend_gmp_pl_kernel(tc, dyT, hE, wm, offs, offs2, out_0, out_1, out_2)
 
     with ExitStack() as ctx:
         keep = ctx.enter_context(tc.tile_pool(name="keep", bufs=1))
-        psum = ctx.enter_context(tc.psum_pool(name="psum", bufs=8))
+        psum = ctx.enter_context(tc.psum_pool(name="psum", bufs=1))
 
         dst_list = keep.tile([P, E // PER_COL], U16, name="dst_list")
         src_list = keep.tile([P, E // PER_COL], U16, name="src_list")
@@ -55,131 +64,139 @@ def tile_attend_gmp_pl_kernel(tc, dyT, hE, wm, offs, offs2, out_0, out_1, out_2)
         w_raw = keep.tile([P, PACK, D], F32, name="w_raw")
         twos = keep.tile([P, CHUNK], F32, name="twos")
 
-        nc.gpsimd.memset(twos[:], 2.0)
+        ones = keep.tile([P, CHUNK], F32, name="ones")
+        nc.gpsimd.memset(ones[:], 1.0)
+        nc.scalar.activation(twos[:], ones[:], COPY, scale=2.0)
         nc.sync.dma_start(dst_list[:], offs)
         for t in range(PACK):
             nc.sync.dma_start(out=dy[t][:], in_=dy_rows[:, t, :])
         for k, (e0, n) in enumerate(H_LOADS):
-            if e0 == 3 * CHUNK:
+            if e0 == W_BEFORE:
                 nc.sync.dma_start(out=w_raw[:], in_=w_rows)
             nc.sync.dma_start(out=h[k][:], in_=h_rows[:, :, e0 : e0 + n])
         nc.sync.dma_start(src_list[:], offs2)
 
-        g = [keep.tile([P, PACK, CHUNK], F32, name="g%d" % c) for c in range(CHUNKS - 1)]
-        g.append(g[0])
-        dz_b = [keep.tile([P, n * PACK], BF16, name="dzb%d" % e0, align_bytes=64) for e0, n in EDGE_PIECES]
-        dz_codes = [keep.tile([P, CHUNK], U32, name="dzc%d" % c, align_bytes=64) for c in range(CHUNKS)]
-        dz_scales = [keep.tile([P, CHUNK], U8, name="dzs%d" % c, align_bytes=64) for c in range(CHUNKS)]
+        g = [keep.tile([P, PACK, n], F32, name="g%d" % n) for n in (512, 768)]
+        w_late = keep.tile([P, 2 * D], BF16, name="w_late", align_bytes=64)
+        dz_b = [keep.tile([P, n * PACK], BF16, name="dzb%d" % e0, align_bytes=64)[:] for e0, n in EDGE_PIECES[:-2]]
+        dz_b = dz_b + [w_late[:, 0:D], w_late[:, D : 2 * D]]
+        dz_codes = keep.tile([P, E], U32, name="dz_codes", align_bytes=64)
+        dz_scales = keep.tile([P, E], U8, name="dz_scales", align_bytes=64)
         dm = [keep.tile([P, E], F32, name="dm%d" % t) for t in range(PACK)]
-        w_b = [keep.tile([P, D], BF16, name="wb%d" % t, align_bytes=64) for t in range(PACK)]
+        w_early = keep.tile([P, 2 * D], BF16, name="w_early", align_bytes=64)
         w_codes = keep.tile([P, D], U32, name="w_codes", align_bytes=64)
         w_scales = keep.tile([P, D], U8, name="w_scales", align_bytes=64)
         w_dealt = w_raw[:].rearrange("p j (m t) -> p m j t", t=PACK)
 
-        def gather_dy(on_vector, t, e0, n):
-            c, r = divmod(e0, CHUNK)
-            picked = dy[t][:].indirect(dst_list[:, e0 // PER_COL : (e0 + n) // PER_COL])
-            if on_vector:
-                nc.vector.tensor_tensor(g[c][:, t, r : r + n], picked, twos[:, 0:n], MULT)
-            else:
-                nc.scalar.activation(g[c][:, t, r : r + n], picked, COPY, scale=2.0)
+        def gather_dy(group):
+            e0, n, buffer, r = GATHER_GROUPS[group]
+            for t in range(PACK):
+                picked = dy[t][:].indirect(dst_list[:, e0 // PER_COL : (e0 + n) // PER_COL])
+                if group == 0:
+                    nc.vector.tensor_tensor(g[buffer][:, t, r : r + n], picked, twos[:, 0:n], MULT)
+                else:
+                    nc.scalar.activation(g[buffer][:, t, r : r + n], picked, COPY, scale=2.0)
 
         def form_dz(k):
             e0, n = EDGE_PIECES[k]
-            c, r = divmod(e0, CHUNK)
             load = max(i for i, (l0, ln) in enumerate(H_LOADS) if l0 <= e0)
             a = e0 - H_LOADS[load][0]
+            g0, gn, buffer, r = max(group for group in GATHER_GROUPS if group[0] <= e0)
+            b = r + e0 - g0
             nc.vector.scalar_tensor_tensor(
-                out=dz_b[k][:].rearrange("p (e t) -> p e t", t=PACK),
+                out=dz_b[k].rearrange("p (e t) -> p e t", t=PACK),
                 in0=h[load][:, :, a : a + n].rearrange("p t e -> p e t"),
                 scalar=0.0,
-                in1=g[c][:, :, r : r + n].rearrange("p t e -> p e t"),
+                in1=g[buffer][:, :, b : b + n].rearrange("p t e -> p e t"),
                 op0=MAX,
                 op1=MULT,
             )
 
         def quantize_dz(k):
             e0, n = EDGE_PIECES[k]
-            c, r = divmod(e0, CHUNK)
             nc.vector.quantize_mx(
-                out=dz_codes[c][:, r : r + n].bitcast(E5M2), scales=dz_scales[c][:, r : r + n], in_=dz_b[k][:]
+                out=dz_codes[:, e0 : e0 + n].bitcast(E5M2), scales=dz_scales[:, e0 : e0 + n], in_=dz_b[k]
             )
 
-        def round_w(t):
-            nc.scalar.copy(w_b[t][:].rearrange("p (m j) -> p m j", j=PACK), w_dealt[:, :, :, t])
+        def round_w(t0, rounded):
+            nc.vector.tensor_copy(rounded.rearrange("p (t m j) -> p m j t", t=2, j=PACK), w_dealt[:, :, :, t0 : t0 + 2])
 
-        def quantize_w(t):
-            cols = slice(t * P, (t + 1) * P)
-            nc.vector.quantize_mx(out=w_codes[:, cols].bitcast(E4M3), scales=w_scales[:, cols], in_=w_b[t][:])
+        def quantize_w(t0, rounded):
+            cols = slice(t0 * P, (t0 + 2) * P)
+            nc.vector.quantize_mx(out=w_codes[:, cols].bitcast(E4M3), scales=w_scales[:, cols], in_=rounded)
 
-        def product(t, e0, n):
-            c, r = divmod(e0, CHUNK)
-            acc = psum.tile([P, CHUNK], F32, name="acc")
+        banks = [psum.tile([P, CHUNK], F32, name="bank%d" % b) for b in range(8)]
+
+        def product(t, e0, n, bank):
+            acc = banks[bank]
             nc.tensor.matmul_mx(
                 out=acc[:, 0:n],
                 lhsT=w_codes[:, t * P : (t + 1) * P].bitcast(E4M3),
                 lhsT_scale=w_scales[:, t * P : (t + 1) * P],
-                rhs=dz_codes[c][:, r : r + n].bitcast(E5M2),
-                rhs_scale=dz_scales[c][:, r : r + n],
+                rhs=dz_codes[:, e0 : e0 + n].bitcast(E5M2),
+                rhs_scale=dz_scales[:, e0 : e0 + n],
                 start=True,
                 stop=True,
             )
             nc.scalar.copy(dm[t][:, e0 : e0 + n], acc[:, 0:n])
 
-        for t in range(PACK):
-            gather_dy(True, t, 0, CHUNK)
-            for c in (1, 2):
-                gather_dy(False, t, c * CHUNK, CHUNK)
+        gather_dy(0)
+        gather_dy(1)
         form_dz(0)
-        for k in (1, 2, 3):
-            form_dz(k)
-            quantize_dz(k - 1)
-        for t in range(PACK):
-            gather_dy(False, t, 3 * CHUNK, CHUNK // 2)
-        round_w(0)
-        for t in range(PACK):
-            gather_dy(False, t, 3 * CHUNK + CHUNK // 2, CHUNK // 2)
-        form_dz(4)
+        form_dz(1)
+        quantize_dz(0)
+        gather_dy(2)
+        gather_dy(3)
+        form_dz(2)
+        quantize_dz(1)
+        gather_dy(4)
+        gather_dy(5)
+        form_dz(3)
+        quantize_dz(2)
+        round_w(0, w_early[:])
         quantize_dz(3)
-        quantize_w(0)
+        quantize_w(0, w_early[:])
+        form_dz(4)
+        form_dz(5)
+        quantize_dz(4)
         for c in range(CHUNKS - 1):
-            product(0, c * CHUNK, CHUNK)
-        for k in (5, 6):
+            product(0, c * CHUNK, CHUNK, c)
+        for k in (6, 7):
             form_dz(k)
             quantize_dz(k - 1)
-            product(0, *EDGE_PIECES[k - 1])
-        quantize_dz(6)
-        product(0, *EDGE_PIECES[6])
-        for t in range(1, PACK):
-            round_w(t)
-            quantize_w(t)
-        for t in (2, 1, 3):
+            product(0, *EDGE_PIECES[k - 1], k - 3)
+        quantize_dz(7)
+        product(0, *EDGE_PIECES[7], 5)
+        for c in range(CHUNKS):
+            product(1, c * CHUNK, CHUNK, 3 + c)
+        round_w(2, w_late[:])
+        quantize_w(2, w_late[:])
+        for t in (2, 3):
             for c in range(CHUNKS):
-                product(t, c * CHUNK, CHUNK)
+                product(t, c * CHUNK, CHUNK, (CHUNKS * t + c - 1) % 8)
 
-        picked = {(t, k): keep.tile([P, 2 * n], F32, name="pk%d_%d" % (t, x0)) for t in range(PACK) for k, (x0, n) in enumerate(NODE_PIECES)}
+        picked = [keep.tile([P, E], F32, name="picked%d" % t) for t in range(PACK)]
         y = [keep.tile([P, PACK, n], F32, name="y%d" % x0) for x0, n in NODE_PIECES]
         y_b = [keep.tile([P, n * PACK], BF16, name="yb%d" % x0, align_bytes=64) for x0, n in NODE_PIECES]
         y_codes = keep.tile([P, V], U32, name="y_codes", align_bytes=64)
         y_scales = keep.tile([P, V], U8, name="y_scales", align_bytes=64)
         last = len(NODE_PIECES) - 1
 
-        def gather_dm(on_vector, t, k):
-            x0, n = NODE_PIECES[k]
+        def gather_dm(on_vector, t, x0, n):
             window = dm[t][:].indirect(src_list[:, 2 * x0 // PER_COL : 2 * (x0 + n) // PER_COL])
             if on_vector:
-                nc.vector.tensor_copy(picked[t, k][:], window)
+                nc.vector.tensor_copy(picked[t][:, 2 * x0 : 2 * (x0 + n)], window)
             else:
-                nc.scalar.activation(picked[t, k][:], window, COPY)
+                nc.scalar.activation(picked[t][:, 2 * x0 : 2 * (x0 + n)], window, COPY)
 
-        def add_pairs(t, k):
-            both = picked[t, k][:].rearrange("p (x j) -> p j x", j=2)
-            engine = nc.vector if k == last and t % 2 == 1 else nc.gpsimd
-            engine.tensor_tensor(y[k][:, t, :], both[:, 0, :], both[:, 1, :], ADD)
-
-        def finish(k):
+        def add_pairs(engine, t, k):
             x0, n = NODE_PIECES[k]
-            nc.sync.dma_start(out=y_rows[:, :, x0 : x0 + n], in_=y[k][:])
+            both = picked[t][:, 2 * x0 : 2 * (x0 + n)].rearrange("p (x j) -> p j x", j=2)
+            engine.tensor_tensor(y[k][:, t, :], both[:, 0, :], both[:, 1, :], ADD)
+            if t % 2 == 1:
+                nc.sync.dma_start(out=y_rows[:, t - 1 : t + 1, x0 : x0 + n], in_=y[k][:, t - 1 : t + 1, :])
+
+        def round_y(k):
             nc.vector.tensor_copy(*interleaved_views(y_b[k][:], y[k][:]))
 
         def quantize_y(k):
@@ -189,17 +206,19 @@ def tile_attend_gmp_pl_kernel(tc, dyT, hE, wm, offs, offs2, out_0, out_1, out_2)
             )
             nc.sync.dma_start(out=words_out[:, x0 : x0 + n], in_=y_codes[:, x0 : x0 + n].bitcast(I32))
 
+        for t in range(2):
+            for x0, n in ((0, 384), (384, 640)):
+                gather_dm(True, t, x0, n)
+            for k in range(last + 1):
+                add_pairs(nc.gpsimd, t, k)
+        gather_dm(True, 2, *NODE_PIECES[last])
+        add_pairs(nc.gpsimd, 2, last)
         for k in range(last + 1):
-            gather_dm(True, 0, k)
-            add_pairs(0, k)
-        for k in range(last + 1):
-            gather_dm(True, 2, k)
-            add_pairs(2, k)
-        for k in range(last + 1):
-            for t in (1, 3):
-                gather_dm(False, t, k)
-                add_pairs(t, k)
-            finish(k)
+            for t in (2, 3):
+                if (t, k) != (2, last):
+                    gather_dm(False, t, *NODE_PIECES[k])
+                    add_pairs(nc.vector if t == 3 and k in (0, last) else nc.gpsimd, t, k)
+            round_y(k)
             if k > 0:
                 quantize_y(k - 1)
         quantize_y(last)

@@ -80,6 +80,7 @@ def tile_attend_gmp_pl_kernel(tc, dyT, hE, wm, offs, offs2, out_0, out_1, out_2)
         w_late = keep.tile([P, 2 * D], BF16, name="w_late", align_bytes=64)
         dz_b = [keep.tile([P, n * PACK], BF16, name="dzb%d" % e0, align_bytes=64)[:] for e0, n in EDGE_PIECES[:-2]]
         dz_b = dz_b + [w_late[:, 0:D], w_late[:, D : 2 * D]]
+        halves = [keep.tile([P, 2, n * 2], BF16, name="half%d" % e0) for e0, n in EDGE_PIECES]
         dz_codes = keep.tile([P, E], U32, name="dz_codes", align_bytes=64)
         dz_scales = keep.tile([P, E], U8, name="dz_scales", align_bytes=64)
         dm = [keep.tile([P, E], F32, name="dm%d" % t) for t in range(PACK)]
@@ -97,20 +98,34 @@ def tile_attend_gmp_pl_kernel(tc, dyT, hE, wm, offs, offs2, out_0, out_1, out_2)
                 else:
                     nc.scalar.activation(g[buffer][:, t, r : r + n], picked, COPY, scale=2.0)
 
-        def form_dz(k):
+        def form_dz(k, u):
             e0, n = EDGE_PIECES[k]
             load = max(i for i, (l0, ln) in enumerate(H_LOADS) if l0 <= e0)
             a = e0 - H_LOADS[load][0]
             g0, gn, buffer, r = max(group for group in GATHER_GROUPS if group[0] <= e0)
             b = r + e0 - g0
             nc.vector.scalar_tensor_tensor(
-                out=dz_b[k].rearrange("p (e t) -> p e t", t=PACK),
-                in0=h[load][:, :, a : a + n].rearrange("p t e -> p e t"),
+                out=halves[k][:, u, :].rearrange("p (e t) -> p e t", t=2),
+                in0=h[load][:, 2 * u : 2 * u + 2, a : a + n].rearrange("p t e -> p e t"),
                 scalar=0.0,
-                in1=g[buffer][:, :, b : b + n].rearrange("p t e -> p e t"),
+                in1=g[buffer][:, 2 * u : 2 * u + 2, b : b + n].rearrange("p t e -> p e t"),
                 op0=MAX,
                 op1=MULT,
             )
+
+        def weave_dz(k):
+            nc.vector.tensor_copy(
+                dz_b[k].bitcast(I32).rearrange("p (e u) -> p e u", u=2),
+                halves[k][:].bitcast(I32).rearrange("p u e -> p e u"),
+            )
+
+        def step(k):
+            form_dz(k, 0)
+            if k > 0:
+                weave_dz(k - 1)
+            form_dz(k, 1)
+            if k > 0:
+                quantize_dz(k - 1)
 
         def quantize_dz(k):
             e0, n = EDGE_PIECES[k]
@@ -142,29 +157,24 @@ def tile_attend_gmp_pl_kernel(tc, dyT, hE, wm, offs, offs2, out_0, out_1, out_2)
 
         gather_dy(0)
         gather_dy(1)
-        form_dz(0)
-        form_dz(1)
-        quantize_dz(0)
+        step(0)
+        step(1)
         gather_dy(2)
         gather_dy(3)
-        form_dz(2)
-        quantize_dz(1)
+        step(2)
         gather_dy(4)
         gather_dy(5)
-        form_dz(3)
-        quantize_dz(2)
+        step(3)
         round_w(0, w_early[:])
-        quantize_dz(3)
+        step(4)
         quantize_w(0, w_early[:])
-        form_dz(4)
-        form_dz(5)
-        quantize_dz(4)
+        step(5)
         for c in range(CHUNKS - 1):
             product(0, c * CHUNK, CHUNK, c)
         for k in (6, 7):
-            form_dz(k)
-            quantize_dz(k - 1)
+            step(k)
             product(0, *EDGE_PIECES[k - 1], k - 3)
+        weave_dz(7)
         quantize_dz(7)
         product(0, *EDGE_PIECES[7], 5)
         for c in range(CHUNKS):

@@ -23,18 +23,7 @@ PACK = 4
 CHUNK = 512
 CHUNKS = E // CHUNK
 PER_COL = 16
-H_LOADS = [(0, 256), (256, 256), (512, 256), (768, 512), (1280, 256), (1536, 256), (1792, 256)]
-W_BEFORE = 1280
-EDGE_PIECES = H_LOADS[:-1] + [(1792, 128), (1920, 128)]
-GATHER_GROUPS = [
-    (0, 512, 0, 0),
-    (512, 768, 1, 0),
-    (1280, 256, 0, 0),
-    (1536, 256, 0, 256),
-    (1792, 128, 1, 0),
-    (1920, 128, 1, 128),
-]
-NODE_PIECES = [(0, 384), (384, 256), (640, 128), (768, 128), (896, 128)]
+NODE_PIECES = [(0, 384), (384, 256), (640, 256), (896, 128)]
 
 
 def interleaved_views(dst, src):
@@ -60,7 +49,10 @@ def tile_attend_gmp_pl_kernel(tc, dyT, hE, wm, offs, offs2, out_0, out_1, out_2)
         dst_list = keep.tile([P, E // PER_COL], U16, name="dst_list")
         src_list = keep.tile([P, E // PER_COL], U16, name="src_list")
         dy = [keep.tile([P, V], F32, name="dy%d" % t) for t in range(PACK)]
-        h = [keep.tile([P, PACK, n], F32, name="h%d" % e0) for e0, n in H_LOADS]
+        h_first = [keep.tile([P, 2, 512], F32, name="h_first%d" % u) for u in range(2)]
+        h_second = [keep.tile([P, 2, 768], F32, name="h_second%d" % u) for u in range(2)]
+        h_third = keep.tile([P, PACK, 512], F32, name="h_third")
+        h_last = keep.tile([P, PACK, 256], F32, name="h_last")
         w_raw = keep.tile([P, PACK, D], F32, name="w_raw")
         twos = keep.tile([P, CHUNK], F32, name="twos")
 
@@ -70,17 +62,21 @@ def tile_attend_gmp_pl_kernel(tc, dyT, hE, wm, offs, offs2, out_0, out_1, out_2)
         nc.sync.dma_start(dst_list[:], offs)
         for t in range(PACK):
             nc.sync.dma_start(out=dy[t][:], in_=dy_rows[:, t, :])
-        for k, (e0, n) in enumerate(H_LOADS):
-            if e0 == W_BEFORE:
-                nc.sync.dma_start(out=w_raw[:], in_=w_rows)
-            nc.sync.dma_start(out=h[k][:], in_=h_rows[:, :, e0 : e0 + n])
+        for u in range(2):
+            nc.sync.dma_start(out=h_first[u][:], in_=h_rows[:, 2 * u : 2 * u + 2, 0:512])
+        for u in range(2):
+            nc.sync.dma_start(out=h_second[u][:], in_=h_rows[:, 2 * u : 2 * u + 2, 512:1280])
+        nc.sync.dma_start(out=w_raw[:], in_=w_rows)
+        nc.sync.dma_start(out=h_third[:], in_=h_rows[:, :, 1280:1792])
+        nc.sync.dma_start(out=h_last[:], in_=h_rows[:, :, 1792:2048])
         nc.sync.dma_start(src_list[:], offs2)
 
-        g = [keep.tile([P, PACK, n], F32, name="g%d" % n) for n in (512, 768)]
+        g_first = [keep.tile([P, 2 * 512], F32, name="g_first%d" % u) for u in range(2)]
+        g_second = [keep.tile([P, 2 * 768], F32, name="g_second%d" % u) for u in range(2)]
         w_late = keep.tile([P, 2 * D], BF16, name="w_late", align_bytes=64)
-        dz_b = [keep.tile([P, n * PACK], BF16, name="dzb%d" % e0, align_bytes=64)[:] for e0, n in EDGE_PIECES[:-2]]
-        dz_b = dz_b + [w_late[:, 0:D], w_late[:, D : 2 * D]]
-        halves = [keep.tile([P, 2, n * 2], BF16, name="half%d" % e0) for e0, n in EDGE_PIECES]
+        woven = [(0, 512), (512, 768), (1280, 256), (1536, 256)]
+        halves = {e0: keep.tile([P, 2, 2 * n], BF16, name="halves%d" % e0) for e0, n in woven}
+        dz_b = {e0: keep.tile([P, PACK * n], BF16, name="dz_b%d" % e0, align_bytes=64) for e0, n in woven}
         dz_codes = keep.tile([P, E], U32, name="dz_codes", align_bytes=64)
         dz_scales = keep.tile([P, E], U8, name="dz_scales", align_bytes=64)
         dm = [keep.tile([P, E], F32, name="dm%d" % t) for t in range(PACK)]
@@ -89,48 +85,38 @@ def tile_attend_gmp_pl_kernel(tc, dyT, hE, wm, offs, offs2, out_0, out_1, out_2)
         w_scales = keep.tile([P, D], U8, name="w_scales", align_bytes=64)
         w_dealt = w_raw[:].rearrange("p j (m t) -> p m j t", t=PACK)
 
-        def gather_dy(group):
-            e0, n, buffer, r = GATHER_GROUPS[group]
-            for t in range(PACK):
-                picked = dy[t][:].indirect(dst_list[:, e0 // PER_COL : (e0 + n) // PER_COL])
-                if group == 0:
-                    nc.vector.tensor_tensor(g[buffer][:, t, r : r + n], picked, twos[:, 0:n], MULT)
-                else:
-                    nc.scalar.activation(g[buffer][:, t, r : r + n], picked, COPY, scale=2.0)
+        def planes(buffer, count, n):
+            return buffer[:, 0 : count * n].rearrange("p (t e) -> p t e", t=count)
 
-        def form_dz(k, u):
-            e0, n = EDGE_PIECES[k]
-            load = max(i for i, (l0, ln) in enumerate(H_LOADS) if l0 <= e0)
-            a = e0 - H_LOADS[load][0]
-            g0, gn, buffer, r = max(group for group in GATHER_GROUPS if group[0] <= e0)
-            b = r + e0 - g0
+        def gather_dy(on_vector, t, e0, n, into):
+            picked = dy[t][:].indirect(dst_list[:, e0 // PER_COL : (e0 + n) // PER_COL])
+            if on_vector:
+                nc.vector.tensor_tensor(into, picked, twos[:, 0:n], MULT)
+            else:
+                nc.scalar.activation(into, picked, COPY, scale=2.0)
+
+        def form_dz(into, h_planes, g_planes):
             nc.vector.scalar_tensor_tensor(
-                out=halves[k][:, u, :].rearrange("p (e t) -> p e t", t=2),
-                in0=h[load][:, 2 * u : 2 * u + 2, a : a + n].rearrange("p t e -> p e t"),
+                out=into.rearrange("p (e t) -> p e t", t=h_planes.shape[1]),
+                in0=h_planes.rearrange("p t e -> p e t"),
                 scalar=0.0,
-                in1=g[buffer][:, 2 * u : 2 * u + 2, b : b + n].rearrange("p t e -> p e t"),
+                in1=g_planes.rearrange("p t e -> p e t"),
                 op0=MAX,
                 op1=MULT,
             )
 
-        def weave_dz(k):
+        def form_half(u, e0, h_planes, g_planes):
+            form_dz(halves[e0][:, u, :], h_planes, g_planes)
+
+        def weave_dz(e0):
             nc.vector.tensor_copy(
-                dz_b[k].bitcast(I32).rearrange("p (e u) -> p e u", u=2),
-                halves[k][:].bitcast(I32).rearrange("p u e -> p e u"),
+                dz_b[e0][:].bitcast(I32).rearrange("p (e u) -> p e u", u=2),
+                halves[e0][:].bitcast(I32).rearrange("p u e -> p e u"),
             )
 
-        def step(k):
-            form_dz(k, 0)
-            if k > 0:
-                weave_dz(k - 1)
-            form_dz(k, 1)
-            if k > 0:
-                quantize_dz(k - 1)
-
-        def quantize_dz(k):
-            e0, n = EDGE_PIECES[k]
+        def quantize_dz(e0, n, rounded):
             nc.vector.quantize_mx(
-                out=dz_codes[:, e0 : e0 + n].bitcast(E5M2), scales=dz_scales[:, e0 : e0 + n], in_=dz_b[k]
+                out=dz_codes[:, e0 : e0 + n].bitcast(E5M2), scales=dz_scales[:, e0 : e0 + n], in_=rounded
             )
 
         def round_w(t0, rounded):
@@ -153,37 +139,64 @@ def tile_attend_gmp_pl_kernel(tc, dyT, hE, wm, offs, offs2, out_0, out_1, out_2)
                 start=True,
                 stop=True,
             )
-            nc.scalar.copy(dm[t][:, e0 : e0 + n], acc[:, 0:n])
 
-        gather_dy(0)
-        gather_dy(1)
-        step(0)
-        step(1)
-        gather_dy(2)
-        gather_dy(3)
-        step(2)
-        gather_dy(4)
-        gather_dy(5)
-        step(3)
+        def empty(t, e0, n, bank):
+            nc.scalar.copy(dm[t][:, e0 : e0 + n], banks[bank][:, 0:n])
+
+        def product_out(t, e0, n, bank):
+            product(t, e0, n, bank)
+            empty(t, e0, n, bank)
+
+        first = [planes(g_first[u], 2, 512) for u in range(2)]
+        second = [planes(g_second[u], 2, 768) for u in range(2)]
+        for t in range(PACK):
+            gather_dy(True, t, 0, 512, first[t // 2][:, t % 2, :])
+            gather_dy(False, t, 512, 768, second[t // 2][:, t % 2, :])
+        form_half(0, 0, h_first[0][:], first[0])
+        form_half(1, 0, h_first[1][:], first[1])
+        form_half(0, 512, h_second[0][:], second[0])
+        weave_dz(0)
+        form_half(1, 512, h_second[1][:], second[1])
+        quantize_dz(0, 512, dz_b[0][:])
+        later = [planes(buffer, PACK, 256) for buffer in (g_first[1], g_second[0], g_second[1])]
+        for i in range(2):
+            for t in range(PACK):
+                gather_dy(False, t, 1280 + 256 * i, 256, later[i][:, t, :])
+        for i in range(2):
+            for t in range(PACK):
+                gather_dy(False, t, 1792 + 128 * i, 128, later[2][:, t, 128 * i : 128 * (i + 1)])
+        weave_dz(512)
         round_w(0, w_early[:])
-        step(4)
+        quantize_dz(512, 256, dz_b[512][:, 0 : PACK * 256])
+        quantize_dz(768, 512, dz_b[512][:, PACK * 256 : PACK * 768])
         quantize_w(0, w_early[:])
-        step(5)
-        for c in range(CHUNKS - 1):
-            product(0, c * CHUNK, CHUNK, c)
-        for k in (6, 7):
-            step(k)
-            product(0, *EDGE_PIECES[k - 1], k - 3)
-        weave_dz(7)
-        quantize_dz(7)
-        product(0, *EDGE_PIECES[7], 5)
-        for c in range(CHUNKS):
-            product(1, c * CHUNK, CHUNK, 3 + c)
+        for t in range(2):
+            for c in range(2):
+                product_out(t, c * CHUNK, CHUNK, 2 * t + c)
+        for u in range(2):
+            form_half(u, 1280, h_third[:, 2 * u : 2 * u + 2, 0:256], later[0][:, 2 * u : 2 * u + 2, :])
+        form_half(0, 1536, h_third[:, 0:2, 256:512], later[1][:, 0:2, :])
+        weave_dz(1280)
+        form_half(1, 1536, h_third[:, 2:4, 256:512], later[1][:, 2:4, :])
+        quantize_dz(1280, 256, dz_b[1280][:])
+        for t in range(2):
+            product_out(t, 2 * CHUNK, CHUNK, 4 + t)
+        weave_dz(1536)
+        form_dz(w_late[:, 0:D], h_last[:, :, 0:128], later[2][:, :, 0:128])
+        quantize_dz(1536, 256, dz_b[1536][:])
+        product_out(0, 1536, 256, 6)
+        form_dz(w_late[:, D : 2 * D], h_last[:, :, 128:256], later[2][:, :, 128:256])
+        quantize_dz(1792, 128, w_late[:, 0:D])
+        product_out(0, 1792, 128, 7)
+        quantize_dz(1920, 128, w_late[:, D : 2 * D])
+        product_out(0, 1920, 128, 0)
+        product_out(1, 3 * CHUNK, CHUNK, 1)
         round_w(2, w_late[:])
         quantize_w(2, w_late[:])
-        for t in (2, 3):
-            for c in range(CHUNKS):
-                product(t, c * CHUNK, CHUNK, (CHUNKS * t + c - 1) % 8)
+        for c in range(CHUNKS):
+            product_out(2, c * CHUNK, CHUNK, 2 + c)
+        for c in range(CHUNKS):
+            product(3, c * CHUNK, CHUNK, (6 + c) % 8)
 
         picked = [keep.tile([P, E], F32, name="picked%d" % t) for t in range(PACK)]
         y = [keep.tile([P, PACK, n], F32, name="y%d" % x0) for x0, n in NODE_PIECES]
@@ -203,8 +216,10 @@ def tile_attend_gmp_pl_kernel(tc, dyT, hE, wm, offs, offs2, out_0, out_1, out_2)
             x0, n = NODE_PIECES[k]
             both = picked[t][:, 2 * x0 : 2 * (x0 + n)].rearrange("p (x j) -> p j x", j=2)
             engine.tensor_tensor(y[k][:, t, :], both[:, 0, :], both[:, 1, :], ADD)
-            if t % 2 == 1:
-                nc.sync.dma_start(out=y_rows[:, t - 1 : t + 1, x0 : x0 + n], in_=y[k][:, t - 1 : t + 1, :])
+
+        def store_y(t0, t1, k):
+            x0, n = NODE_PIECES[k]
+            nc.sync.dma_start(out=y_rows[:, t0:t1, x0 : x0 + n], in_=y[k][:, t0:t1, :])
 
         def round_y(k):
             nc.vector.tensor_copy(*interleaved_views(y_b[k][:], y[k][:]))
@@ -216,21 +231,33 @@ def tile_attend_gmp_pl_kernel(tc, dyT, hE, wm, offs, offs2, out_0, out_1, out_2)
             )
             nc.sync.dma_start(out=words_out[:, x0 : x0 + n], in_=y_codes[:, x0 : x0 + n].bitcast(I32))
 
-        for t in range(2):
-            for x0, n in ((0, 384), (384, 640)):
-                gather_dm(True, t, x0, n)
-            for k in range(last + 1):
-                add_pairs(nc.gpsimd, t, k)
-        gather_dm(True, 2, *NODE_PIECES[last])
-        add_pairs(nc.gpsimd, 2, last)
+        for x0, n in ((0, 384), (384, 640)):
+            gather_dm(True, 0, x0, n)
         for k in range(last + 1):
-            for t in (2, 3):
-                if (t, k) != (2, last):
-                    gather_dm(False, t, *NODE_PIECES[k])
-                    add_pairs(nc.vector if t == 3 and k in (0, last) else nc.gpsimd, t, k)
-            round_y(k)
+            add_pairs(nc.gpsimd, 0, k)
+            store_y(0, 1, k)
+        for k in range(last):
+            gather_dm(False, 1, *NODE_PIECES[k])
+            add_pairs(nc.gpsimd, 1, k)
+            gather_dm(True, 2, *NODE_PIECES[k])
+            add_pairs(nc.gpsimd, 2, k)
+            store_y(1, 3, k)
+        for c in range(CHUNKS):
+            empty(3, c * CHUNK, CHUNK, (6 + c) % 8)
+        for t in (2, 1):
+            gather_dm(t == 2, t, *NODE_PIECES[last])
+            add_pairs(nc.gpsimd, t, last)
+        store_y(1, 3, last)
+        gather_dm(True, 3, 0, 256)
+        gather_dm(False, 3, 256, 128)
+        for k in range(last + 1):
+            if k > 0:
+                gather_dm(False, 3, *NODE_PIECES[k])
+            add_pairs(nc.vector, 3, k)
+            store_y(3, 4, k)
             if k > 0:
                 quantize_y(k - 1)
+            round_y(k)
         quantize_y(last)
         for q in range(4):
             queue = nc.scalar if q % 2 else nc.sync

@@ -81,8 +81,8 @@ def tile_attend_gmp_pl_kernel(tc, dyT, hE, wm, offs, offs2, out_0, out_1, out_2)
         dz_scales = keep.tile([P, E], U8, name="dz_scales", align_bytes=64)
         dm = [keep.tile([P, E], F32, name="dm%d" % t) for t in range(PACK)]
         w_early = keep.tile([P, 2 * D], BF16, name="w_early", align_bytes=64)
-        w_codes = keep.tile([P, D], U32, name="w_codes", align_bytes=64)
-        w_scales = keep.tile([P, D], U8, name="w_scales", align_bytes=64)
+        w_codes = [keep.tile([P, 2 * P], U32, name="w_codes%d" % u, align_bytes=64) for u in range(2)]
+        w_scales = [keep.tile([P, 2 * P], U8, name="w_scales%d" % u, align_bytes=64) for u in range(2)]
         w_dealt = w_raw[:].rearrange("p j (m t) -> p m j t", t=PACK)
 
         def planes(buffer, count, n):
@@ -123,8 +123,7 @@ def tile_attend_gmp_pl_kernel(tc, dyT, hE, wm, offs, offs2, out_0, out_1, out_2)
             nc.vector.tensor_copy(rounded.rearrange("p (t m j) -> p m j t", t=2, j=PACK), w_dealt[:, :, :, t0 : t0 + 2])
 
         def quantize_w(t0, rounded):
-            cols = slice(t0 * P, (t0 + 2) * P)
-            nc.vector.quantize_mx(out=w_codes[:, cols].bitcast(E4M3), scales=w_scales[:, cols], in_=rounded)
+            nc.vector.quantize_mx(out=w_codes[t0 // 2][:].bitcast(E4M3), scales=w_scales[t0 // 2][:], in_=rounded)
 
         banks = [psum.tile([P, CHUNK], F32, name="bank%d" % b) for b in range(8)]
 
@@ -132,8 +131,8 @@ def tile_attend_gmp_pl_kernel(tc, dyT, hE, wm, offs, offs2, out_0, out_1, out_2)
             acc = banks[bank]
             nc.tensor.matmul_mx(
                 out=acc[:, 0:n],
-                lhsT=w_codes[:, t * P : (t + 1) * P].bitcast(E4M3),
-                lhsT_scale=w_scales[:, t * P : (t + 1) * P],
+                lhsT=w_codes[t // 2][:, t % 2 * P : (t % 2 + 1) * P].bitcast(E4M3),
+                lhsT_scale=w_scales[t // 2][:, t % 2 * P : (t % 2 + 1) * P],
                 rhs=dz_codes[:, e0 : e0 + n].bitcast(E5M2),
                 rhs_scale=dz_scales[:, e0 : e0 + n],
                 start=True,
@@ -154,10 +153,10 @@ def tile_attend_gmp_pl_kernel(tc, dyT, hE, wm, offs, offs2, out_0, out_1, out_2)
             gather_dy(False, t, 512, 768, second[t // 2][:, t % 2, :])
         form_half(0, 0, h_first[0][:], first[0])
         form_half(1, 0, h_first[1][:], first[1])
-        form_half(0, 512, h_second[0][:], second[0])
         weave_dz(0)
-        form_half(1, 512, h_second[1][:], second[1])
+        form_half(0, 512, h_second[0][:], second[0])
         quantize_dz(0, 512, dz_b[0][:])
+        form_half(1, 512, h_second[1][:], second[1])
         later = [planes(buffer, PACK, 256) for buffer in (g_first[1], g_second[0], g_second[1])]
         for i in range(2):
             for t in range(PACK):
@@ -191,31 +190,51 @@ def tile_attend_gmp_pl_kernel(tc, dyT, hE, wm, offs, offs2, out_0, out_1, out_2)
         quantize_dz(1920, 128, w_late[:, D : 2 * D])
         product_out(0, 1920, 128, 0)
         product_out(1, 3 * CHUNK, CHUNK, 1)
-        round_w(2, w_late[:])
-        quantize_w(2, w_late[:])
+        for t in (2, 3):
+            nc.vector.tensor_copy(
+                w_late[:, (t - 2) * D : (t - 1) * D].rearrange("p (m j) -> p m j", j=PACK), w_dealt[:, :, :, t]
+            )
+        for t in (2, 3):
+            cols = slice((t - 2) * P, (t - 1) * P)
+            nc.vector.quantize_mx(
+                out=w_codes[1][:, cols].bitcast(E4M3),
+                scales=w_scales[1][:, cols],
+                in_=w_late[:, (t - 2) * D : (t - 1) * D],
+            )
         for c in range(CHUNKS):
             product_out(2, c * CHUNK, CHUNK, 2 + c)
         for c in range(CHUNKS):
-            product(3, c * CHUNK, CHUNK, (6 + c) % 8)
+            product_out(3, c * CHUNK, CHUNK, (6 + c) % 8)
 
-        picked = [keep.tile([P, E], F32, name="picked%d" % t) for t in range(PACK)]
+        picked = [keep.tile([P, E], F32, name="picked%d" % t) for t in range(2)]
+        picked_late = [keep.tile([P, 2, 2 * n], F32, name="late%d" % x0) for x0, n in NODE_PIECES]
         y = [keep.tile([P, PACK, n], F32, name="y%d" % x0) for x0, n in NODE_PIECES]
         y_b = [keep.tile([P, n * PACK], BF16, name="yb%d" % x0, align_bytes=64) for x0, n in NODE_PIECES]
         y_codes = keep.tile([P, V], U32, name="y_codes", align_bytes=64)
         y_scales = keep.tile([P, V], U8, name="y_scales", align_bytes=64)
         last = len(NODE_PIECES) - 1
 
-        def gather_dm(on_vector, t, x0, n):
+        def gather_dm(on_vector, t, x0, n, into):
             window = dm[t][:].indirect(src_list[:, 2 * x0 // PER_COL : 2 * (x0 + n) // PER_COL])
             if on_vector:
-                nc.vector.tensor_copy(picked[t][:, 2 * x0 : 2 * (x0 + n)], window)
+                nc.vector.tensor_copy(into, window)
             else:
-                nc.scalar.activation(picked[t][:, 2 * x0 : 2 * (x0 + n)], window, COPY)
+                nc.scalar.activation(into, window, COPY)
 
-        def add_pairs(engine, t, k):
+        def gather_early(t, x0, n):
+            gather_dm(True, t, x0, n, picked[t][:, 2 * x0 : 2 * (x0 + n)])
+
+        def gather_late(t, k):
+            gather_dm(False, t, *NODE_PIECES[k], picked_late[k][:, t - 2, :])
+
+        def add_early(t, k):
             x0, n = NODE_PIECES[k]
             both = picked[t][:, 2 * x0 : 2 * (x0 + n)].rearrange("p (x j) -> p j x", j=2)
-            engine.tensor_tensor(y[k][:, t, :], both[:, 0, :], both[:, 1, :], ADD)
+            nc.gpsimd.tensor_tensor(y[k][:, t, :], both[:, 0, :], both[:, 1, :], ADD)
+
+        def add_late(k):
+            both = picked_late[k][:].rearrange("p t (x j) -> p j t x", j=2)
+            nc.vector.tensor_tensor(y[k][:, 2:4, :], both[:, 0, :, :], both[:, 1, :, :], ADD)
 
         def store_y(t0, t1, k):
             x0, n = NODE_PIECES[k]
@@ -232,29 +251,19 @@ def tile_attend_gmp_pl_kernel(tc, dyT, hE, wm, offs, offs2, out_0, out_1, out_2)
             nc.sync.dma_start(out=words_out[:, x0 : x0 + n], in_=y_codes[:, x0 : x0 + n].bitcast(I32))
 
         for x0, n in ((0, 384), (384, 640)):
-            gather_dm(True, 0, x0, n)
+            gather_early(0, x0, n)
         for k in range(last + 1):
-            add_pairs(nc.gpsimd, 0, k)
-            store_y(0, 1, k)
-        for k in range(last):
-            gather_dm(False, 1, *NODE_PIECES[k])
-            add_pairs(nc.gpsimd, 1, k)
-            gather_dm(True, 2, *NODE_PIECES[k])
-            add_pairs(nc.gpsimd, 2, k)
-            store_y(1, 3, k)
-        for c in range(CHUNKS):
-            empty(3, c * CHUNK, CHUNK, (6 + c) % 8)
-        for t in (2, 1):
-            gather_dm(t == 2, t, *NODE_PIECES[last])
-            add_pairs(nc.gpsimd, t, last)
-        store_y(1, 3, last)
-        gather_dm(True, 3, 0, 256)
-        gather_dm(False, 3, 256, 128)
+            add_early(0, k)
+        for x0, n in ((0, 384), (384, 256), (640, 256), (896, 128)):
+            gather_early(1, x0, n)
         for k in range(last + 1):
-            if k > 0:
-                gather_dm(False, 3, *NODE_PIECES[k])
-            add_pairs(nc.vector, 3, k)
-            store_y(3, 4, k)
+            add_early(1, k)
+            store_y(0, 2, k)
+        for k in range(last + 1):
+            for t in (2, 3):
+                gather_late(t, k)
+            add_late(k)
+            store_y(2, 4, k)
             if k > 0:
                 quantize_y(k - 1)
             round_y(k)

@@ -73,10 +73,10 @@ def tile_attend_gmp_pl_kernel(tc, dyT, hE, wm, offs, offs2, out_0, out_1, out_2)
 
         g_first = [keep.tile([P, 2 * 512], F32, name="g_first%d" % u) for u in range(2)]
         g_second = [keep.tile([P, 2 * 768], F32, name="g_second%d" % u) for u in range(2)]
-        w_late = keep.tile([P, 2 * D], BF16, name="w_late", align_bytes=64)
-        woven = [(0, 512), (512, 768), (1280, 256), (1536, 256)]
+        woven = [(0, 512), (512, 768), (1280, 256), (1536, 256), (1792, 256)]
         halves = {e0: keep.tile([P, 2, 2 * n], BF16, name="halves%d" % e0) for e0, n in woven}
         dz_b = {e0: keep.tile([P, PACK * n], BF16, name="dz_b%d" % e0, align_bytes=64) for e0, n in woven}
+        w_late = dz_b[1792]
         dz_codes = keep.tile([P, E], U32, name="dz_codes", align_bytes=64)
         dz_scales = keep.tile([P, E], U8, name="dz_scales", align_bytes=64)
         dm = [keep.tile([P, E], F32, name="dm%d" % t) for t in range(PACK)]
@@ -108,10 +108,10 @@ def tile_attend_gmp_pl_kernel(tc, dyT, hE, wm, offs, offs2, out_0, out_1, out_2)
         def form_half(u, e0, h_planes, g_planes):
             form_dz(halves[e0][:, u, :], h_planes, g_planes)
 
-        def weave_dz(e0):
+        def weave_dz(e0, a, n):
             nc.vector.tensor_copy(
-                dz_b[e0][:].bitcast(I32).rearrange("p (e u) -> p e u", u=2),
-                halves[e0][:].bitcast(I32).rearrange("p u e -> p e u"),
+                dz_b[e0][:].bitcast(I32).rearrange("p (e u) -> p e u", u=2)[:, a : a + n, :],
+                halves[e0][:].bitcast(I32).rearrange("p u e -> p e u")[:, a : a + n, :],
             )
 
         def quantize_dz(e0, n, rounded):
@@ -152,19 +152,19 @@ def tile_attend_gmp_pl_kernel(tc, dyT, hE, wm, offs, offs2, out_0, out_1, out_2)
             gather_dy(True, t, 0, 512, first[t // 2][:, t % 2, :])
             gather_dy(False, t, 512, 768, second[t // 2][:, t % 2, :])
         form_half(0, 0, h_first[0][:], first[0])
-        form_half(1, 0, h_first[1][:], first[1])
-        weave_dz(0)
+        for a in (0, 256):
+            form_dz(halves[0][:, 1, 2 * a : 2 * (a + 256)], h_first[1][:, :, a : a + 256], first[1][:, :, a : a + 256])
+        for a in (0, 256):
+            weave_dz(0, a, 256)
+        for a in (0, 256):
+            quantize_dz(a, 256, dz_b[0][:, PACK * a : PACK * (a + 256)])
         form_half(0, 512, h_second[0][:], second[0])
-        quantize_dz(0, 512, dz_b[0][:])
         form_half(1, 512, h_second[1][:], second[1])
         later = [planes(buffer, PACK, 256) for buffer in (g_first[1], g_second[0], g_second[1])]
-        for i in range(2):
+        for i in range(3):
             for t in range(PACK):
                 gather_dy(False, t, 1280 + 256 * i, 256, later[i][:, t, :])
-        for i in range(2):
-            for t in range(PACK):
-                gather_dy(False, t, 1792 + 128 * i, 128, later[2][:, t, 128 * i : 128 * (i + 1)])
-        weave_dz(512)
+        weave_dz(512, 0, 768)
         round_w(0, w_early[:])
         quantize_dz(512, 256, dz_b[512][:, 0 : PACK * 256])
         quantize_dz(768, 512, dz_b[512][:, PACK * 256 : PACK * 768])
@@ -175,21 +175,20 @@ def tile_attend_gmp_pl_kernel(tc, dyT, hE, wm, offs, offs2, out_0, out_1, out_2)
         for u in range(2):
             form_half(u, 1280, h_third[:, 2 * u : 2 * u + 2, 0:256], later[0][:, 2 * u : 2 * u + 2, :])
         form_half(0, 1536, h_third[:, 0:2, 256:512], later[1][:, 0:2, :])
-        weave_dz(1280)
+        weave_dz(1280, 0, 256)
         form_half(1, 1536, h_third[:, 2:4, 256:512], later[1][:, 2:4, :])
         quantize_dz(1280, 256, dz_b[1280][:])
         for t in range(2):
             product_out(t, 2 * CHUNK, CHUNK, 4 + t)
-        weave_dz(1536)
-        form_dz(w_late[:, 0:D], h_last[:, :, 0:128], later[2][:, :, 0:128])
+        form_half(0, 1792, h_last[:, 0:2, :], later[2][:, 0:2, :])
+        weave_dz(1536, 0, 256)
+        form_half(1, 1792, h_last[:, 2:4, :], later[2][:, 2:4, :])
         quantize_dz(1536, 256, dz_b[1536][:])
         product_out(0, 1536, 256, 6)
-        form_dz(w_late[:, D : 2 * D], h_last[:, :, 128:256], later[2][:, :, 128:256])
-        quantize_dz(1792, 128, w_late[:, 0:D])
-        product_out(0, 1792, 128, 7)
-        quantize_dz(1920, 128, w_late[:, D : 2 * D])
-        product_out(0, 1920, 128, 0)
-        product_out(1, 3 * CHUNK, CHUNK, 1)
+        weave_dz(1792, 0, 256)
+        quantize_dz(1792, 256, dz_b[1792][:])
+        product_out(0, 1792, 256, 7)
+        product_out(1, 3 * CHUNK, CHUNK, 0)
         for t in (2, 3):
             nc.vector.tensor_copy(
                 w_late[:, (t - 2) * D : (t - 1) * D].rearrange("p (m j) -> p m j", j=PACK), w_dealt[:, :, :, t]
@@ -202,9 +201,9 @@ def tile_attend_gmp_pl_kernel(tc, dyT, hE, wm, offs, offs2, out_0, out_1, out_2)
                 in_=w_late[:, (t - 2) * D : (t - 1) * D],
             )
         for c in range(CHUNKS):
-            product_out(2, c * CHUNK, CHUNK, 2 + c)
+            product_out(2, c * CHUNK, CHUNK, 1 + c)
         for c in range(CHUNKS):
-            product_out(3, c * CHUNK, CHUNK, (6 + c) % 8)
+            product_out(3, c * CHUNK, CHUNK, (5 + c) % 8)
 
         picked = [keep.tile([P, E], F32, name="picked%d" % t) for t in range(2)]
         picked_late = [keep.tile([P, 2, 2 * n], F32, name="late%d" % x0) for x0, n in NODE_PIECES]

@@ -23,7 +23,8 @@ PACK = 4
 CHUNK = 512
 CHUNKS = E // CHUNK
 PER_COL = 16
-NODE_PIECES = [(0, 384), (384, 256), (640, 256), (896, 128)]
+NODE_GROUPS = [(0, 384), (384, 256), (640, 192), (832, 192)]
+NODE_STEPS = [(0, 0, 384), (1, 0, 256), (2, 0, 192), (3, 0, 128), (3, 128, 64)]
 
 
 def interleaved_views(dst, src):
@@ -50,9 +51,8 @@ def tile_attend_gmp_pl_kernel(tc, dyT, hE, wm, offs, offs2, out_0, out_1, out_2)
         src_list = keep.tile([P, E // PER_COL], U16, name="src_list")
         dy = [keep.tile([P, V], F32, name="dy%d" % t) for t in range(PACK)]
         h_first = [keep.tile([P, 2, 512], F32, name="h_first%d" % u) for u in range(2)]
-        h_second = [keep.tile([P, 2, 768], F32, name="h_second%d" % u) for u in range(2)]
-        h_third = keep.tile([P, PACK, 512], F32, name="h_third")
-        h_last = keep.tile([P, PACK, 256], F32, name="h_last")
+        h_second = [keep.tile([P, 2, 1024], F32, name="h_second%d" % u) for u in range(2)]
+        h_last = keep.tile([P, PACK, 512], F32, name="h_last")
         w_raw = keep.tile([P, PACK, D], F32, name="w_raw")
         twos = keep.tile([P, CHUNK], F32, name="twos")
 
@@ -65,10 +65,9 @@ def tile_attend_gmp_pl_kernel(tc, dyT, hE, wm, offs, offs2, out_0, out_1, out_2)
         for u in range(2):
             nc.sync.dma_start(out=h_first[u][:], in_=h_rows[:, 2 * u : 2 * u + 2, 0:512])
         for u in range(2):
-            nc.sync.dma_start(out=h_second[u][:], in_=h_rows[:, 2 * u : 2 * u + 2, 512:1280])
+            nc.sync.dma_start(out=h_second[u][:], in_=h_rows[:, 2 * u : 2 * u + 2, 512:1536])
         nc.sync.dma_start(out=w_raw[:], in_=w_rows)
-        nc.sync.dma_start(out=h_third[:], in_=h_rows[:, :, 1280:1792])
-        nc.sync.dma_start(out=h_last[:], in_=h_rows[:, :, 1792:2048])
+        nc.sync.dma_start(out=h_last[:], in_=h_rows[:, :, 1536:2048])
         nc.sync.dma_start(src_list[:], offs2)
 
         g_first = [keep.tile([P, 2 * 512], F32, name="g_first%d" % u) for u in range(2)]
@@ -158,31 +157,30 @@ def tile_attend_gmp_pl_kernel(tc, dyT, hE, wm, offs, offs2, out_0, out_1, out_2)
             weave_dz(0, a, 256)
         for a in (0, 256):
             quantize_dz(a, 256, dz_b[0][:, PACK * a : PACK * (a + 256)])
-        form_half(0, 512, h_second[0][:], second[0])
-        form_half(1, 512, h_second[1][:], second[1])
         later = [planes(buffer, PACK, 256) for buffer in (g_first[1], g_second[0], g_second[1])]
-        for i in range(3):
+        for t in range(PACK):
+            gather_dy(False, t, 1280, 256, later[0][:, t, :])
+        for u in range(2):
+            form_half(u, 512, h_second[u][:, :, 0:768], second[u])
+            form_half(u, 1280, h_second[u][:, :, 768:1024], later[0][:, 2 * u : 2 * u + 2, :])
+        for i in (1, 2):
             for t in range(PACK):
                 gather_dy(False, t, 1280 + 256 * i, 256, later[i][:, t, :])
         weave_dz(512, 0, 768)
         round_w(0, w_early[:])
+        weave_dz(1280, 0, 256)
+        quantize_w(0, w_early[:])
         quantize_dz(512, 256, dz_b[512][:, 0 : PACK * 256])
         quantize_dz(768, 512, dz_b[512][:, PACK * 256 : PACK * 768])
-        quantize_w(0, w_early[:])
-        for t in range(2):
-            for c in range(2):
-                product_out(t, c * CHUNK, CHUNK, 2 * t + c)
-        for u in range(2):
-            form_half(u, 1280, h_third[:, 2 * u : 2 * u + 2, 0:256], later[0][:, 2 * u : 2 * u + 2, :])
-        form_half(0, 1536, h_third[:, 0:2, 256:512], later[1][:, 0:2, :])
-        weave_dz(1280, 0, 256)
-        form_half(1, 1536, h_third[:, 2:4, 256:512], later[1][:, 2:4, :])
         quantize_dz(1280, 256, dz_b[1280][:])
-        for t in range(2):
-            product_out(t, 2 * CHUNK, CHUNK, 4 + t)
-        form_half(0, 1792, h_last[:, 0:2, :], later[2][:, 0:2, :])
+        for c in range(CHUNKS - 1):
+            for t in range(2):
+                product_out(t, c * CHUNK, CHUNK, 2 * c + t)
+        for u in range(2):
+            form_half(u, 1536, h_last[:, 2 * u : 2 * u + 2, 0:256], later[1][:, 2 * u : 2 * u + 2, :])
+        form_half(0, 1792, h_last[:, 0:2, 256:512], later[2][:, 0:2, :])
         weave_dz(1536, 0, 256)
-        form_half(1, 1792, h_last[:, 2:4, :], later[2][:, 2:4, :])
+        form_half(1, 1792, h_last[:, 2:4, 256:512], later[2][:, 2:4, :])
         quantize_dz(1536, 256, dz_b[1536][:])
         product_out(0, 1536, 256, 6)
         weave_dz(1792, 0, 256)
@@ -205,68 +203,79 @@ def tile_attend_gmp_pl_kernel(tc, dyT, hE, wm, offs, offs2, out_0, out_1, out_2)
         for c in range(CHUNKS):
             product_out(3, c * CHUNK, CHUNK, (5 + c) % 8)
 
+        last = len(NODE_GROUPS) - 1
+        first_late = [2] * last + [1]
         picked = [keep.tile([P, E], F32, name="picked%d" % t) for t in range(2)]
-        picked_late = [keep.tile([P, 2, 2 * n], F32, name="late%d" % x0) for x0, n in NODE_PIECES]
-        y = [keep.tile([P, PACK, n], F32, name="y%d" % x0) for x0, n in NODE_PIECES]
-        y_b = [keep.tile([P, n * PACK], BF16, name="yb%d" % x0, align_bytes=64) for x0, n in NODE_PIECES]
+        picked_late = [
+            keep.tile([P, PACK - first_late[k], 2 * n], F32, name="late%d" % x0) for k, (x0, n) in enumerate(NODE_GROUPS)
+        ]
+        y = [keep.tile([P, PACK, n], F32, name="y%d" % x0) for x0, n in NODE_GROUPS]
+        y_b = [keep.tile([P, n * PACK], BF16, name="yb%d" % x0, align_bytes=64) for x0, n in NODE_GROUPS]
         y_codes = keep.tile([P, V], U32, name="y_codes", align_bytes=64)
         y_scales = keep.tile([P, V], U8, name="y_scales", align_bytes=64)
-        last = len(NODE_PIECES) - 1
 
-        def gather_dm(on_vector, t, x0, n, into):
+        def gather_dm(t, x0, n, into):
             window = dm[t][:].indirect(src_list[:, 2 * x0 // PER_COL : 2 * (x0 + n) // PER_COL])
-            if on_vector:
+            if t < 2:
                 nc.vector.tensor_copy(into, window)
             else:
                 nc.scalar.activation(into, window, COPY)
 
         def gather_early(t, x0, n):
-            gather_dm(True, t, x0, n, picked[t][:, 2 * x0 : 2 * (x0 + n)])
+            gather_dm(t, x0, n, picked[t][:, 2 * x0 : 2 * (x0 + n)])
 
-        def gather_late(t, k):
-            gather_dm(False, t, *NODE_PIECES[k], picked_late[k][:, t - 2, :])
+        def gather_late(t, k, a, n):
+            gather_dm(t, NODE_GROUPS[k][0] + a, n, picked_late[k][:, t - first_late[k], 2 * a : 2 * (a + n)])
 
         def add_early(t, k):
-            x0, n = NODE_PIECES[k]
+            x0, n = NODE_GROUPS[k]
             both = picked[t][:, 2 * x0 : 2 * (x0 + n)].rearrange("p (x j) -> p j x", j=2)
             nc.gpsimd.tensor_tensor(y[k][:, t, :], both[:, 0, :], both[:, 1, :], ADD)
 
-        def add_late(k):
-            both = picked_late[k][:].rearrange("p t (x j) -> p j t x", j=2)
-            nc.vector.tensor_tensor(y[k][:, 2:4, :], both[:, 0, :, :], both[:, 1, :, :], ADD)
+        def add_late(k, a, n):
+            both = picked_late[k][:, :, 2 * a : 2 * (a + n)].rearrange("p t (x j) -> p j t x", j=2)
+            nc.vector.tensor_tensor(y[k][:, first_late[k] : PACK, a : a + n], both[:, 0, :, :], both[:, 1, :, :], ADD)
 
-        def store_y(t0, t1, k):
-            x0, n = NODE_PIECES[k]
-            nc.sync.dma_start(out=y_rows[:, t0:t1, x0 : x0 + n], in_=y[k][:, t0:t1, :])
+        def store_y(t0, t1, k, a, n):
+            x0 = NODE_GROUPS[k][0] + a
+            nc.sync.dma_start(out=y_rows[:, t0:t1, x0 : x0 + n], in_=y[k][:, t0:t1, a : a + n])
 
-        def round_y(k):
-            nc.vector.tensor_copy(*interleaved_views(y_b[k][:], y[k][:]))
+        def round_y(k, a, n):
+            nc.vector.tensor_copy(*interleaved_views(y_b[k][:, PACK * a : PACK * (a + n)], y[k][:, :, a : a + n]))
 
-        def quantize_y(k):
-            x0, n = NODE_PIECES[k]
-            nc.vector.quantize_mx(
-                out=y_codes[:, x0 : x0 + n].bitcast(E4M3), scales=y_scales[:, x0 : x0 + n], in_=y_b[k][:]
-            )
-            nc.sync.dma_start(out=words_out[:, x0 : x0 + n], in_=y_codes[:, x0 : x0 + n].bitcast(I32))
+        def quantize_y(k, a, n):
+            x0 = NODE_GROUPS[k][0] + a
+            for b, m in ((0, 128), (128, 64)) if n == 192 else ((0, n),):
+                nc.vector.quantize_mx(
+                    out=y_codes[:, x0 + b : x0 + b + m].bitcast(E4M3),
+                    scales=y_scales[:, x0 + b : x0 + b + m],
+                    in_=y_b[k][:, PACK * (a + b) : PACK * (a + b + m)],
+                )
+            g0, gn = NODE_GROUPS[k]
+            if a + n == gn:
+                nc.sync.dma_start(out=words_out[:, g0 : g0 + gn], in_=y_codes[:, g0 : g0 + gn].bitcast(I32))
 
         for x0, n in ((0, 384), (384, 640)):
             gather_early(0, x0, n)
         for k in range(last + 1):
             add_early(0, k)
-        for x0, n in ((0, 384), (384, 256), (640, 256), (896, 128)):
+        for x0, n in NODE_GROUPS[:last]:
             gather_early(1, x0, n)
-        for k in range(last + 1):
+        gather_late(1, last, 0, NODE_GROUPS[last][1])
+        store_y(0, 1, last, 0, NODE_GROUPS[last][1])
+        for k in range(last):
             add_early(1, k)
-            store_y(0, 2, k)
-        for k in range(last + 1):
+            store_y(0, 2, k, 0, NODE_GROUPS[k][1])
+        for s, (k, a, n) in enumerate(NODE_STEPS):
             for t in (2, 3):
-                gather_late(t, k)
-            add_late(k)
-            store_y(2, 4, k)
-            if k > 0:
-                quantize_y(k - 1)
-            round_y(k)
-        quantize_y(last)
+                gather_late(t, k, a, n)
+            add_late(k, a, n)
+            if a + n == NODE_GROUPS[k][1]:
+                store_y(first_late[k], PACK, k, 0, a + n)
+            if s > 0:
+                quantize_y(*NODE_STEPS[s - 1])
+            round_y(k, a, n)
+        quantize_y(*NODE_STEPS[-1])
         for q in range(4):
             queue = nc.scalar if q % 2 else nc.sync
             queue.dma_start(out=scales_out[4 * q : 4 * q + 4, :], in_=y_scales[32 * q : 32 * q + 4, :].bitcast(I32))

@@ -145,6 +145,13 @@ def tile_attend_gmp_pl_kernel(tc, dyT, hE, wm, offs, offs2, out_0, out_1, out_2)
             product(t, e0, n, bank)
             empty(t, e0, n, bank)
 
+        def gather_dm(on_vector, t, x0, n, into):
+            window = dm[t][:].indirect(src_list[:, 2 * x0 // PER_COL : 2 * (x0 + n) // PER_COL])
+            if on_vector:
+                nc.vector.tensor_copy(into, window)
+            else:
+                nc.scalar.activation(into, window, COPY)
+
         first = [planes(g_first[u], 2, 512) for u in range(2)]
         second = [planes(g_second[u], 2, 768) for u in range(2)]
         for t in range(PACK):
@@ -186,6 +193,8 @@ def tile_attend_gmp_pl_kernel(tc, dyT, hE, wm, offs, offs2, out_0, out_1, out_2)
         weave_dz(1792, 0, 256)
         quantize_dz(1792, 256, dz_b[1792][:])
         product_out(0, 1792, 256, 7)
+        picked = [keep.tile([P, E], F32, name="picked%d" % t) for t in range(2)]
+        gather_dm(False, 0, 896, 128, picked[0][:, 2 * 896 : E])
         product_out(1, 3 * CHUNK, CHUNK, 0)
         for t in (2, 3):
             nc.vector.tensor_copy(
@@ -205,7 +214,6 @@ def tile_attend_gmp_pl_kernel(tc, dyT, hE, wm, offs, offs2, out_0, out_1, out_2)
 
         last = len(NODE_GROUPS) - 1
         first_late = [2] * last + [1]
-        picked = [keep.tile([P, E], F32, name="picked%d" % t) for t in range(2)]
         picked_late = [
             keep.tile([P, PACK - first_late[k], 2 * n], F32, name="late%d" % x0) for k, (x0, n) in enumerate(NODE_GROUPS)
         ]
@@ -214,18 +222,11 @@ def tile_attend_gmp_pl_kernel(tc, dyT, hE, wm, offs, offs2, out_0, out_1, out_2)
         y_codes = keep.tile([P, V], U32, name="y_codes", align_bytes=64)
         y_scales = keep.tile([P, V], U8, name="y_scales", align_bytes=64)
 
-        def gather_dm(t, x0, n, into):
-            window = dm[t][:].indirect(src_list[:, 2 * x0 // PER_COL : 2 * (x0 + n) // PER_COL])
-            if t < 2:
-                nc.vector.tensor_copy(into, window)
-            else:
-                nc.scalar.activation(into, window, COPY)
-
         def gather_early(t, x0, n):
-            gather_dm(t, x0, n, picked[t][:, 2 * x0 : 2 * (x0 + n)])
+            gather_dm(True, t, x0, n, picked[t][:, 2 * x0 : 2 * (x0 + n)])
 
         def gather_late(t, k, a, n):
-            gather_dm(t, NODE_GROUPS[k][0] + a, n, picked_late[k][:, t - first_late[k], 2 * a : 2 * (a + n)])
+            gather_dm(t < 2, t, NODE_GROUPS[k][0] + a, n, picked_late[k][:, t - first_late[k], 2 * a : 2 * (a + n)])
 
         def add_early(t, k):
             x0, n = NODE_GROUPS[k]
@@ -255,7 +256,7 @@ def tile_attend_gmp_pl_kernel(tc, dyT, hE, wm, offs, offs2, out_0, out_1, out_2)
             if a + n == gn:
                 nc.sync.dma_start(out=words_out[:, g0 : g0 + gn], in_=y_codes[:, g0 : g0 + gn].bitcast(I32))
 
-        for x0, n in ((0, 384), (384, 640)):
+        for x0, n in ((0, 384), (384, 512)):
             gather_early(0, x0, n)
         for k in range(last + 1):
             add_early(0, k)

@@ -184,14 +184,14 @@ def tile_attend_gmp_pl_kernel(tc, dyT, hE, wm, offs, offs2, out_0, out_1, out_2)
             for t in range(2):
                 product_out(t, c * CHUNK, CHUNK, 2 * c + t)
         for u in range(2):
-            form_half(u, 1536, h_last[:, 2 * u : 2 * u + 2, 0:256], later[1][:, 2 * u : 2 * u + 2, :])
-        form_half(0, 1792, h_last[:, 0:2, 256:512], later[2][:, 0:2, :])
-        weave_dz(1536, 0, 256)
-        form_half(1, 1792, h_last[:, 2:4, 256:512], later[2][:, 2:4, :])
-        quantize_dz(1536, 256, dz_b[1536][:])
+            for i in (1, 2):
+                h_planes = h_last[:, 2 * u : 2 * u + 2, 256 * (i - 1) : 256 * i]
+                form_half(u, 1280 + 256 * i, h_planes, later[i][:, 2 * u : 2 * u + 2, :])
+        for e0 in (1536, 1792):
+            weave_dz(e0, 0, 256)
+        for e0 in (1536, 1792):
+            quantize_dz(e0, 256, dz_b[e0][:])
         product_out(0, 1536, 256, 6)
-        weave_dz(1792, 0, 256)
-        quantize_dz(1792, 256, dz_b[1792][:])
         product_out(0, 1792, 256, 7)
         picked = [keep.tile([P, E], F32, name="picked%d" % t) for t in range(2)]
         gather_dm(False, 0, 896, 128, picked[0][:, 2 * 896 : E])

@@ -23,8 +23,7 @@ PACK = 4
 CHUNK = 512
 CHUNKS = E // CHUNK
 PER_COL = 16
-NODE_GROUPS = [(0, 384), (384, 256), (640, 192), (832, 192)]
-NODE_STEPS = [(0, 0, 384), (1, 0, 256), (2, 0, 192), (3, 0, 128), (3, 128, 64)]
+NODE_STEPS = [(0, 384, 3), (384, 256, 4), (640, 192, 3), (832, 128, 3), (960, 64, 3)]
 
 
 def interleaved_views(dst, src):
@@ -51,8 +50,7 @@ def tile_attend_gmp_pl_kernel(tc, dyT, hE, wm, offs, offs2, out_0, out_1, out_2)
         src_list = keep.tile([P, E // PER_COL], U16, name="src_list")
         dy = [keep.tile([P, V], F32, name="dy%d" % t) for t in range(PACK)]
         h_first = [keep.tile([P, 2, 512], F32, name="h_first%d" % u) for u in range(2)]
-        h_second = [keep.tile([P, 2, 1024], F32, name="h_second%d" % u) for u in range(2)]
-        h_last = keep.tile([P, PACK, 512], F32, name="h_last")
+        h_rest = [keep.tile([P, PACK, CHUNK], F32, name="h_rest%d" % c) for c in range(1, CHUNKS)]
         w_raw = keep.tile([P, PACK, D], F32, name="w_raw")
         twos = keep.tile([P, CHUNK], F32, name="twos")
 
@@ -64,28 +62,23 @@ def tile_attend_gmp_pl_kernel(tc, dyT, hE, wm, offs, offs2, out_0, out_1, out_2)
             nc.sync.dma_start(out=dy[t][:], in_=dy_rows[:, t, :])
         for u in range(2):
             nc.sync.dma_start(out=h_first[u][:], in_=h_rows[:, 2 * u : 2 * u + 2, 0:512])
-        for u in range(2):
-            nc.sync.dma_start(out=h_second[u][:], in_=h_rows[:, 2 * u : 2 * u + 2, 512:1536])
+        nc.sync.dma_start(out=h_rest[0][:], in_=h_rows[:, :, 512:1024])
         nc.sync.dma_start(out=w_raw[:], in_=w_rows)
-        nc.sync.dma_start(out=h_last[:], in_=h_rows[:, :, 1536:2048])
+        for c in (2, 3):
+            nc.sync.dma_start(out=h_rest[c - 1][:], in_=h_rows[:, :, c * CHUNK : (c + 1) * CHUNK])
         nc.sync.dma_start(src_list[:], offs2)
 
-        g_first = [keep.tile([P, 2 * 512], F32, name="g_first%d" % u) for u in range(2)]
-        g_second = [keep.tile([P, 2 * 768], F32, name="g_second%d" % u) for u in range(2)]
-        woven = [(0, 512), (512, 768), (1280, 256), (1536, 256), (1792, 256)]
+        g = [[keep.tile([P, 2, CHUNK], F32, name="g%d_%d" % (c, u)) for u in range(2)] for c in range(3)]
+        woven = [(c * CHUNK, CHUNK) for c in range(CHUNKS)]
         halves = {e0: keep.tile([P, 2, 2 * n], BF16, name="halves%d" % e0) for e0, n in woven}
         dz_b = {e0: keep.tile([P, PACK * n], BF16, name="dz_b%d" % e0, align_bytes=64) for e0, n in woven}
-        w_late = dz_b[1792]
         dz_codes = keep.tile([P, E], U32, name="dz_codes", align_bytes=64)
         dz_scales = keep.tile([P, E], U8, name="dz_scales", align_bytes=64)
         dm = [keep.tile([P, E], F32, name="dm%d" % t) for t in range(PACK)]
-        w_early = keep.tile([P, 2 * D], BF16, name="w_early", align_bytes=64)
-        w_codes = [keep.tile([P, 2 * P], U32, name="w_codes%d" % u, align_bytes=64) for u in range(2)]
-        w_scales = [keep.tile([P, 2 * P], U8, name="w_scales%d" % u, align_bytes=64) for u in range(2)]
+        w_b = keep.tile([P, PACK * D], BF16, name="w_b", align_bytes=64)
+        w_codes = keep.tile([P, D], U32, name="w_codes", align_bytes=64)
+        w_scales = keep.tile([P, D], U8, name="w_scales", align_bytes=64)
         w_dealt = w_raw[:].rearrange("p j (m t) -> p m j t", t=PACK)
-
-        def planes(buffer, count, n):
-            return buffer[:, 0 : count * n].rearrange("p (t e) -> p t e", t=count)
 
         def gather_dy(on_vector, t, e0, n, into):
             picked = dy[t][:].indirect(dst_list[:, e0 // PER_COL : (e0 + n) // PER_COL])
@@ -118,20 +111,14 @@ def tile_attend_gmp_pl_kernel(tc, dyT, hE, wm, offs, offs2, out_0, out_1, out_2)
                 out=dz_codes[:, e0 : e0 + n].bitcast(E5M2), scales=dz_scales[:, e0 : e0 + n], in_=rounded
             )
 
-        def round_w(t0, rounded):
-            nc.vector.tensor_copy(rounded.rearrange("p (t m j) -> p m j t", t=2, j=PACK), w_dealt[:, :, :, t0 : t0 + 2])
-
-        def quantize_w(t0, rounded):
-            nc.vector.quantize_mx(out=w_codes[t0 // 2][:].bitcast(E4M3), scales=w_scales[t0 // 2][:], in_=rounded)
-
         banks = [psum.tile([P, CHUNK], F32, name="bank%d" % b) for b in range(8)]
 
         def product(t, e0, n, bank):
             acc = banks[bank]
             nc.tensor.matmul_mx(
                 out=acc[:, 0:n],
-                lhsT=w_codes[t // 2][:, t % 2 * P : (t % 2 + 1) * P].bitcast(E4M3),
-                lhsT_scale=w_scales[t // 2][:, t % 2 * P : (t % 2 + 1) * P],
+                lhsT=w_codes[:, t * P : (t + 1) * P].bitcast(E4M3),
+                lhsT_scale=w_scales[:, t * P : (t + 1) * P],
                 rhs=dz_codes[:, e0 : e0 + n].bitcast(E5M2),
                 rhs_scale=dz_scales[:, e0 : e0 + n],
                 start=True,
@@ -152,131 +139,102 @@ def tile_attend_gmp_pl_kernel(tc, dyT, hE, wm, offs, offs2, out_0, out_1, out_2)
             else:
                 nc.scalar.activation(into, window, COPY)
 
-        first = [planes(g_first[u], 2, 512) for u in range(2)]
-        second = [planes(g_second[u], 2, 768) for u in range(2)]
-        for t in range(PACK):
-            gather_dy(True, t, 0, 512, first[t // 2][:, t % 2, :])
-            gather_dy(False, t, 512, 768, second[t // 2][:, t % 2, :])
-        form_half(0, 0, h_first[0][:], first[0])
-        for a in (0, 256):
-            form_dz(halves[0][:, 1, 2 * a : 2 * (a + 256)], h_first[1][:, :, a : a + 256], first[1][:, :, a : a + 256])
-        for a in (0, 256):
-            weave_dz(0, a, 256)
-        for a in (0, 256):
-            quantize_dz(a, 256, dz_b[0][:, PACK * a : PACK * (a + 256)])
-        later = [planes(buffer, PACK, 256) for buffer in (g_first[1], g_second[0], g_second[1])]
-        for t in range(PACK):
-            gather_dy(False, t, 1280, 256, later[0][:, t, :])
-        for u in range(2):
-            form_half(u, 512, h_second[u][:, :, 0:768], second[u])
-            form_half(u, 1280, h_second[u][:, :, 768:1024], later[0][:, 2 * u : 2 * u + 2, :])
-        for i in (1, 2):
-            for t in range(PACK):
-                gather_dy(False, t, 1280 + 256 * i, 256, later[i][:, t, :])
-        weave_dz(512, 0, 768)
-        round_w(0, w_early[:])
-        weave_dz(1280, 0, 256)
-        quantize_w(0, w_early[:])
-        quantize_dz(512, 256, dz_b[512][:, 0 : PACK * 256])
-        quantize_dz(768, 512, dz_b[512][:, PACK * 256 : PACK * 768])
-        quantize_dz(1280, 256, dz_b[1280][:])
-        for c in range(CHUNKS - 1):
-            for t in range(2):
-                product_out(t, c * CHUNK, CHUNK, 2 * c + t)
-        for u in range(2):
-            for i in (1, 2):
-                h_planes = h_last[:, 2 * u : 2 * u + 2, 256 * (i - 1) : 256 * i]
-                form_half(u, 1280 + 256 * i, h_planes, later[i][:, 2 * u : 2 * u + 2, :])
-        for e0 in (1536, 1792):
-            weave_dz(e0, 0, 256)
-        for e0 in (1536, 1792):
-            quantize_dz(e0, 256, dz_b[e0][:])
-        product_out(0, 1536, 256, 6)
-        product_out(0, 1792, 256, 7)
-        picked = [keep.tile([P, E], F32, name="picked%d" % t) for t in range(2)]
-        gather_dm(False, 0, 896, 128, picked[0][:, 2 * 896 : E])
-        product_out(1, 3 * CHUNK, CHUNK, 0)
-        for t in (2, 3):
-            nc.vector.tensor_copy(
-                w_late[:, (t - 2) * D : (t - 1) * D].rearrange("p (m j) -> p m j", j=PACK), w_dealt[:, :, :, t]
-            )
-        for t in (2, 3):
-            cols = slice((t - 2) * P, (t - 1) * P)
-            nc.vector.quantize_mx(
-                out=w_codes[1][:, cols].bitcast(E4M3),
-                scales=w_scales[1][:, cols],
-                in_=w_late[:, (t - 2) * D : (t - 1) * D],
-            )
-        for c in range(CHUNKS):
-            product_out(2, c * CHUNK, CHUNK, 1 + c)
-        for c in range(CHUNKS):
-            product_out(3, c * CHUNK, CHUNK, (5 + c) % 8)
+        def h_pair(c, u):
+            return h_first[u][:] if c == 0 else h_rest[c - 1][:, 2 * u : 2 * u + 2, :]
 
-        last = len(NODE_GROUPS) - 1
-        first_late = [2] * last + [1]
-        picked_late = [
-            keep.tile([P, PACK - first_late[k], 2 * n], F32, name="late%d" % x0) for k, (x0, n) in enumerate(NODE_GROUPS)
-        ]
-        y = [keep.tile([P, PACK, n], F32, name="y%d" % x0) for x0, n in NODE_GROUPS]
-        y_b = [keep.tile([P, n * PACK], BF16, name="yb%d" % x0, align_bytes=64) for x0, n in NODE_GROUPS]
+        def form_and_weave(c):
+            e0 = c * CHUNK
+            form_half(0, e0, h_pair(c, 0), g[c % 3][0][:])
+            for a in (0, 256):
+                form_dz(halves[e0][:, 1, 2 * a : 2 * (a + 256)], h_pair(c, 1)[:, :, a : a + 256], g[c % 3][1][:, :, a : a + 256])
+            for a in (0, 256):
+                weave_dz(e0, a, 256)
+
+        def quantize_halves(c):
+            for a in (0, 256):
+                quantize_dz(c * CHUNK + a, 256, dz_b[c * CHUNK][:, PACK * a : PACK * (a + 256)])
+
+        for t in range(PACK):
+            for c in range(3):
+                gather_dy(c == 0, t, c * CHUNK, CHUNK, g[c][t // 2][:, t % 2, :])
+        form_and_weave(0)
+        quantize_halves(0)
+        for t in range(PACK):
+            gather_dy(False, t, 3 * CHUNK, CHUNK, g[0][t // 2][:, t % 2, :])
+        form_and_weave(1)
+        nc.vector.tensor_copy(w_b[:].rearrange("p (t m j) -> p m j t", t=PACK, j=PACK), w_dealt)
+        quantize_dz(CHUNK, CHUNK, dz_b[CHUNK][:])
+        nc.vector.quantize_mx(out=w_codes[:].bitcast(E4M3), scales=w_scales[:], in_=w_b[:])
+        form_and_weave(2)
+        quantize_halves(2)
+        for c in range(CHUNKS - 1):
+            for t in range(PACK):
+                product_out(t, c * CHUNK, CHUNK, (PACK * c + t) % 8)
+        form_and_weave(3)
+        quantize_halves(3)
+        for t, e0, n, bank in ((0, 1536, 256, 4), (0, 1792, 256, 5), (1, 1536, 512, 6)):
+            product(t, e0, n, bank)
+            nc.vector.tensor_copy(dm[t][:, e0 : e0 + n], banks[bank][:, 0:n])
+        for t in (3, 2):
+            product_out(t, 3 * CHUNK, CHUNK, (5 + t) % 8)
+
+        early = {t: keep.tile([P, E], F32, name="early%d" % t) for t in (0, 3)}
+        late = {x0: keep.tile([P, t1 - 1, 2 * n], F32, name="late%d" % x0) for x0, n, t1 in NODE_STEPS}
+        y = keep.tile([P, PACK, V], F32, name="y")
+        y_b = keep.tile([P, V * PACK], BF16, name="y_b", align_bytes=64)
         y_codes = keep.tile([P, V], U32, name="y_codes", align_bytes=64)
         y_scales = keep.tile([P, V], U8, name="y_scales", align_bytes=64)
 
-        def gather_early(t, x0, n):
-            gather_dm(True, t, x0, n, picked[t][:, 2 * x0 : 2 * (x0 + n)])
+        def look_up(on_vector, t, x0, x1):
+            gather_dm(on_vector, t, x0, x1 - x0, early[t][:, 2 * x0 : 2 * x1])
 
-        def gather_late(t, k, a, n):
-            gather_dm(t < 2, t, NODE_GROUPS[k][0] + a, n, picked_late[k][:, t - first_late[k], 2 * a : 2 * (a + n)])
+        def add_early(t, x0, x1):
+            both = early[t][:, 2 * x0 : 2 * x1].rearrange("p (x j) -> p j x", j=2)
+            nc.gpsimd.tensor_tensor(y[:, t, x0:x1], both[:, 0, :], both[:, 1, :], ADD)
 
-        def add_early(t, k):
-            x0, n = NODE_GROUPS[k]
-            both = picked[t][:, 2 * x0 : 2 * (x0 + n)].rearrange("p (x j) -> p j x", j=2)
-            nc.gpsimd.tensor_tensor(y[k][:, t, :], both[:, 0, :], both[:, 1, :], ADD)
+        def add_late(x0, n, t1):
+            both = late[x0][:].rearrange("p t (x j) -> p j t x", j=2)
+            nc.vector.tensor_tensor(y[:, 1:t1, x0 : x0 + n], both[:, 0, :, :], both[:, 1, :, :], ADD)
 
-        def add_late(k, a, n):
-            both = picked_late[k][:, :, 2 * a : 2 * (a + n)].rearrange("p t (x j) -> p j t x", j=2)
-            nc.vector.tensor_tensor(y[k][:, first_late[k] : PACK, a : a + n], both[:, 0, :, :], both[:, 1, :, :], ADD)
+        def store_y(t0, t1, x0, x1):
+            nc.sync.dma_start(out=y_rows[:, t0:t1, x0:x1], in_=y[:, t0:t1, x0:x1])
 
-        def store_y(t0, t1, k, a, n):
-            x0 = NODE_GROUPS[k][0] + a
-            nc.sync.dma_start(out=y_rows[:, t0:t1, x0 : x0 + n], in_=y[k][:, t0:t1, a : a + n])
+        def round_y(x0, n):
+            nc.vector.tensor_copy(*interleaved_views(y_b[:, PACK * x0 : PACK * (x0 + n)], y[:, :, x0 : x0 + n]))
 
-        def round_y(k, a, n):
-            nc.vector.tensor_copy(*interleaved_views(y_b[k][:, PACK * a : PACK * (a + n)], y[k][:, :, a : a + n]))
-
-        def quantize_y(k, a, n):
-            x0 = NODE_GROUPS[k][0] + a
-            for b, m in ((0, 128), (128, 64)) if n == 192 else ((0, n),):
+        def quantize_y(x0, n):
+            for b, m in ((x0, 128), (x0 + 128, 64)) if n == 192 else ((x0, n),):
                 nc.vector.quantize_mx(
-                    out=y_codes[:, x0 + b : x0 + b + m].bitcast(E4M3),
-                    scales=y_scales[:, x0 + b : x0 + b + m],
-                    in_=y_b[k][:, PACK * (a + b) : PACK * (a + b + m)],
+                    out=y_codes[:, b : b + m].bitcast(E4M3),
+                    scales=y_scales[:, b : b + m],
+                    in_=y_b[:, PACK * b : PACK * (b + m)],
                 )
-            g0, gn = NODE_GROUPS[k]
-            if a + n == gn:
-                nc.sync.dma_start(out=words_out[:, g0 : g0 + gn], in_=y_codes[:, g0 : g0 + gn].bitcast(I32))
 
-        for x0, n in ((0, 384), (384, 512)):
-            gather_early(0, x0, n)
-        for k in range(last + 1):
-            add_early(0, k)
-        for x0, n in NODE_GROUPS[:last]:
-            gather_early(1, x0, n)
-        gather_late(1, last, 0, NODE_GROUPS[last][1])
-        store_y(0, 1, last, 0, NODE_GROUPS[last][1])
-        for k in range(last):
-            add_early(1, k)
-            store_y(0, 2, k, 0, NODE_GROUPS[k][1])
-        for s, (k, a, n) in enumerate(NODE_STEPS):
-            for t in (2, 3):
-                gather_late(t, k, a, n)
-            add_late(k, a, n)
-            if a + n == NODE_GROUPS[k][1]:
-                store_y(first_late[k], PACK, k, 0, a + n)
+        def store_words(x0, x1):
+            nc.sync.dma_start(out=words_out[:, x0:x1], in_=y_codes[:, x0:x1].bitcast(I32))
+
+        for on_vector, t, x0, x1 in ((True, 0, 0, 256), (True, 0, 256, 640)):
+            look_up(on_vector, t, x0, x1)
+            add_early(t, x0, x1)
+        store_y(0, 1, 0, 640)
+        for on_vector, t, x0, x1 in ((False, 3, 640, 1024), (True, 3, 0, 384), (True, 0, 640, 1024)):
+            look_up(on_vector, t, x0, x1)
+            add_early(t, x0, x1)
+            store_y(t, t + 1, x0, x1)
+        gather_dm(True, 3, 384, 256, late[384][:, 2, :])
+        for s, (x0, n, t1) in enumerate(NODE_STEPS):
+            for t in (1, 2):
+                gather_dm(False, t, x0, n, late[x0][:, t - 1, :])
+            add_late(x0, n, t1)
+            store_y(1, t1, x0, x0 + n)
             if s > 0:
-                quantize_y(*NODE_STEPS[s - 1])
-            round_y(k, a, n)
-        quantize_y(*NODE_STEPS[-1])
+                p0, pn = NODE_STEPS[s - 1][0:2]
+                quantize_y(p0, pn)
+                if p0 != 832:
+                    store_words(p0, p0 + pn)
+            round_y(x0, n)
+        quantize_y(960, 64)
+        store_words(832, 1024)
         for q in range(4):
             queue = nc.scalar if q % 2 else nc.sync
             queue.dma_start(out=scales_out[4 * q : 4 * q + 4, :], in_=y_scales[32 * q : 32 * q + 4, :].bitcast(I32))

@@ -162,7 +162,10 @@ def tile_attend_gmp_pl_kernel(tc, dyT, hE, wm, offs, offs2, out_0, out_1, out_2)
         for t in range(PACK):
             gather_dy(False, t, 3 * CHUNK, CHUNK, g[0][t // 2][:, t % 2, :])
         form_and_weave(1)
-        nc.vector.tensor_copy(w_b[:].rearrange("p (t m j) -> p m j t", t=PACK, j=PACK), w_dealt)
+        for t0 in (0, 2):
+            nc.vector.tensor_copy(
+                w_b[:, t0 * D : (t0 + 2) * D].rearrange("p (t m j) -> p m j t", t=2, j=PACK), w_dealt[:, :, :, t0 : t0 + 2]
+            )
         quantize_dz(CHUNK, CHUNK, dz_b[CHUNK][:])
         nc.vector.quantize_mx(out=w_codes[:].bitcast(E4M3), scales=w_scales[:], in_=w_b[:])
         form_and_weave(2)

@@ -23,7 +23,7 @@ PACK = 4
 CHUNK = 512
 CHUNKS = E // CHUNK
 PER_COL = 16
-NODE_STEPS = [(0, 384, 3), (384, 256, 4), (640, 192, 3), (832, 128, 3), (960, 64, 3)]
+NODE_STEPS = [(0, 384, 4), (384, 256, 3), (640, 192, 3), (832, 128, 4), (960, 64, 4)]
 
 
 def interleaved_views(dst, src):
@@ -178,9 +178,6 @@ def tile_attend_gmp_pl_kernel(tc, dyT, hE, wm, offs, offs2, out_0, out_1, out_2)
         for t, e0, n, bank in ((0, 1536, 256, 4), (0, 1792, 256, 5), (1, 1536, 512, 6)):
             product(t, e0, n, bank)
             nc.vector.tensor_copy(dm[t][:, e0 : e0 + n], banks[bank][:, 0:n])
-        for t in (3, 2):
-            product_out(t, 3 * CHUNK, CHUNK, (5 + t) % 8)
-
         early = {t: keep.tile([P, E], F32, name="early%d" % t) for t in (0, 3)}
         late = {x0: keep.tile([P, t1 - 1, 2 * n], F32, name="late%d" % x0) for x0, n, t1 in NODE_STEPS}
         y = keep.tile([P, PACK, V], F32, name="y")
@@ -216,17 +213,21 @@ def tile_attend_gmp_pl_kernel(tc, dyT, hE, wm, offs, offs2, out_0, out_1, out_2)
         def store_words(x0, x1):
             nc.sync.dma_start(out=words_out[:, x0:x1], in_=y_codes[:, x0:x1].bitcast(I32))
 
-        for on_vector, t, x0, x1 in ((True, 0, 0, 256), (True, 0, 256, 640)):
-            look_up(on_vector, t, x0, x1)
-            add_early(t, x0, x1)
-        store_y(0, 1, 0, 640)
-        for on_vector, t, x0, x1 in ((False, 3, 640, 1024), (True, 3, 0, 384), (True, 0, 640, 1024)):
-            look_up(on_vector, t, x0, x1)
-            add_early(t, x0, x1)
-            store_y(t, t + 1, x0, x1)
-        gather_dm(True, 3, 384, 256, late[384][:, 2, :])
+        look_up(False, 0, 768, 1024)
+        add_early(0, 768, 1024)
+        for t in (3, 2):
+            product_out(t, 3 * CHUNK, CHUNK, (5 + t) % 8)
+        look_up(True, 0, 384, 768)
+        add_early(0, 384, 768)
+        look_up(True, 3, 384, 832)
+        add_early(3, 384, 832)
+        store_y(3, 4, 384, 832)
+        look_up(True, 0, 0, 384)
+        add_early(0, 0, 384)
+        store_y(0, 1, 0, V)
+        gather_dm(True, 3, 0, 384, late[0][:, 2, :])
         for s, (x0, n, t1) in enumerate(NODE_STEPS):
-            for t in (1, 2):
+            for t in range(1, t1 if s else 3):
                 gather_dm(False, t, x0, n, late[x0][:, t - 1, :])
             add_late(x0, n, t1)
             store_y(1, t1, x0, x0 + n)

@@ -100,10 +100,11 @@ def tile_attend_gmp_pl_kernel(tc, dyT, hE, wm, offs, offs2, out_0, out_1, out_2)
         def form_half(u, e0, h_planes, g_planes):
             form_dz(halves[e0][:, u, :], h_planes, g_planes)
 
-        def weave_dz(e0, a, n):
-            nc.vector.tensor_copy(
-                dz_b[e0][:].bitcast(I32).rearrange("p (e u) -> p e u", u=2)[:, a : a + n, :],
-                halves[e0][:].bitcast(I32).rearrange("p u e -> p e u")[:, a : a + n, :],
+        def weave_dz(e0, a, n, on_vector=True):
+            copy, word = (nc.vector.tensor_copy, I32) if on_vector else (nc.scalar.copy, U32)
+            copy(
+                dz_b[e0][:].bitcast(word).rearrange("p (e u) -> p e u", u=2)[:, a : a + n, :],
+                halves[e0][:].bitcast(word).rearrange("p u e -> p e u")[:, a : a + n, :],
             )
 
         def quantize_dz(e0, n, rounded):
@@ -142,13 +143,17 @@ def tile_attend_gmp_pl_kernel(tc, dyT, hE, wm, offs, offs2, out_0, out_1, out_2)
         def h_pair(c, u):
             return h_first[u][:] if c == 0 else h_rest[c - 1][:, 2 * u : 2 * u + 2, :]
 
+        def form_second(c, a):
+            form_dz(
+                halves[c * CHUNK][:, 1, 2 * a : 2 * (a + 256)], h_pair(c, 1)[:, :, a : a + 256], g[c % 3][1][:, :, a : a + 256]
+            )
+
         def form_and_weave(c):
-            e0 = c * CHUNK
-            form_half(0, e0, h_pair(c, 0), g[c % 3][0][:])
+            form_half(0, c * CHUNK, h_pair(c, 0), g[c][0][:])
             for a in (0, 256):
-                form_dz(halves[e0][:, 1, 2 * a : 2 * (a + 256)], h_pair(c, 1)[:, :, a : a + 256], g[c % 3][1][:, :, a : a + 256])
+                form_second(c, a)
             for a in (0, 256):
-                weave_dz(e0, a, 256)
+                weave_dz(c * CHUNK, a, 256, on_vector=(c, a) != (2, 256))
 
         def quantize_halves(c):
             for a in (0, 256):
@@ -169,13 +174,19 @@ def tile_attend_gmp_pl_kernel(tc, dyT, hE, wm, offs, offs2, out_0, out_1, out_2)
         quantize_dz(CHUNK, CHUNK, dz_b[CHUNK][:])
         nc.vector.quantize_mx(out=w_codes[:].bitcast(E4M3), scales=w_scales[:], in_=w_b[:])
         form_and_weave(2)
-        quantize_halves(2)
+        form_half(0, 3 * CHUNK, h_pair(3, 0), g[0][0][:])
+        form_second(3, 0)
+        quantize_dz(2 * CHUNK, CHUNK, dz_b[2 * CHUNK][:])
         for c in range(CHUNKS - 1):
-            for t in range(PACK):
+            for t in range(PACK if c < 2 else 2):
                 product_out(t, c * CHUNK, CHUNK, (PACK * c + t) % 8)
-        form_and_weave(3)
+        form_second(3, 256)
+        for a in (0, 256):
+            weave_dz(3 * CHUNK, a, 256)
         quantize_halves(3)
-        for t, e0, n, bank in ((0, 1536, 256, 4), (0, 1792, 256, 5), (1, 1536, 512, 6)):
+        product_out(0, 1536, 256, 4)
+        product_out(2, 1024, 512, 2)
+        for t, e0, n, bank in ((3, 1024, 512, 3), (0, 1792, 256, 5), (1, 1536, 512, 6)):
             product(t, e0, n, bank)
             nc.vector.tensor_copy(dm[t][:, e0 : e0 + n], banks[bank][:, 0:n])
         early = {t: keep.tile([P, E], F32, name="early%d" % t) for t in (0, 3)}

@@ -23,7 +23,7 @@ PACK = 4
 CHUNK = 512
 CHUNKS = E // CHUNK
 PER_COL = 16
-NODE_STEPS = [(0, 384, 4), (384, 256, 3), (640, 192, 3), (832, 128, 4), (960, 64, 4)]
+NODE_STEPS = [(0, 384, 4), (384, 256, 3), (640, 256, 3), (896, 64, 4), (960, 64, 4)]
 
 
 def interleaved_views(dst, src):
@@ -214,12 +214,11 @@ def tile_attend_gmp_pl_kernel(tc, dyT, hE, wm, offs, offs2, out_0, out_1, out_2)
             nc.vector.tensor_copy(*interleaved_views(y_b[:, PACK * x0 : PACK * (x0 + n)], y[:, :, x0 : x0 + n]))
 
         def quantize_y(x0, n):
-            for b, m in ((x0, 128), (x0 + 128, 64)) if n == 192 else ((x0, n),):
-                nc.vector.quantize_mx(
-                    out=y_codes[:, b : b + m].bitcast(E4M3),
-                    scales=y_scales[:, b : b + m],
-                    in_=y_b[:, PACK * b : PACK * (b + m)],
-                )
+            nc.vector.quantize_mx(
+                out=y_codes[:, x0 : x0 + n].bitcast(E4M3),
+                scales=y_scales[:, x0 : x0 + n],
+                in_=y_b[:, PACK * x0 : PACK * (x0 + n)],
+            )
 
         def store_words(x0, x1):
             nc.sync.dma_start(out=words_out[:, x0:x1], in_=y_codes[:, x0:x1].bitcast(I32))
@@ -230,9 +229,9 @@ def tile_attend_gmp_pl_kernel(tc, dyT, hE, wm, offs, offs2, out_0, out_1, out_2)
             product_out(t, 3 * CHUNK, CHUNK, (5 + t) % 8)
         look_up(True, 0, 384, 768)
         add_early(0, 384, 768)
-        look_up(True, 3, 384, 832)
-        add_early(3, 384, 832)
-        store_y(3, 4, 384, 832)
+        look_up(True, 3, 384, 896)
+        add_early(3, 384, 896)
+        store_y(3, 4, 384, 896)
         look_up(True, 0, 0, 384)
         add_early(0, 0, 384)
         store_y(0, 1, 0, V)
@@ -241,15 +240,16 @@ def tile_attend_gmp_pl_kernel(tc, dyT, hE, wm, offs, offs2, out_0, out_1, out_2)
             for t in range(1, t1 if s else 3):
                 gather_dm(False, t, x0, n, late[x0][:, t - 1, :])
             add_late(x0, n, t1)
-            store_y(1, t1, x0, x0 + n)
+            if x0 != 896:
+                store_y(1, t1, min(x0, 896), x0 + n)
             if s > 0:
                 p0, pn = NODE_STEPS[s - 1][0:2]
                 quantize_y(p0, pn)
-                if p0 != 832:
+                if p0 != 896:
                     store_words(p0, p0 + pn)
             round_y(x0, n)
         quantize_y(960, 64)
-        store_words(832, 1024)
+        store_words(896, V)
         for q in range(4):
             queue = nc.scalar if q % 2 else nc.sync
             queue.dma_start(out=scales_out[4 * q : 4 * q + 4, :], in_=y_scales[32 * q : 32 * q + 4, :].bitcast(I32))

@@ -223,18 +223,17 @@ def tile_attend_gmp_pl_kernel(tc, dyT, hE, wm, offs, offs2, out_0, out_1, out_2)
         def store_words(x0, x1):
             nc.sync.dma_start(out=words_out[:, x0:x1], in_=y_codes[:, x0:x1].bitcast(I32))
 
-        look_up(False, 0, 768, 1024)
-        add_early(0, 768, 1024)
+        look_up(False, 0, 640, 1024)
+        add_early(0, 640, 1024)
         for t in (3, 2):
             product_out(t, 3 * CHUNK, CHUNK, (5 + t) % 8)
-        look_up(True, 0, 384, 768)
-        add_early(0, 384, 768)
+        for x0, x1 in ((0, 384), (384, 640)):
+            look_up(True, 0, x0, x1)
+            add_early(0, x0, x1)
+        store_y(0, 1, 0, V)
         look_up(True, 3, 384, 896)
         add_early(3, 384, 896)
         store_y(3, 4, 384, 896)
-        look_up(True, 0, 0, 384)
-        add_early(0, 0, 384)
-        store_y(0, 1, 0, V)
         gather_dm(True, 3, 0, 384, late[0][:, 2, :])
         for s, (x0, n, t1) in enumerate(NODE_STEPS):
             for t in range(1, t1 if s else 3):

@@ -223,11 +223,11 @@ def tile_attend_gmp_pl_kernel(tc, dyT, hE, wm, offs, offs2, out_0, out_1, out_2)
         def store_words(x0, x1):
             nc.sync.dma_start(out=words_out[:, x0:x1], in_=y_codes[:, x0:x1].bitcast(I32))
 
-        look_up(False, 0, 640, 1024)
-        add_early(0, 640, 1024)
+        look_up(False, 0, 704, 1024)
+        add_early(0, 704, 1024)
         for t in (3, 2):
             product_out(t, 3 * CHUNK, CHUNK, (5 + t) % 8)
-        for x0, x1 in ((0, 384), (384, 640)):
+        for x0, x1 in ((0, 384), (384, 704)):
             look_up(True, 0, x0, x1)
             add_early(0, x0, x1)
         store_y(0, 1, 0, V)

@@ -186,7 +186,7 @@ def tile_attend_gmp_pl_kernel(tc, dyT, hE, wm, offs, offs2, out_0, out_1, out_2)
         quantize_halves(3)
         product_out(0, 1536, 256, 4)
         product_out(2, 1024, 512, 2)
-        for t, e0, n, bank in ((3, 1024, 512, 3), (0, 1792, 256, 5), (1, 1536, 512, 6)):
+        for t, e0, n, bank in ((3, 1024, 512, 3), (0, 1792, 256, 5), (3, 1536, 512, 6)):
             product(t, e0, n, bank)
             nc.vector.tensor_copy(dm[t][:, e0 : e0 + n], banks[bank][:, 0:n])
         early = {t: keep.tile([P, E], F32, name="early%d" % t) for t in (0, 3)}
@@ -203,9 +203,9 @@ def tile_attend_gmp_pl_kernel(tc, dyT, hE, wm, offs, offs2, out_0, out_1, out_2)
             both = early[t][:, 2 * x0 : 2 * x1].rearrange("p (x j) -> p j x", j=2)
             nc.gpsimd.tensor_tensor(y[:, t, x0:x1], both[:, 0, :], both[:, 1, :], ADD)
 
-        def add_late(x0, n, t1):
-            both = late[x0][:].rearrange("p t (x j) -> p j t x", j=2)
-            nc.vector.tensor_tensor(y[:, 1:t1, x0 : x0 + n], both[:, 0, :, :], both[:, 1, :, :], ADD)
+        def add_late(x0, a, n, t1):
+            both = late[x0][:, :, 2 * a : 2 * (a + n)].rearrange("p t (x j) -> p j t x", j=2)
+            nc.vector.tensor_tensor(y[:, 1:t1, x0 + a : x0 + a + n], both[:, 0, :, :], both[:, 1, :, :], ADD)
 
         def store_y(t0, t1, x0, x1):
             nc.sync.dma_start(out=y_rows[:, t0:t1, x0:x1], in_=y[:, t0:t1, x0:x1])
@@ -223,22 +223,22 @@ def tile_attend_gmp_pl_kernel(tc, dyT, hE, wm, offs, offs2, out_0, out_1, out_2)
         def store_words(x0, x1):
             nc.sync.dma_start(out=words_out[:, x0:x1], in_=y_codes[:, x0:x1].bitcast(I32))
 
-        look_up(False, 0, 704, 1024)
-        add_early(0, 704, 1024)
-        for t in (3, 2):
-            product_out(t, 3 * CHUNK, CHUNK, (5 + t) % 8)
-        for x0, x1 in ((0, 384), (384, 704)):
-            look_up(True, 0, x0, x1)
-            add_early(0, x0, x1)
-        store_y(0, 1, 0, V)
-        look_up(True, 3, 384, 896)
-        add_early(3, 384, 896)
+        look_up(False, 0, 720, 1024)
+        add_early(0, 720, 1024)
+        for t, bank in ((1, 7), (2, 0)):
+            product_out(t, 3 * CHUNK, CHUNK, bank)
+        for t, x0, x1 in ((0, 0, 384), (3, 384, 896), (0, 384, 720)):
+            look_up(True, t, x0, x1)
+            add_early(t, x0, x1)
         store_y(3, 4, 384, 896)
-        gather_dm(True, 3, 0, 384, late[0][:, 2, :])
+        store_y(0, 1, 0, V)
+        for a in (0, 192):
+            gather_dm(True, 3, a, 192, late[0][:, 2, 2 * a : 2 * (a + 192)])
         for s, (x0, n, t1) in enumerate(NODE_STEPS):
             for t in range(1, t1 if s else 3):
                 gather_dm(False, t, x0, n, late[x0][:, t - 1, :])
-            add_late(x0, n, t1)
+            for a, m in ((0, n),) if s else ((0, 192), (192, 192)):
+                add_late(x0, a, m, t1)
             if x0 != 896:
                 store_y(1, t1, min(x0, 896), x0 + n)
             if s > 0:

@@ -21,16 +21,9 @@ COPY = mybir.ActivationFunctionType.Copy
 P = 128
 PACK = 4
 CHUNK = 512
+HALF = CHUNK // 2
 CHUNKS = E // CHUNK
 PER_COL = 16
-NODE_STEPS = [(0, 384, 4), (384, 256, 3), (640, 256, 3), (896, 64, 4), (960, 64, 4)]
-
-
-def interleaved_views(dst, src):
-    return (
-        dst.rearrange("p (c i t) -> p c t i", i=4, t=PACK),
-        src.rearrange("p t (c i) -> p c t i", i=4),
-    )
 
 
 def tile_attend_gmp_pl_kernel(tc, dyT, hE, wm, offs, offs2, out_0, out_1, out_2):
@@ -49,75 +42,80 @@ def tile_attend_gmp_pl_kernel(tc, dyT, hE, wm, offs, offs2, out_0, out_1, out_2)
         dst_list = keep.tile([P, E // PER_COL], U16, name="dst_list")
         src_list = keep.tile([P, E // PER_COL], U16, name="src_list")
         dy = [keep.tile([P, V], F32, name="dy%d" % t) for t in range(PACK)]
-        h_first = [keep.tile([P, 2, 512], F32, name="h_first%d" % u) for u in range(2)]
+        h_first = [keep.tile([P, 2, CHUNK], F32, name="h_first%d" % u) for u in range(2)]
         h_rest = [keep.tile([P, PACK, CHUNK], F32, name="h_rest%d" % c) for c in range(1, CHUNKS)]
         w_raw = keep.tile([P, PACK, D], F32, name="w_raw")
-        twos = keep.tile([P, CHUNK], F32, name="twos")
 
         ones = keep.tile([P, CHUNK], F32, name="ones")
-        nc.gpsimd.memset(ones[:], 1.0)
+        twos = keep.tile([P, CHUNK], F32, name="twos")
+        nc.vector.memset(ones[:], 1.0)
         nc.scalar.activation(twos[:], ones[:], COPY, scale=2.0)
         nc.sync.dma_start(dst_list[:], offs)
         for t in range(PACK):
             nc.sync.dma_start(out=dy[t][:], in_=dy_rows[:, t, :])
         for u in range(2):
-            nc.sync.dma_start(out=h_first[u][:], in_=h_rows[:, 2 * u : 2 * u + 2, 0:512])
-        nc.sync.dma_start(out=h_rest[0][:], in_=h_rows[:, :, 512:1024])
-        nc.sync.dma_start(out=w_raw[:], in_=w_rows)
-        for c in (2, 3):
+            nc.sync.dma_start(out=h_first[u][:], in_=h_rows[:, 2 * u : 2 * u + 2, 0:CHUNK])
+        for c in range(1, CHUNKS):
             nc.sync.dma_start(out=h_rest[c - 1][:], in_=h_rows[:, :, c * CHUNK : (c + 1) * CHUNK])
+            if c == 1:
+                nc.sync.dma_start(out=w_raw[:], in_=w_rows)
         nc.sync.dma_start(src_list[:], offs2)
 
         g = [[keep.tile([P, 2, CHUNK], F32, name="g%d_%d" % (c, u)) for u in range(2)] for c in range(3)]
-        woven = [(c * CHUNK, CHUNK) for c in range(CHUNKS)]
-        halves = {e0: keep.tile([P, 2, 2 * n], BF16, name="halves%d" % e0) for e0, n in woven}
-        dz_b = {e0: keep.tile([P, PACK * n], BF16, name="dz_b%d" % e0, align_bytes=64) for e0, n in woven}
+        halves = [keep.tile([P, 2, 2 * CHUNK], BF16, name="halves%d" % c) for c in range(CHUNKS)]
+        dz_b = [keep.tile([P, PACK * CHUNK], BF16, name="dz_b%d" % c, align_bytes=64) for c in range(CHUNKS)]
         dz_codes = keep.tile([P, E], U32, name="dz_codes", align_bytes=64)
         dz_scales = keep.tile([P, E], U8, name="dz_scales", align_bytes=64)
         dm = [keep.tile([P, E], F32, name="dm%d" % t) for t in range(PACK)]
         w_b = keep.tile([P, PACK * D], BF16, name="w_b", align_bytes=64)
         w_codes = keep.tile([P, D], U32, name="w_codes", align_bytes=64)
         w_scales = keep.tile([P, D], U8, name="w_scales", align_bytes=64)
-        w_dealt = w_raw[:].rearrange("p j (m t) -> p m j t", t=PACK)
+        banks = [psum.tile([P, CHUNK], F32, name="bank%d" % b) for b in range(8)]
 
-        def gather_dy(on_vector, t, e0, n, into):
-            picked = dy[t][:].indirect(dst_list[:, e0 // PER_COL : (e0 + n) // PER_COL])
+        def gather_dy(on_vector, t, c):
+            picked = dy[t][:].indirect(dst_list[:, c * CHUNK // PER_COL : (c + 1) * CHUNK // PER_COL])
+            into = g[c % 3][t // 2][:, t % 2, :]
             if on_vector:
-                nc.vector.tensor_tensor(into, picked, twos[:, 0:n], MULT)
+                nc.vector.tensor_tensor(into, picked, twos[:], MULT)
             else:
                 nc.scalar.activation(into, picked, COPY, scale=2.0)
 
-        def form_dz(into, h_planes, g_planes):
+        def round_w(t0):
+            nc.vector.tensor_copy(
+                w_b[:, t0 * D : (t0 + 2) * D].rearrange("p (t m j) -> p m j t", t=2, j=PACK),
+                w_raw[:].rearrange("p j (m t) -> p m j t", t=PACK)[:, :, :, t0 : t0 + 2],
+            )
+
+        def form(c, u, a, n):
+            h_pair = h_first[u][:] if c == 0 else h_rest[c - 1][:, 2 * u : 2 * u + 2, :]
             nc.vector.scalar_tensor_tensor(
-                out=into.rearrange("p (e t) -> p e t", t=h_planes.shape[1]),
-                in0=h_planes.rearrange("p t e -> p e t"),
+                out=halves[c][:, u, 2 * a : 2 * (a + n)].rearrange("p (e t) -> p e t", t=2),
+                in0=h_pair[:, :, a : a + n].rearrange("p t e -> p e t"),
                 scalar=0.0,
-                in1=g_planes.rearrange("p t e -> p e t"),
+                in1=g[c % 3][u][:, :, a : a + n].rearrange("p t e -> p e t"),
                 op0=MAX,
                 op1=MULT,
             )
 
-        def form_half(u, e0, h_planes, g_planes):
-            form_dz(halves[e0][:, u, :], h_planes, g_planes)
-
-        def weave_dz(e0, a, n, on_vector=True):
+        def weave(on_vector, c, a, n):
             copy, word = (nc.vector.tensor_copy, I32) if on_vector else (nc.scalar.copy, U32)
             copy(
-                dz_b[e0][:].bitcast(word).rearrange("p (e u) -> p e u", u=2)[:, a : a + n, :],
-                halves[e0][:].bitcast(word).rearrange("p u e -> p e u")[:, a : a + n, :],
+                dz_b[c][:].bitcast(word).rearrange("p (e u) -> p e u", u=2)[:, a : a + n, :],
+                halves[c][:].bitcast(word).rearrange("p u e -> p e u")[:, a : a + n, :],
             )
 
-        def quantize_dz(e0, n, rounded):
+        def quantize_dz(c, a, n):
+            e0 = c * CHUNK + a
             nc.vector.quantize_mx(
-                out=dz_codes[:, e0 : e0 + n].bitcast(E5M2), scales=dz_scales[:, e0 : e0 + n], in_=rounded
+                out=dz_codes[:, e0 : e0 + n].bitcast(E5M2),
+                scales=dz_scales[:, e0 : e0 + n],
+                in_=dz_b[c][:, PACK * a : PACK * (a + n)],
             )
 
-        banks = [psum.tile([P, CHUNK], F32, name="bank%d" % b) for b in range(8)]
-
-        def product(t, e0, n, bank):
-            acc = banks[bank]
+        def product(on_vector, t, c, a, n, bank):
+            e0 = c * CHUNK + a
             nc.tensor.matmul_mx(
-                out=acc[:, 0:n],
+                out=banks[bank][:, 0:n],
                 lhsT=w_codes[:, t * P : (t + 1) * P].bitcast(E4M3),
                 lhsT_scale=w_scales[:, t * P : (t + 1) * P],
                 rhs=dz_codes[:, e0 : e0 + n].bitcast(E5M2),
@@ -125,129 +123,144 @@ def tile_attend_gmp_pl_kernel(tc, dyT, hE, wm, offs, offs2, out_0, out_1, out_2)
                 start=True,
                 stop=True,
             )
+            copy = nc.vector.tensor_copy if on_vector else nc.scalar.copy
+            copy(dm[t][:, e0 : e0 + n], banks[bank][:, 0:n])
 
-        def empty(t, e0, n, bank):
-            nc.scalar.copy(dm[t][:, e0 : e0 + n], banks[bank][:, 0:n])
+        for t in range(PACK):
+            for c in range(3):
+                gather_dy(c == 0, t, c)
+        form(0, 0, 0, CHUNK)
+        for a in (0, HALF):
+            form(0, 1, a, HALF)
+        for a in (0, HALF):
+            weave(True, 0, a, HALF)
+        for a in (0, HALF):
+            quantize_dz(0, a, HALF)
+        for t in range(PACK):
+            gather_dy(False, t, 3)
+        form(1, 0, 0, CHUNK)
+        for a in (0, HALF):
+            form(1, 1, a, HALF)
+        for a in (0, HALF):
+            weave(True, 1, a, HALF)
+        for t0 in (0, 2):
+            round_w(t0)
+        quantize_dz(1, 0, CHUNK)
+        nc.vector.quantize_mx(out=w_codes[:].bitcast(E4M3), scales=w_scales[:], in_=w_b[:])
+        form(2, 0, 0, CHUNK)
+        for a in (0, HALF):
+            form(2, 1, a, HALF)
+        for a in (0, HALF):
+            weave(a == 0, 2, a, HALF)
+        form(3, 0, 0, CHUNK)
+        form(3, 1, 0, HALF)
+        quantize_dz(2, 0, CHUNK)
+        for c in range(CHUNKS - 1):
+            for k, t in enumerate(range(PACK) if c < 2 else (0, 3)):
+                product(False, t, c, 0, CHUNK, (PACK * c + k) % 8)
+        form(3, 1, HALF, HALF)
+        for a in (0, HALF):
+            weave(True, 3, a, HALF)
+        for a in (0, HALF):
+            quantize_dz(3, a, HALF)
+        product(False, 0, 3, 0, HALF, 4)
+        product(False, 2, 2, 0, CHUNK, 2)
+        product(True, 1, 2, 0, CHUNK, 3)
+        product(True, 0, 3, HALF, HALF, 5)
+        product(True, 1, 3, 0, CHUNK, 6)
 
-        def product_out(t, e0, n, bank):
-            product(t, e0, n, bank)
-            empty(t, e0, n, bank)
+        y_flat = keep.tile([P, PACK * V], F32, name="y")
+        y = y_flat[:].rearrange("p (t x) -> p t x", t=PACK)
+        y_b = keep.tile([P, V * PACK], BF16, name="y_b", align_bytes=64)
+        y_codes = keep.tile([P, V], U32, name="y_codes", align_bytes=64)
+        y_scales = keep.tile([P, V], U8, name="y_scales", align_bytes=64)
 
-        def gather_dm(on_vector, t, x0, n, into):
-            window = dm[t][:].indirect(src_list[:, 2 * x0 // PER_COL : 2 * (x0 + n) // PER_COL])
+        def look_up(on_vector, t, x0, x1, into):
+            window = dm[t][:].indirect(src_list[:, 2 * x0 // PER_COL : 2 * x1 // PER_COL])
             if on_vector:
                 nc.vector.tensor_copy(into, window)
             else:
                 nc.scalar.activation(into, window, COPY)
 
-        def h_pair(c, u):
-            return h_first[u][:] if c == 0 else h_rest[c - 1][:, 2 * u : 2 * u + 2, :]
+        def add_pairs(engine, t0, t1, x0, x1, pairs):
+            both = pairs.rearrange("p t (x j) -> p j t x", j=2)
+            engine.tensor_tensor(y[:, t0:t1, x0:x1], both[:, 0, :, :], both[:, 1, :, :], ADD)
 
-        def form_second(c, a):
-            form_dz(
-                halves[c * CHUNK][:, 1, 2 * a : 2 * (a + 256)], h_pair(c, 1)[:, :, a : a + 256], g[c % 3][1][:, :, a : a + 256]
-            )
+        def side_by_side(on_vector, on_scalar, n, pairs):
+            starts = sorted((t * V + x0, t, x0, engine) for engine, (t, x0) in enumerate((on_scalar, on_vector)))
+            for k, (at, t, x0, engine) in enumerate(starts):
+                look_up(engine == 1, t, x0, x0 + n, pairs[:, 2 * n * k : 2 * n * (k + 1)])
+            first, step = starts[0][0], starts[1][0] - starts[0][0]
+            sums = y_flat[:, first : first + 2 * step].rearrange("p (r x) -> p r x", r=2)[:, :, 0:n]
+            both = pairs.rearrange("p (r x j) -> p j r x", r=2, j=2)
+            nc.gpsimd.tensor_tensor(sums, both[:, 0, :, :], both[:, 1, :, :], ADD)
 
-        def form_and_weave(c):
-            form_half(0, c * CHUNK, h_pair(c, 0), g[c][0][:])
-            for a in (0, 256):
-                form_second(c, a)
-            for a in (0, 256):
-                weave_dz(c * CHUNK, a, 256, on_vector=(c, a) != (2, 256))
+        def shared(t, x0, cut, x1, pairs):
+            look_up(True, t, x0, cut, pairs[:, 0 : 2 * (cut - x0)])
+            look_up(False, t, cut, x1, pairs[:, 2 * (cut - x0) : 2 * (x1 - x0)])
+            add_pairs(nc.gpsimd, t, t + 1, x0, x1, pairs.rearrange("p (t c) -> p t c", t=1))
 
-        def quantize_halves(c):
-            for a in (0, 256):
-                quantize_dz(c * CHUNK + a, 256, dz_b[c * CHUNK][:, PACK * a : PACK * (a + 256)])
-
-        for t in range(PACK):
-            for c in range(3):
-                gather_dy(c == 0, t, c * CHUNK, CHUNK, g[c][t // 2][:, t % 2, :])
-        form_and_weave(0)
-        quantize_halves(0)
-        for t in range(PACK):
-            gather_dy(False, t, 3 * CHUNK, CHUNK, g[0][t // 2][:, t % 2, :])
-        form_and_weave(1)
-        for t0 in (0, 2):
-            nc.vector.tensor_copy(
-                w_b[:, t0 * D : (t0 + 2) * D].rearrange("p (t m j) -> p m j t", t=2, j=PACK), w_dealt[:, :, :, t0 : t0 + 2]
-            )
-        quantize_dz(CHUNK, CHUNK, dz_b[CHUNK][:])
-        nc.vector.quantize_mx(out=w_codes[:].bitcast(E4M3), scales=w_scales[:], in_=w_b[:])
-        form_and_weave(2)
-        form_half(0, 3 * CHUNK, h_pair(3, 0), g[0][0][:])
-        form_second(3, 0)
-        quantize_dz(2 * CHUNK, CHUNK, dz_b[2 * CHUNK][:])
-        for c in range(CHUNKS - 1):
-            for t in range(PACK if c < 2 else 2):
-                product_out(t, c * CHUNK, CHUNK, (PACK * c + t) % 8)
-        form_second(3, 256)
-        for a in (0, 256):
-            weave_dz(3 * CHUNK, a, 256)
-        quantize_halves(3)
-        product_out(0, 1536, 256, 4)
-        product_out(2, 1024, 512, 2)
-        for t, e0, n, bank in ((3, 1024, 512, 3), (0, 1792, 256, 5), (3, 1536, 512, 6)):
-            product(t, e0, n, bank)
-            nc.vector.tensor_copy(dm[t][:, e0 : e0 + n], banks[bank][:, 0:n])
-        early = {t: keep.tile([P, E], F32, name="early%d" % t) for t in (0, 3)}
-        late = {x0: keep.tile([P, t1 - 1, 2 * n], F32, name="late%d" % x0) for x0, n, t1 in NODE_STEPS}
-        y = keep.tile([P, PACK, V], F32, name="y")
-        y_b = keep.tile([P, V * PACK], BF16, name="y_b", align_bytes=64)
-        y_codes = keep.tile([P, V], U32, name="y_codes", align_bytes=64)
-        y_scales = keep.tile([P, V], U8, name="y_scales", align_bytes=64)
-
-        def look_up(on_vector, t, x0, x1):
-            gather_dm(on_vector, t, x0, x1 - x0, early[t][:, 2 * x0 : 2 * x1])
-
-        def add_early(t, x0, x1):
-            both = early[t][:, 2 * x0 : 2 * x1].rearrange("p (x j) -> p j x", j=2)
-            nc.gpsimd.tensor_tensor(y[:, t, x0:x1], both[:, 0, :], both[:, 1, :], ADD)
-
-        def add_late(x0, a, n, t1):
-            both = late[x0][:, :, 2 * a : 2 * (a + n)].rearrange("p t (x j) -> p j t x", j=2)
-            nc.vector.tensor_tensor(y[:, 1:t1, x0 + a : x0 + a + n], both[:, 0, :, :], both[:, 1, :, :], ADD)
+        def late(t0, t1, x0, x1, pairs):
+            n = 2 * (x1 - x0)
+            for t in range(t0, t1):
+                look_up(False, t, x0, x1, pairs[:, (t - t0) * n : (t - t0 + 1) * n])
+            add_pairs(nc.vector, t0, t1, x0, x1, pairs.rearrange("p (t c) -> p t c", t=t1 - t0))
 
         def store_y(t0, t1, x0, x1):
             nc.sync.dma_start(out=y_rows[:, t0:t1, x0:x1], in_=y[:, t0:t1, x0:x1])
 
-        def round_y(x0, n):
-            nc.vector.tensor_copy(*interleaved_views(y_b[:, PACK * x0 : PACK * (x0 + n)], y[:, :, x0 : x0 + n]))
+        def round_y(x0, x1):
+            nc.vector.tensor_copy(
+                y_b[:, PACK * x0 : PACK * x1].rearrange("p (c i t) -> p c t i", i=4, t=PACK),
+                y[:, :, x0:x1].rearrange("p t (c i) -> p c t i", i=4),
+            )
 
-        def quantize_y(x0, n):
+        def quantize_y(x0, x1):
             nc.vector.quantize_mx(
-                out=y_codes[:, x0 : x0 + n].bitcast(E4M3),
-                scales=y_scales[:, x0 : x0 + n],
-                in_=y_b[:, PACK * x0 : PACK * (x0 + n)],
+                out=y_codes[:, x0:x1].bitcast(E4M3), scales=y_scales[:, x0:x1], in_=y_b[:, PACK * x0 : PACK * x1]
             )
 
         def store_words(x0, x1):
             nc.sync.dma_start(out=words_out[:, x0:x1], in_=y_codes[:, x0:x1].bitcast(I32))
 
-        look_up(False, 0, 720, 1024)
-        add_early(0, 720, 1024)
-        for t, bank in ((1, 7), (2, 0)):
-            product_out(t, 3 * CHUNK, CHUNK, bank)
-        for t, x0, x1 in ((0, 0, 384), (3, 384, 896), (0, 384, 720)):
-            look_up(True, t, x0, x1)
-            add_early(t, x0, x1)
-        store_y(3, 4, 384, 896)
-        store_y(0, 1, 0, V)
-        for a in (0, 192):
-            gather_dm(True, 3, a, 192, late[0][:, 2, 2 * a : 2 * (a + 192)])
-        for s, (x0, n, t1) in enumerate(NODE_STEPS):
-            for t in range(1, t1 if s else 3):
-                gather_dm(False, t, x0, n, late[x0][:, t - 1, :])
-            for a, m in ((0, n),) if s else ((0, 192), (192, 192)):
-                add_late(x0, a, m, t1)
-            if x0 != 896:
-                store_y(1, t1, min(x0, 896), x0 + n)
-            if s > 0:
-                p0, pn = NODE_STEPS[s - 1][0:2]
-                quantize_y(p0, pn)
-                if p0 != 896:
-                    store_words(p0, p0 + pn)
-            round_y(x0, n)
-        quantize_y(960, 64)
+        stage = [keep.tile([P, 2048], F32, name="stage%d" % k) for k in range(4)]
+        spare = stage[3]
+        shared(0, 0, 240, 480, stage[0][:, 0:960])
+        side_by_side((0, 480), (1, 0), 272, stage[0][:, 960:2048])
+        product(False, 2, 3, 0, CHUNK, 7)
+        shared(1, 272, 576, 752, stage[1][:, 0:960])
+        side_by_side((1, 752), (0, 752), 272, stage[2][:, 0:1088])
+        store_y(0, 2, 0, V)
+        product(False, 3, 3, 0, CHUNK, 0)
+        shared(2, 0, 160, 320, y_flat[:, 2 * V + 496 : 3 * V + 112])
+        last_three = [(False, 3, 256, 512), (True, 2, 320, 512), (True, 3, 0, 256)]
+        held = [stage[1][:, 1024:1536], stage[1][:, 1536:1920], stage[2][:, 1280:1792]]
+        for (on_vector, t, x0, x1), pairs in zip(last_three, held):
+            look_up(on_vector, t, x0, x1, pairs)
+        for (on_vector, t, x0, x1), pairs in zip(last_three, held):
+            add_pairs(nc.vector, t, t + 1, x0, x1, pairs.rearrange("p (t c) -> p t c", t=1))
+        store_y(2, 4, 0, 512)
+        round_y(256, 512)
+        round_y(0, 256)
+        quantize_y(256, 512)
+        late(2, 4, 512, 768, spare[:, 0:1024])
+        store_y(2, 4, 512, 768)
+        quantize_y(0, 256)
+        store_words(0, 512)
+        round_y(512, 768)
+        late(2, 4, 768, 896, spare[:, 1024:1536])
+        quantize_y(512, 768)
+        store_words(512, 768)
+        round_y(768, 896)
+        late(2, 4, 896, 960, spare[:, 1536:1792])
+        quantize_y(768, 896)
+        store_words(768, 896)
+        late(2, 4, 960, V, spare[:, 1792:2048])
+        store_y(2, 4, 768, V)
+        round_y(896, 960)
+        round_y(960, V)
+        quantize_y(896, 960)
+        quantize_y(960, V)
         store_words(896, V)
         for q in range(4):
             queue = nc.scalar if q % 2 else nc.sync

@@ -229,8 +229,9 @@ def tile_attend_gmp_pl_kernel(tc, dyT, hE, wm, offs, offs2, out_0, out_1, out_2)
         side_by_side((0, 480), (1, 0), 272, stage[0][:, 960:2048])
         product(False, 2, 3, 0, CHUNK, 7)
         shared(1, 272, 576, 752, stage[1][:, 0:960])
+        store_y(0, 2, 0, 752)
         side_by_side((1, 752), (0, 752), 272, stage[2][:, 0:1088])
-        store_y(0, 2, 0, V)
+        store_y(0, 2, 752, V)
         product(False, 3, 3, 0, CHUNK, 0)
         shared(2, 0, 160, 320, y_flat[:, 2 * V + 496 : 3 * V + 112])
         last_three = [(False, 3, 256, 512), (True, 2, 320, 512), (True, 3, 0, 256)]
@@ -254,14 +255,13 @@ def tile_attend_gmp_pl_kernel(tc, dyT, hE, wm, offs, offs2, out_0, out_1, out_2)
         round_y(768, 896)
         late(2, 4, 896, 960, spare[:, 1536:1792])
         quantize_y(768, 896)
-        store_words(768, 896)
         late(2, 4, 960, V, spare[:, 1792:2048])
         store_y(2, 4, 768, V)
         round_y(896, 960)
         round_y(960, V)
         quantize_y(896, 960)
         quantize_y(960, V)
-        store_words(896, V)
+        store_words(768, V)
         for q in range(4):
             queue = nc.scalar if q % 2 else nc.sync
             queue.dma_start(out=scales_out[4 * q : 4 * q + 4, :], in_=y_scales[32 * q : 32 * q + 4, :].bitcast(I32))

@@ -173,7 +173,7 @@ def tile_attend_gmp_pl_kernel(tc, dyT, hE, wm, offs, offs2, out_0, out_1, out_2)
         y = y_flat[:].rearrange("p (t x) -> p t x", t=PACK)
         y_b = keep.tile([P, V * PACK], BF16, name="y_b", align_bytes=64)
         y_codes = keep.tile([P, V], U32, name="y_codes", align_bytes=64)
-        y_scales = keep.tile([P, V], U8, name="y_scales", align_bytes=64)
+        y_scales = keep.tile([P, V // 4], U8, name="y_scales", align_bytes=64)
 
         def look_up(on_vector, t, x0, x1, into):
             window = dm[t][:].indirect(src_list[:, 2 * x0 // PER_COL : 2 * x1 // PER_COL])
@@ -216,8 +216,11 @@ def tile_attend_gmp_pl_kernel(tc, dyT, hE, wm, offs, offs2, out_0, out_1, out_2)
             )
 
         def quantize_y(x0, x1):
+            j = x0 // 256
             nc.vector.quantize_mx(
-                out=y_codes[:, x0:x1].bitcast(E4M3), scales=y_scales[:, x0:x1], in_=y_b[:, PACK * x0 : PACK * x1]
+                out=y_codes[:, x0:x1].bitcast(E4M3),
+                scales=y_scales[4 * j : P, x0 - 256 * j : x1 - 256 * j],
+                in_=y_b[:, PACK * x0 : PACK * x1],
             )
 
         def store_words(x0, x1):
@@ -233,35 +236,38 @@ def tile_attend_gmp_pl_kernel(tc, dyT, hE, wm, offs, offs2, out_0, out_1, out_2)
         side_by_side((1, 752), (0, 752), 272, stage[2][:, 0:1088])
         store_y(0, 2, 752, V)
         product(False, 3, 3, 0, CHUNK, 0)
-        shared(2, 0, 160, 320, y_flat[:, 2 * V + 496 : 3 * V + 112])
-        last_three = [(False, 3, 256, 512), (True, 2, 320, 512), (True, 3, 0, 256)]
+        shared(2, 256, 416, 576, y_flat[:, 2 * V + 752 : 3 * V + 368])
+        last_three = [(False, 3, 512, 768), (True, 2, 576, 768), (True, 3, 256, 512)]
         held = [stage[1][:, 1024:1536], stage[1][:, 1536:1920], stage[2][:, 1280:1792]]
         for (on_vector, t, x0, x1), pairs in zip(last_three, held):
             look_up(on_vector, t, x0, x1, pairs)
         for (on_vector, t, x0, x1), pairs in zip(last_three, held):
             add_pairs(nc.vector, t, t + 1, x0, x1, pairs.rearrange("p (t c) -> p t c", t=1))
-        store_y(2, 4, 0, 512)
-        round_y(256, 512)
-        round_y(0, 256)
-        quantize_y(256, 512)
-        late(2, 4, 512, 768, spare[:, 0:1024])
-        store_y(2, 4, 512, 768)
-        quantize_y(0, 256)
-        store_words(0, 512)
+        store_y(2, 4, 256, 768)
         round_y(512, 768)
-        late(2, 4, 768, 896, spare[:, 1024:1536])
+        round_y(256, 512)
         quantize_y(512, 768)
-        store_words(512, 768)
-        round_y(768, 896)
-        late(2, 4, 896, 960, spare[:, 1536:1792])
-        quantize_y(768, 896)
-        late(2, 4, 960, V, spare[:, 1792:2048])
+        late(2, 4, 768, V, spare[:, 0:1024])
         store_y(2, 4, 768, V)
-        round_y(896, 960)
-        round_y(960, V)
-        quantize_y(896, 960)
-        quantize_y(960, V)
+        quantize_y(256, 512)
+        store_words(256, 768)
+        round_y(768, V)
+        late(2, 4, 0, 128, spare[:, 1024:1536])
+        quantize_y(768, V)
         store_words(768, V)
+        round_y(0, 128)
+        late(2, 4, 128, 192, spare[:, 1536:1792])
+        quantize_y(0, 128)
+        late(2, 4, 192, 256, spare[:, 1792:2048])
+        store_y(2, 4, 0, 256)
+        round_y(128, 192)
+        round_y(192, 256)
+        quantize_y(128, 192)
+        quantize_y(192, 256)
+        store_words(0, 256)
         for q in range(4):
             queue = nc.scalar if q % 2 else nc.sync
-            queue.dma_start(out=scales_out[4 * q : 4 * q + 4, :], in_=y_scales[32 * q : 32 * q + 4, :].bitcast(I32))
+            queue.dma_start(
+                out=scales_out[4 * q : 4 * q + 4, :].rearrange("r (j x) -> j r x", j=4),
+                in_=y_scales[32 * q : 32 * q + 16, :].bitcast(I32),
+            )

@@ -32,6 +32,7 @@ def tile_attend_gmp_pl_kernel(tc, dyT, hE, wm, offs, offs2, out_0, out_1, out_2)
     h_rows = hE.rearrange("(p t) e -> p t e", t=PACK)
     w_rows = wm.rearrange("(p j) d -> p j d", j=PACK)
     y_rows = out_0.rearrange("(p t) x -> p t x", t=PACK)
+    y_flat_out = out_0.rearrange("(p t) x -> p (t x)", t=PACK)
     words_out = out_1.rearrange("o p x l -> p (o x l)").bitcast(I32)
     scales_out = out_2.rearrange("o f x -> (o f) x").bitcast(I32)
 
@@ -209,6 +210,9 @@ def tile_attend_gmp_pl_kernel(tc, dyT, hE, wm, offs, offs2, out_0, out_1, out_2)
         def store_y(t0, t1, x0, x1):
             nc.sync.dma_start(out=y_rows[:, t0:t1, x0:x1], in_=y[:, t0:t1, x0:x1])
 
+        def store_run(first, end):
+            nc.sync.dma_start(out=y_flat_out[:, first:end], in_=y_flat[:, first:end])
+
         def round_y(x0, x1):
             nc.vector.tensor_copy(
                 y_b[:, PACK * x0 : PACK * x1].rearrange("p (c i t) -> p c t i", i=4, t=PACK),
@@ -229,12 +233,12 @@ def tile_attend_gmp_pl_kernel(tc, dyT, hE, wm, offs, offs2, out_0, out_1, out_2)
         stage = [keep.tile([P, 2048], F32, name="stage%d" % k) for k in range(4)]
         spare = stage[3]
         shared(0, 0, 240, 480, stage[0][:, 0:960])
+        store_run(0, 480)
         side_by_side((0, 480), (1, 0), 272, stage[0][:, 960:2048])
         product(False, 2, 3, 0, CHUNK, 7)
         shared(1, 272, 576, 752, stage[1][:, 0:960])
-        store_y(0, 2, 0, 752)
         side_by_side((1, 752), (0, 752), 272, stage[2][:, 0:1088])
-        store_y(0, 2, 752, V)
+        store_run(480, 2 * V)
         product(False, 3, 3, 0, CHUNK, 0)
         shared(2, 256, 416, 576, y_flat[:, 2 * V + 752 : 3 * V + 368])
         last_three = [(False, 3, 512, 768), (True, 2, 576, 768), (True, 3, 256, 512)]

from contextlib import ExitStack

import concourse.mybir as mybir

V, E, D, DV = 1024, 2048, 512, 512
FLOPS = 2 * DV * D * E

F32 = mybir.dt.float32
BF16 = mybir.dt.bfloat16
I32 = mybir.dt.int32
U32 = mybir.dt.uint32
U16 = mybir.dt.uint16
U8 = mybir.dt.uint8
E4M3 = mybir.dt.float8_e4m3fn_x4
E5M2 = mybir.dt.float8_e5m2_x4
MULT = mybir.AluOpType.mult
ADD = mybir.AluOpType.add
MAX = mybir.AluOpType.max
COPY = mybir.ActivationFunctionType.Copy

P = 128
PACK = 4
CHUNK = 512
HALF = CHUNK // 2
CHUNKS = E // CHUNK
PER_COL = 16


def tile_attend_gmp_pl_kernel(tc, dyT, hE, wm, offs, offs2, out_0, out_1, out_2):
    nc = tc.nc
    dy_rows = dyT.rearrange("(p t) v -> p t v", t=PACK)
    h_rows = hE.rearrange("(p t) e -> p t e", t=PACK)
    w_rows = wm.rearrange("(p j) d -> p j d", j=PACK)
    y_rows = out_0.rearrange("(p t) x -> p t x", t=PACK)
    y_flat_out = out_0.rearrange("(p t) x -> p (t x)", t=PACK)
    words_out = out_1.rearrange("o p x l -> p (o x l)").bitcast(I32)
    scales_out = out_2.rearrange("o f x -> (o f) x").bitcast(I32)

    with ExitStack() as ctx:
        keep = ctx.enter_context(tc.tile_pool(name="keep", bufs=1))
        psum = ctx.enter_context(tc.psum_pool(name="psum", bufs=1))

        dst_list = keep.tile([P, E // PER_COL], U16, name="dst_list")
        src_list = keep.tile([P, E // PER_COL], U16, name="src_list")
        dy = [keep.tile([P, V], F32, name="dy%d" % t) for t in range(PACK)]
        h_first = [keep.tile([P, 2, CHUNK], F32, name="h_first%d" % u) for u in range(2)]
        h_rest = [keep.tile([P, PACK, CHUNK], F32, name="h_rest%d" % c) for c in range(1, CHUNKS)]
        w_raw = keep.tile([P, PACK, D], F32, name="w_raw")

        ones = keep.tile([P, CHUNK], F32, name="ones")
        twos = keep.tile([P, CHUNK], F32, name="twos")
        nc.vector.memset(ones[:], 1.0)
        nc.scalar.activation(twos[:], ones[:], COPY, scale=2.0)
        nc.sync.dma_start(dst_list[:], offs)
        for t in range(PACK):
            nc.sync.dma_start(out=dy[t][:], in_=dy_rows[:, t, :])
        for u in range(2):
            nc.sync.dma_start(out=h_first[u][:], in_=h_rows[:, 2 * u : 2 * u + 2, 0:CHUNK])
        for c in range(1, CHUNKS):
            nc.sync.dma_start(out=h_rest[c - 1][:], in_=h_rows[:, :, c * CHUNK : (c + 1) * CHUNK])
            if c == 1:
                nc.sync.dma_start(out=w_raw[:], in_=w_rows)
        nc.sync.dma_start(src_list[:], offs2)

        g = [[keep.tile([P, 2, CHUNK], F32, name="g%d_%d" % (c, u)) for u in range(2)] for c in range(3)]
        halves = [keep.tile([P, 2, 2 * CHUNK], BF16, name="halves%d" % c) for c in range(CHUNKS)]
        dz_b = [keep.tile([P, PACK * CHUNK], BF16, name="dz_b%d" % c, align_bytes=64) for c in range(CHUNKS)]
        dz_codes = keep.tile([P, E], U32, name="dz_codes", align_bytes=64)
        dz_scales = keep.tile([P, E], U8, name="dz_scales", align_bytes=64)
        dm = [keep.tile([P, E], F32, name="dm%d" % t) for t in range(PACK)]
        w_b = keep.tile([P, PACK * D], BF16, name="w_b", align_bytes=64)
        w_codes = keep.tile([P, D], U32, name="w_codes", align_bytes=64)
        w_scales = keep.tile([P, D], U8, name="w_scales", align_bytes=64)
        banks = [psum.tile([P, CHUNK], F32, name="bank%d" % b) for b in range(8)]

        def gather_dy(on_vector, t, c):
            picked = dy[t][:].indirect(dst_list[:, c * CHUNK // PER_COL : (c + 1) * CHUNK // PER_COL])
            into = g[c % 3][t // 2][:, t % 2, :]
            if on_vector:
                nc.vector.tensor_tensor(into, picked, twos[:], MULT)
            else:
                nc.scalar.activation(into, picked, COPY, scale=2.0)

        def round_w(t0):
            nc.vector.tensor_copy(
                w_b[:, t0 * D : (t0 + 2) * D].rearrange("p (t m j) -> p m j t", t=2, j=PACK),
                w_raw[:].rearrange("p j (m t) -> p m j t", t=PACK)[:, :, :, t0 : t0 + 2],
            )

        def form(c, u, a, n):
            h_pair = h_first[u][:] if c == 0 else h_rest[c - 1][:, 2 * u : 2 * u + 2, :]
            nc.vector.scalar_tensor_tensor(
                out=halves[c][:, u, 2 * a : 2 * (a + n)].rearrange("p (e t) -> p e t", t=2),
                in0=h_pair[:, :, a : a + n].rearrange("p t e -> p e t"),
                scalar=0.0,
                in1=g[c % 3][u][:, :, a : a + n].rearrange("p t e -> p e t"),
                op0=MAX,
                op1=MULT,
            )

        def weave(on_vector, c, a, n):
            copy, word = (nc.vector.tensor_copy, I32) if on_vector else (nc.scalar.copy, U32)
            copy(
                dz_b[c][:].bitcast(word).rearrange("p (e u) -> p e u", u=2)[:, a : a + n, :],
                halves[c][:].bitcast(word).rearrange("p u e -> p e u")[:, a : a + n, :],
            )

        def quantize_dz(c, a, n):
            e0 = c * CHUNK + a
            nc.vector.quantize_mx(
                out=dz_codes[:, e0 : e0 + n].bitcast(E5M2),
                scales=dz_scales[:, e0 : e0 + n],
                in_=dz_b[c][:, PACK * a : PACK * (a + n)],
            )

        def product(on_vector, t, c, a, n, bank):
            e0 = c * CHUNK + a
            nc.tensor.matmul_mx(
                out=banks[bank][:, 0:n],
                lhsT=w_codes[:, t * P : (t + 1) * P].bitcast(E4M3),
                lhsT_scale=w_scales[:, t * P : (t + 1) * P],
                rhs=dz_codes[:, e0 : e0 + n].bitcast(E5M2),
                rhs_scale=dz_scales[:, e0 : e0 + n],
                start=True,
                stop=True,
            )
            copy = nc.vector.tensor_copy if on_vector else nc.scalar.copy
            copy(dm[t][:, e0 : e0 + n], banks[bank][:, 0:n])

        for t in range(PACK):
            for c in range(3):
                gather_dy(c == 0, t, c)
        form(0, 0, 0, CHUNK)
        for a in (0, HALF):
            form(0, 1, a, HALF)
        for a in (0, HALF):
            weave(True, 0, a, HALF)
        for a in (0, HALF):
            quantize_dz(0, a, HALF)
        for t in range(PACK):
            gather_dy(False, t, 3)
        form(1, 0, 0, CHUNK)
        for a in (0, HALF):
            form(1, 1, a, HALF)
        for a in (0, HALF):
            weave(True, 1, a, HALF)
        for t0 in (0, 2):
            round_w(t0)
        quantize_dz(1, 0, CHUNK)
        nc.vector.quantize_mx(out=w_codes[:].bitcast(E4M3), scales=w_scales[:], in_=w_b[:])
        form(2, 0, 0, CHUNK)
        for a in (0, HALF):
            form(2, 1, a, HALF)
        for a in (0, HALF):
            weave(a == 0, 2, a, HALF)
        form(3, 0, 0, CHUNK)
        form(3, 1, 0, HALF)
        quantize_dz(2, 0, CHUNK)
        for c in range(CHUNKS - 1):
            for k, t in enumerate(range(PACK) if c < 2 else (0, 3)):
                product(False, t, c, 0, CHUNK, (PACK * c + k) % 8)
        form(3, 1, HALF, HALF)
        for a in (0, HALF):
            weave(True, 3, a, HALF)
        for a in (0, HALF):
            quantize_dz(3, a, HALF)
        product(False, 0, 3, 0, HALF, 4)
        product(False, 2, 2, 0, CHUNK, 2)
        product(True, 1, 2, 0, CHUNK, 3)
        product(True, 0, 3, HALF, HALF, 5)
        product(True, 1, 3, 0, CHUNK, 6)

        y_flat = keep.tile([P, PACK * V], F32, name="y")
        y = y_flat[:].rearrange("p (t x) -> p t x", t=PACK)
        y_b = keep.tile([P, V * PACK], BF16, name="y_b", align_bytes=64)
        y_codes = keep.tile([P, V], U32, name="y_codes", align_bytes=64)
        y_scales = keep.tile([P, V // 4], U8, name="y_scales", align_bytes=64)

        def look_up(on_vector, t, x0, x1, into):
            window = dm[t][:].indirect(src_list[:, 2 * x0 // PER_COL : 2 * x1 // PER_COL])
            if on_vector:
                nc.vector.tensor_copy(into, window)
            else:
                nc.scalar.activation(into, window, COPY)

        def add_pairs(engine, t0, t1, x0, x1, pairs):
            both = pairs.rearrange("p t (x j) -> p j t x", j=2)
            engine.tensor_tensor(y[:, t0:t1, x0:x1], both[:, 0, :, :], both[:, 1, :, :], ADD)

        def side_by_side(on_vector, on_scalar, n, pairs):
            starts = sorted((t * V + x0, t, x0, engine) for engine, (t, x0) in enumerate((on_scalar, on_vector)))
            for k, (at, t, x0, engine) in enumerate(starts):
                look_up(engine == 1, t, x0, x0 + n, pairs[:, 2 * n * k : 2 * n * (k + 1)])
            first, step = starts[0][0], starts[1][0] - starts[0][0]
            sums = y_flat[:, first : first + 2 * step].rearrange("p (r x) -> p r x", r=2)[:, :, 0:n]
            both = pairs.rearrange("p (r x j) -> p j r x", r=2, j=2)
            nc.gpsimd.tensor_tensor(sums, both[:, 0, :, :], both[:, 1, :, :], ADD)

        def shared(t, x0, cut, x1, pairs):
            look_up(True, t, x0, cut, pairs[:, 0 : 2 * (cut - x0)])
            look_up(False, t, cut, x1, pairs[:, 2 * (cut - x0) : 2 * (x1 - x0)])
            add_pairs(nc.gpsimd, t, t + 1, x0, x1, pairs.rearrange("p (t c) -> p t c", t=1))

        def late(t0, t1, x0, x1, pairs):
            n = 2 * (x1 - x0)
            for t in range(t0, t1):
                look_up(False, t, x0, x1, pairs[:, (t - t0) * n : (t - t0 + 1) * n])
            add_pairs(nc.vector, t0, t1, x0, x1, pairs.rearrange("p (t c) -> p t c", t=t1 - t0))

        def store_y(t0, t1, x0, x1):
            nc.sync.dma_start(out=y_rows[:, t0:t1, x0:x1], in_=y[:, t0:t1, x0:x1])

        def store_run(first, end):
            nc.sync.dma_start(out=y_flat_out[:, first:end], in_=y_flat[:, first:end])

        def round_y(x0, x1):
            nc.vector.tensor_copy(
                y_b[:, PACK * x0 : PACK * x1].rearrange("p (c i t) -> p c t i", i=4, t=PACK),
                y[:, :, x0:x1].rearrange("p t (c i) -> p c t i", i=4),
            )

        def quantize_y(x0, x1):
            j = x0 // 256
            nc.vector.quantize_mx(
                out=y_codes[:, x0:x1].bitcast(E4M3),
                scales=y_scales[4 * j : P, x0 - 256 * j : x1 - 256 * j],
                in_=y_b[:, PACK * x0 : PACK * x1],
            )

        def store_words(x0, x1):
            nc.sync.dma_start(out=words_out[:, x0:x1], in_=y_codes[:, x0:x1].bitcast(I32))

        stage = [keep.tile([P, 2048], F32, name="stage%d" % k) for k in range(4)]
        spare = stage[3]
        shared(0, 0, 240, 480, stage[0][:, 0:960])
        store_run(0, 480)
        side_by_side((0, 480), (1, 0), 272, stage[0][:, 960:2048])
        product(False, 2, 3, 0, CHUNK, 7)
        shared(1, 272, 576, 752, stage[1][:, 0:960])
        side_by_side((1, 752), (0, 752), 272, stage[2][:, 0:1088])
        store_run(480, 2 * V)
        product(False, 3, 3, 0, CHUNK, 0)
        shared(2, 256, 416, 576, y_flat[:, 2 * V + 752 : 3 * V + 368])
        last_three = [(False, 3, 512, 768), (True, 2, 576, 768), (True, 3, 256, 512)]
        held = [stage[1][:, 1024:1536], stage[1][:, 1536:1920], stage[2][:, 1280:1792]]
        for (on_vector, t, x0, x1), pairs in zip(last_three, held):
            look_up(on_vector, t, x0, x1, pairs)
        for (on_vector, t, x0, x1), pairs in zip(last_three, held):
            add_pairs(nc.vector, t, t + 1, x0, x1, pairs.rearrange("p (t c) -> p t c", t=1))
        store_y(2, 4, 256, 768)
        round_y(512, 768)
        round_y(256, 512)
        quantize_y(512, 768)
        late(2, 4, 768, V, spare[:, 0:1024])
        store_y(2, 4, 768, V)
        quantize_y(256, 512)
        store_words(256, 768)
        round_y(768, V)
        late(2, 4, 0, 128, spare[:, 1024:1536])
        quantize_y(768, V)
        store_words(768, V)
        round_y(0, 128)
        late(2, 4, 128, 192, spare[:, 1536:1792])
        quantize_y(0, 128)
        late(2, 4, 192, 256, spare[:, 1792:2048])
        store_y(2, 4, 0, 256)
        round_y(128, 192)
        round_y(192, 256)
        quantize_y(128, 192)
        quantize_y(192, 256)
        store_words(0, 256)
        for q in range(4):
            queue = nc.scalar if q % 2 else nc.sync
            queue.dma_start(
                out=scales_out[4 * q : 4 * q + 4, :].rearrange("r (j x) -> j r x", j=4),
                in_=y_scales[32 * q : 32 * q + 16, :].bitcast(I32),
            )
